import numpy as np, ml_dtypes
CORES = [5,29,101,125,133,157,229,253]
N = 8
BF = ml_dtypes.bfloat16
def gentries(a):
    return np.ascontiguousarray(a.reshape(8, 16, -1).transpose(0, 2, 1)).reshape(8, -1)
def gtable(e):
    e = np.asarray(e); return np.ascontiguousarray(e.reshape(8, -1, 16).transpose(0, 2, 1)).reshape(128, -1).astype(np.int32)
W, K, O, TH, CAP, RO = 4096, 8, 256, 150, 48, 5
def ring(rng):
    gap = rng.integers(0, W // K, (N, 8, K, O)) + 1; gap[:, :, 0] = rng.integers(0, W, (N, 8, O))
    return np.add.accumulate(gap, axis=2) & (W - 1)
def held(c, want, pri):
    h = np.zeros(c.shape, np.int64)
    for q in range(N):
        for g in range(8):
            p = np.broadcast_to(pri[q, g], (K, O)); low = np.full(W, O); w = want[q, g]
            np.minimum.at(low, c[q, g][w], p[w]); h[q, g] = w & (low[c[q, g]] == p)
    return h
def crew(rng):
    c = ring(rng); lv = rng.choice(np.array([0, K // 2, K - 2, K - 1, K]), (8, O)); pri = np.zeros((8, O), np.int64); cls = np.zeros((8, 1, O), bool)
    nf = rng.permutation(8 + (O * 45 // 100 - 8) * np.arange(8) // 7)
    for g in range(8):
        n = int(nf[g]); o = rng.permutation(O); lv[g, o[:n]] = K; pri[g, o] = np.arange(O); cls[g, 0, o[:n]] = True
        for q in range(N):
            own = rng.permutation(W)[:n * K].reshape(K, n); c[q, g][:, o[:n]] = own
            rest = c[q, g][:, o[n:]]; t = rng.choice(own.reshape(-1), O - n); k = rng.integers(0, K, O - n)
            ok = (rng.random(O - n) < 0.3) & ~np.any(rest == t, axis=0)
            rest[k[ok], np.flatnonzero(ok)] = t[ok]; c[q, g][:, o[n:]] = rest
    want = (np.arange(K)[:, None] < lv[:, None, :]) & (cls | (rng.random((N, 8, K, O)) < 0.95))
    return c, held(c, want, np.broadcast_to(pri, (N, 8, O)))
def far(rng, m, share, over):
    k = rng.integers(0, K, (N, 8, O)); k = np.where(rng.random(k.shape) < 0.5, k, (K - 1) * rng.integers(0, 2, k.shape))
    hit = (rng.random((N, 8, 1, O)) < share) & (np.arange(K)[:, None] == k[:, :, None, :])
    return np.where(hit, TH + rng.integers(1, over + 1, m.shape), m)
def naps(rng, share):
    return np.add.reduce((rng.random((N, 8, O, RO)) < share).astype(np.int64) << np.arange(RO), axis=3)
def pack(x, c, h, m, wk, lump=None):
    ix = c.reshape(N, 8, 1, K * O); xc = np.take_along_axis(x, ix, 3); m = m.reshape(N, 8, 1, K * O)
    d = (m >> 4) + (((np.arange(16).reshape(16, 1) + ix) & 15) < (m & 15))
    if lump is not None:
        s = lump.reshape(N, 8, 1, K * O); i = (np.arange(16).reshape(16, 1) + s) & 15
        most = np.take_along_axis(np.maximum(xc, 255 - xc), i, 2).astype(np.int64); before = np.add.accumulate(most, axis=2) - most
        u = np.zeros(i.shape, np.int64); np.put_along_axis(u, i, np.minimum(np.maximum(m - before, 0), most), 2)
        d = np.where(s < 16, u, d)
    e = np.where(xc < 128, xc + d, xc - d)
    return {"x": np.ascontiguousarray(x.reshape(N, 128, W)).astype(np.float32).astype(BF), "snap": np.ascontiguousarray(e.reshape(N, 128, K * O)).astype(np.float32).astype(BF),
            "cs": np.stack([gtable(a.reshape(8, -1)) for a in c]), "hold": np.stack([gtable(a.reshape(8, -1)) for a in h]), "wake": np.stack([gtable(a) for a in wk])}
def cells(rng):
    return rng.integers(0, 256, (N, 8, 16, W), dtype=np.int32)
def setup_inputs(rng):
    x = cells(rng); c, h = crew(rng); m = far(rng, rng.integers(0, TH + 1, c.shape), 0.08, 600)
    return pack(x, c, h, m, naps(rng, rng.choice(np.array([0.5, 0.7, 0.9]), (N, 8, 1, 1))))
def setup_inputs_room(rng):
    x = cells(rng); c = np.zeros((N, 8, K, O), np.int64); h = np.ones((N, 8, K, O), np.int64); m = rng.integers(0, TH + 1, c.shape); wk = naps(rng, 0.7)
    cnt = rng.permutation(np.array([0, 1, CAP - 1, CAP, CAP + 1, 2 * CAP, O - 1, O]))
    for g in range(8):
        n = int(cnt[g]); o = rng.permutation(O)
        if n == 0: wk[:, g] = 1
        for q in range(N):
            c[q, g] = rng.permutation(W)[:K * O].reshape(K, O)
            rest = o[n:] if q & 1 else o[n:][rng.random(O - n) < 0.5]
            h[q, g][rng.integers(0, K, len(rest)), rest] = 0
            if q & 1 == 0 and n > 0: m[q, g][rng.integers(0, K), rest[rng.random(len(rest)) < 0.15]] = TH + 1
    return pack(x, c, h, m, wk)
def setup_inputs_storm(rng):
    x = cells(rng); c = ring(rng); m = rng.integers(0, TH + 1, c.shape); want = rng.random(c.shape) < 0.5; wk = naps(rng, 0.8)
    pri = np.argsort(rng.random((N, 8, O)), axis=-1); deal = rng.permutation(8); role = deal & 3
    for g in range(8):
        if deal[g] == 0:
            want[:, g] = True
            for q in range(N): c[q, g] = rng.permutation(W)[:K * O].reshape(K, O)
        if role[g] == 0: m[:, g, rng.integers(0, K)] = TH + 1 + rng.integers(0, 600, (N, O))
        if role[g] == 1: m[::2, g, 0, ::2] = TH + 1
        if role[g] == 2:
            o = int(rng.integers(0, O))
            for q in range(N):
                v = int(rng.integers(0, W)); k = rng.integers(0, K, O); ok = ~np.any(c[q, g] == v, axis=0)
                c[q, g][k[ok], np.flatnonzero(ok)] = v; x[q, g, :, v] = rng.integers(0, 16, 16) + 240 * (q & 1)
                want[q, g, :, o] = True; i = int(np.flatnonzero(pri[q, g] == 0)[0]); pri[q, g, i] = pri[q, g, o]; pri[q, g, o] = 0
        if role[g] == 3: want[:, g] = False; wk[:, g] = wk[:, g] & ~1
    p = 2 * int(rng.integers(0, N // 2)); m[p:p + 2] = far(rng, m, 1.0, 600)[p:p + 2]
    return pack(x, c, held(c, want, pri), m, wk)
def setup_inputs_crowd(rng):
    x = cells(rng); c = np.zeros((N, 8, K, O), np.int64)
    for q in range(N):
        for g in range(8):
            P = 64 if g & 1 else 256
            pool = rng.permutation(np.concatenate([np.array([0, W - 1]), 1 + rng.permutation(W - 2)[:P - 2]]))
            c[q, g] = pool[(rng.integers(0, P, O) + np.arange(K)[:, None] * (2 * rng.integers(0, P // 2, O) + 1)) & (P - 1)]
    pri = np.argsort(rng.random((8, O)), axis=-1); lv = np.where(pri < 3, K, rng.integers(0, K + 1, (8, O)))
    lv[rng.permutation(8)[:4]] = 0
    want = np.broadcast_to(np.arange(K)[:, None] < lv[:, None, :], (N, 8, K, O))
    m = far(rng, rng.integers(0, TH + 1, c.shape), 0.01, 600)
    return pack(x, c, held(c, want, np.broadcast_to(pri, (N, 8, O))), m, naps(rng, rng.choice(np.array([0.6, 1.0]), (N, 8, 1, 1))))
def setup_inputs_ties(rng):
    x = cells(rng); z = rng.random((N, 8, 1, W)); x = np.where(z < 0.06, 0, np.where(z < 0.12, 255, x)).astype(np.int32)
    c, h = crew(rng); m = far(rng, rng.choice(np.array([0, TH - 1, TH]), c.shape), 0.12, 1)
    wk = naps(rng, 0.75) & ~(1 << int(rng.integers(1, 3)))
    return pack(x, c, h, m, wk, np.minimum(rng.integers(0, 32, c.shape), 16))
def setup_inputs_spread(rng):
    x = np.minimum((np.exp2(8.01 * rng.random((N, 8, 1, W))) * rng.random((N, 8, 16, W))).astype(np.int32), 255)
    c, h = crew(rng); m = far(rng, (TH * rng.random(c.shape) ** 4).astype(np.int64), 0.1, 1000)
    share = np.ones((N, 1, 1, 1)) * rng.permutation(np.array([0.0, 0.2, 0.4, 0.6, 0.8, 0.9, 1.0, 1.0])).reshape(1, 8, 1, 1)
    return pack(x, c, h, m, naps(rng, share))
def check_inputs(d):
    bad = []
    for k in ("x", "snap"):
        v = np.asarray(d[k]).astype(np.float32)
        if not (np.all(v >= 0) and np.all(v <= 255) and np.all(v == np.floor(v))): bad.append("range of " + k)
    for k, hi in (("cs", W - 1), ("hold", 1), ("wake", 2 ** RO - 1)):
        if np.min(d[k]) < 0 or np.max(d[k]) > hi: bad.append("range of " + k)
    c = np.stack([gentries(a) for a in d["cs"]]).reshape(N, 8, K, O); h = np.stack([gentries(a) for a in d["hold"]]).reshape(N, 8, K, O)
    s = np.sort(c, axis=2)
    if np.any(s[:, :, 1:] == s[:, :, :-1]): bad.append("cells of an operation differ")
    for q in range(N):
        for g in range(8):
            v = c[q, g][h[q, g] == 1]
            if len(np.unique(v)) != len(v) and "a cell has one holder" not in bad: bad.append("a cell has one holder")
    return bad
def reference(x, snap, cs, hold, wake):
    v = np.zeros((N, 8, 16, W + 1), np.int32)
    v[..., :W] = x.astype(np.float32).astype(np.int32).reshape(N, 8, 16, W)
    e = snap.astype(np.float32).astype(np.int32).reshape(N, 8, 16, K * O)
    c = np.stack([gentries(a) for a in cs]).astype(np.int64).reshape(N, 8, K, O); h = np.stack([gentries(a) for a in hold]).reshape(N, 8, K, O)
    wk = np.stack([gentries(a) for a in wake]).astype(np.int64)
    own = np.arange(O) + 1; lane = np.broadcast_to(np.arange(O), (N, 8, O)); cur = np.array(lane)
    lock = np.zeros((N, 8, W + 1), np.int64)
    np.put_along_axis(lock, np.where(h == 1, c, W).reshape(N, 8, -1), np.broadcast_to(own, c.shape).reshape(N, 8, -1), 2)
    for t in range(RO):
        twin = np.arange(N) ^ (1 + t % (N - 1))
        got = np.take_along_axis(v, c.reshape(N, 8, 1, -1), 3)
        dist = np.add.reduce(np.abs(got - e), axis=2).reshape(N, 8, K, O)
        who = np.take_along_axis(lock, c.reshape(N, 8, -1), 2).reshape(N, 8, K, O); mine = who == own
        bad = np.any(dist > TH, axis=2); full = np.all(mine, axis=2)
        abort = bad | bad[twin]; ready = full & full[twin] & ~abort
        before = np.add.accumulate(ready.astype(np.int64), axis=2) - ready
        commit = ready & (before < CAP); done = abort | commit
        first = np.argmin(mine, axis=2)[:, :, None, :]
        cell = np.take_along_axis(np.take_along_axis(c, first, 2)[:, :, 0], cur, 2); by = np.take_along_axis(np.take_along_axis(who, first, 2)[:, :, 0], cur, 2)
        gone = np.take_along_axis(done, cur, 2); act = (((wk >> t) & 1) == 1) & ~gone & ~np.take_along_axis(full, cur, 2)
        np.put_along_axis(lock, np.where(done[:, :, None, :] & mine, c, W).reshape(N, 8, -1), 0, 2)
        for q in range(N):
            for g in range(8):
                w = np.flatnonzero(act[q, g] & (by[q, g] == 0)); low = np.full(W, O); a = cell[q, g][w]
                np.minimum.at(low, a, w); win = low[a] == w
                lock[q, g][a[win]] = cur[q, g][w[win]] + 1
        cur = np.where(gone, lane, np.where(act & (by > 0), by - 1, cur))
        cm = np.broadcast_to(commit[:, :, None, :], (N, 8, K, O)); dn = np.broadcast_to(done[:, :, None, :], (N, 8, K, O)).reshape(N, 8, 1, -1)
        d = np.where(cm.reshape(N, 8, 1, -1), got[twin], e)
        np.put_along_axis(v, np.where(cm, c, W).reshape(N, 8, 1, -1), d, 3)
        u = np.add.reduce(d.reshape(N, 8, 2, 8, K, O).astype(np.int64), axis=3); hs = (u[:, :, 0] * u[:, :, 1]) >> 3
        new = np.zeros((N, 8, K, O), np.int64); new[:, :, 0] = hs[:, :, 0] & (W - 1)
        for k in range(1, K): new[:, :, k] = (new[:, :, k - 1] + 1 + (hs[:, :, k] & (W // K - 1))) & (W - 1)
        c = np.where(done[:, :, None, :], new, c)
        e = np.where(dn, np.take_along_axis(v, c.reshape(N, 8, 1, -1), 3), e)
    lock[..., W] = 0
    mine = np.take_along_axis(lock, c.reshape(N, 8, -1), 2).reshape(N, 8, K, O) == own
    ys = np.add.reduce(v[..., :W] * np.arange(1, 17, dtype=np.int32).reshape(16, 1), axis=2)
    return {"ys": ys.astype(np.float32), "yc": np.stack([gtable(a.reshape(8, -1)) for a in c]).astype(np.float32),
            "yh": np.stack([gtable(a.reshape(8, -1)) for a in mine]).astype(np.float32), "yl": np.stack([gtable(a) for a in cur]).astype(np.float32)}

@@ -1,0 +1,752 @@
+import math
+from concourse.mybir import AluOpType as OP, ActivationFunctionType as AF
+
+STEPS = 5
+E0, VB, DB, E1, VE = 0, 2048, 6144, 6528, 8576
+LW = 4112
+LAG = (2.5, 4.5, 6.0, 0.1, 0.15)
+
+SCRATCH = {
+    "V": ("sbuf", [128, VE], "bfloat16"),
+    "got0": ("sbuf", [128, 2048], "bfloat16"), "got1": ("sbuf", [128, 2048], "bfloat16"),
+    "mx": ("sbuf", [128, 2048], "bfloat16"), "cR": ("sbuf", [128, 2048], "float32"),
+    "IW": ("sbuf", [128, LW], "float32"), "LK": ("sbuf", [128, 6144], "float32"),
+    "LV0": ("sbuf", [128, 2048], "float32"), "LV": ("sbuf", [128, 256], "float32"),
+    "SEL2": ("sbuf", [128, 2048], "bfloat16"), "SELPK": ("sbuf", [128, 2048], "bfloat16"), "SELW": ("sbuf", [128, 2048], "bfloat16"),
+    "MK": ("sbuf", [128, 256], "bfloat16"), "PKP": ("sbuf", [128, 128], "bfloat16"), "PKO": ("sbuf", [128, 128], "bfloat16"),
+    "PKH": ("sbuf", [128, 128], "float16"), "PK8": ("sbuf", [128, 128], "bfloat16"),
+    "B8": ("sbuf", [128, 8], "bfloat16"), "B8H": ("sbuf", [128, 8], "float16"),
+    "q0": ("sbuf", [128, 256], "bfloat16"), "q1": ("sbuf", [128, 256], "bfloat16"), "qh": ("sbuf", [128, 256], "float16"),
+    "EQ": ("sbuf", [128, 4096], "bfloat16"), "LH": ("sbuf", [128, 128], "bfloat16"),
+    "ONE": ("sbuf", [128, 256], "bfloat16"), "ZB": ("sbuf", [128, 256], "bfloat16"), "OPW": ("sbuf", [128, 512], "bfloat16"),
+    "B128": ("sbuf", [128, 128], "bfloat16"), "BTM": ("sbuf", [128, 128], "bfloat16"), "ID": ("sbuf", [128, 128], "bfloat16"),
+    "OR": ("sbuf", [128, 256], "float32"), "JC": ("sbuf", [128, 256], "float32"), "K": ("sbuf", [128, 256], "float32"),
+    "COMP": ("sbuf", [128, 512], "float32"), "DUM": ("sbuf", [128, 48], "float32"), "thrR": ("sbuf", [128, 256], "float32"),
+    "clOp": ("sbuf", [128, 256], "float32"), "clR": ("sbuf", [128, 256], "float16"),
+    "G1": ("sbuf", [128, 256], "bfloat16"), "decR": ("sbuf", [128, 256], "bfloat16"), "decL": ("sbuf", [128, 256], "bfloat16"),
+    "dnR": ("sbuf", [128, 256], "bfloat16"), "gnR": ("sbuf", [128, 256], "bfloat16"), "winR": ("sbuf", [128, 256], "bfloat16"),
+    "Dl": ("sbuf", [128, 384], "bfloat16"), "yso": ("sbuf", [128, 256], "float32"),
+    "i1": ("sbuf", [128, 8], "int32"), "col": ("sbuf", [128, 32], "float32"), "GC": ("sbuf", [128, 8], "float32"),
+    "lane": ("sbuf", [128, 688], "float32"), "red": ("sbuf", [128, 128], "float32"),
+    "code0": ("sbuf", [128, 16], "float32"), "code1": ("sbuf", [128, 16], "float32"),
+    "rdy": ("sbuf", [128, 16], "bfloat16"), "rw": ("sbuf", [128, 16], "bfloat16"), "cab": ("sbuf", [128, 32], "bfloat16"),
+    "Ls": ("sbuf", [128, 72], "int32"), "Lt": ("sbuf", [128, 48], "float32"), "L16": ("sbuf", [128, 48], "uint16"),
+}
+for _n in ("csI", "hdI", "kI", "Pi", "A", "Bv", "pr", "h", "yI0", "yI1"):
+    SCRATCH[_n] = ("sbuf", [128, 128], "int32")
+for _n in ("HB", "kp1", "NCE", "sm", "d1", "bd", "cmS", "key", "jW", "eaA", "ejA", "eaB", "ejB", "t1", "t2", "t3", "t4", "t5"):
+    SCRATCH[_n] = ("sbuf", [128, 128], "float32")
+for _n in ("c16", "ei16"):
+    SCRATCH[_n] = ("sbuf", [128, 128], "uint16")
+for _n in ("wkI", "keI", "ceI", "fkI", "acI"):
+    SCRATCH[_n] = ("sbuf", [128, 16], "int32")
+for _n in ("cl16", "cur16", "lc16", "p16", "dn16", "off16", "oo16", "ol16", "dec16"):
+    SCRATCH[_n] = ("sbuf", [128, 16], "uint16")
+for _t in range(STEPS):
+    SCRATCH["lb%d" % _t] = ("sbuf", [128, 2048], "bfloat16")
+    SCRATCH["lc%d" % _t] = ("sbuf", [128, 16], "float32")
+    SCRATCH["ln%d" % _t] = ("sbuf", [128, 128], "int32")
+for _n in ("PSP", "PSM", "PSC", "PSR", "PSA", "PSD", "V0", "V1"):
+    SCRATCH[_n] = ("psum", [128, 512], "float32")
+PLACES = {"lane": 4, "q0": 3, "q1": 2, "t1": 3, "t2": 3, "t5": 3, "Pi": 2, "A": 2, "Bv": 2, "key": 2, "cl16": 2, "p16": 2}
+for _n in PLACES:
+    SCRATCH[_n] = (SCRATCH[_n][0], [128, SCRATCH[_n][1][1] * PLACES[_n]], SCRATCH[_n][2])
+
+MSG = ("b0", "b1", "co", "nc")
+SEMAPHORES = ["qv", "qs", "qt", "qg"] + ["d%d" % i for i in range(28)]
+for _t in range(STEPS):
+    for _m in MSG:
+        SEMAPHORES += ["a%s%d" % (_m, _t), "l%s%d" % (_m, _t)]
+
+_L = {}
+for _i, _n in enumerate("cur cl clS p act nf an mv cand ac aw wW dm256 dm4096 win cur1 x1 x2 x3 x4 x5 x6 X rank inc e cm done n32 n32a wo "
+                        "keyv full tr z lm fk1 dec val nr lose".split()):
+    _L[_n] = 16 * _i
+
+
+def landing(m, t):
+    if m == "b0": return "lb%d" % t, 0, 1024
+    if m == "b1": return "lb%d" % t, 1024, 2048
+    if m == "co": return "lc%d" % t, 0, 16
+    return "ln%d" % t, 0, 128
+
+
+def route(core, t, T, topo):
+    dst = T.cores[T.rank_of(core) ^ (1 + t % 7)]
+    near = [x for x in topo.cores_of(core) if x != core and topo.die(x) == topo.die(core) and topo.may_write(x, dst)]
+    far = [x for x in topo.cores_of(core) if topo.die(x) != topo.die(core) and topo.may_write(x, dst)]
+    via = {"b0": near[-1], "b1": near[-2], "co": None, "nc": None}
+    if not topo.may_write(core, dst):
+        via["co"] = far[0]; via["nc"] = far[1]
+    return dst, via
+
+
+def engines8(topo, a, b):
+    return sum(1 << e for e in topo.engines(a, b)[:8])
+
+
+def send(g, T, topo, core, dst, m, t, src):
+    buf, lo, hi = landing(m, t)
+    rid, pid = topo.addr(dst, core)
+    return g.remote_dma(out_ap=T[buf][:, lo:hi], in_ap=src, remote_sem=T.sem["a%s%d" % (m, t)], local_sem=T.sem["l%s%d" % (m, t)],
+                        pid=pid, routing_id=rid, dma_engine_mask=engines8(topo, core, dst))
+
+
+def relay_program(g, core, T, topo):
+    for src in [x for x in topo.cores_of(core) if T.rank_of(x) is not None]:
+        for t in range(STEPS):
+            dst, via = route(src, t, T, topo)
+            mine = [m for m in MSG if via[m] == core]
+            for m in mine:
+                buf, lo, hi = landing(m, t)
+                g.wait_ge(T.sem["a%s%d" % (m, t)], 8)
+                send(g, T, topo, core, dst, m, t, T[buf][:, lo:hi])
+            for m in mine:
+                g.wait_ge(T.sem["l%s%d" % (m, t)], 8)
+
+
+def rank_program(g, core, T, topo):
+    if T.rank_of(core) is None:
+        relay_program(g, core, T, topo)
+        return
+    Q = {"v": g.vector, "s": g.scalar, "t": g.tensor, "y": g.sync, "g": g}
+    width = {n: b[1][1] // PLACES.get(n, 1) for n, b in SCRATCH.items()}
+    ispsum = {n: b[0] == "psum" for n, b in SCRATCH.items()}
+    hist = {}
+    ops = []
+    known = {q: {} for q in Q}
+    cnt = {}
+    nd = [0]
+
+    def R(b, lo=0, hi=None, st=1, np=128):
+        return ("n", b, lo, width[b] if hi is None else hi, st, np)
+
+    def L(n, a=0, b=16):
+        return ("n", "lane", _L[n] + a, _L[n] + b, 1, 128)
+
+    def C(i):
+        return ("n", "col", i, i + 1, 1, 128)
+
+    def IX(w, o):
+        return ("i", w, o)
+
+    def ap(s):
+        if s[0] == "i": return ap(s[1]).indirect(ap(s[2]))
+        p = slice(0, s[5]) if s[5] < 128 else slice(None)
+        if s[4] == 1: return T[s[1]][p, s[2]:s[3]]
+        return T[s[1]][p, s[2]:s[3]:s[4]]
+
+    def flat(s):
+        if not isinstance(s, tuple): return []
+        if s[0] == "i": return flat(s[1]) + flat(s[2])
+        return [(s[1], s[2], s[3])]
+
+    def need(q, deps):
+        for d in sorted(deps, reverse=True):
+            _, sem, n, kn = ops[d]
+            if known[q].get(sem, 0) >= n: continue
+            Q[q].wait_ge(T.sem[sem], n)
+            for k2, v2 in kn.items():
+                if known[q].get(k2, 0) < v2: known[q][k2] = v2
+
+    def track(q, reads, writes):
+        deps = set()
+        acc = [(b, lo, hi, False) for b, lo, hi in reads] + [(b, lo, hi, True) for b, lo, hi in writes]
+        for b, lo, hi, w in acc:
+            for lo2, hi2, w2, d in hist.get(b, ()):
+                meet = lo < hi2 and lo2 < hi and (w or w2)
+                if ispsum.get(b, False):
+                    if ops[d][0] != q or (q != "t" and meet): deps.add(d)
+                elif meet:
+                    deps.add(d)
+        return deps, acc
+
+    def record(q, acc, sem, n):
+        kn = dict(known[q]) if q in known else {}
+        kn[sem] = n
+        ops.append((q, sem, n, kn))
+        d = len(ops) - 1
+        for b, lo, hi, w in acc:
+            hl = hist.setdefault(b, [])
+            if w and not ispsum.get(b, False):
+                hist[b] = hl = [x for x in hl if not (lo <= x[0] and x[1] <= hi)]
+            elif ispsum.get(b, False):
+                hist[b] = hl = [x for x in hl if not (ops[x[3]][0] == q and lo <= x[0] and x[1] <= hi and (w or not x[2]))]
+            hl.append((lo, hi, w, d))
+
+    ver = {}
+
+    def res(s, w=False):
+        if not isinstance(s, tuple): return s
+        if s[0] == "i": return ("i", res(s[1]), res(s[2]))
+        b = s[1]
+        if b not in PLACES: return s
+        wd = width[b]
+        key = (b, s[2] // 16) if b == "lane" else b
+        if w and (s[3] - s[2] == (16 if b == "lane" else wd)): ver[key] = (ver.get(key, -1) + 1) % PLACES[b]
+        sh = ver.get(key, 0) * wd
+        return ("n", b, s[2] + sh, s[3] + sh, s[4], s[5])
+
+    recs = []
+    group = []
+    sent = {}
+
+    def wid(s):
+        if s[0] == "i": return 16 * (s[2][3] - s[2][2])
+        return (s[3] - s[2] + s[4] - 1) // s[4]
+
+    def short(s):
+        b = s[1][1] if s[0] == "i" else s[1]
+        return SCRATCH[b][2] in ("bfloat16", "float16", "uint16")
+
+    def span(q, kind, r, w):
+        out, n = w[0], wid(w[0])
+        cyc = n
+        if out[0] == "i": cyc = 3.8 * n
+        elif any(isinstance(x, tuple) and x[0] == "i" for x in r): cyc = 1.56 * n
+        elif q == "t": cyc = max(64, wid(r[1]))
+        elif kind == "tt": cyc = n if any(ispsum[x[1]] for x in r) else 2 * n
+        elif q == "g": cyc = 2 * n + 150
+        elif q == "v" and kind == "ts" and short(out) and all(short(x) for x in r[:1]): cyc = n / 2
+        return 1.2 * (max(64, cyc) * 0.00083 + (0.06 if q == "s" else 0.01))
+
+    def comp(q, reads, writes, fn, kind="ts"):
+        r = [res(x) for x in reads]
+        w = [res(x, True) for x in writes]
+        rd = sum((flat(x) for x in r), [])
+        wr = []
+        for x in w:
+            if x[0] == "i":
+                wr += flat(x[1]); rd += flat(x[2])
+            else:
+                wr += flat(x)
+        item = (rd, wr, lambda: fn(r, w))
+        if group: group[-1].append((item, span(q, kind, r, w)))
+        else: recs.append((q, [item], span(q, kind, r, w), "c", None))
+
+    def together(fn):
+        group.append([])
+        fn()
+        got = group.pop()
+        recs.append(("t", [x[0] for x in got], sum(x[1] for x in got), "c", None))
+
+    def dma(q, out, in_, reads, writes):
+        recs.append((q, [(reads, writes, lambda: Q[q].dma_start(out, in_))], 0.06, "d", 2.5))
+
+    def out_send(t, m, srcspec):
+        s = res(srcspec)
+        recs.append(("g", [(flat(s), [], lambda: (t, m, s))], 0.9, "r", None))
+        sent[(t, m)] = len(recs) - 1
+        recs.append(("net", [([], [landing(m, t)], None)], 0.0, "a", (t, m)))
+
+    def build():
+        n = len(recs)
+        pred = [set() for _ in range(n)]
+        old = {}
+        for i in range(n):
+            q = recs[i][0]
+            for rd, wr, _ in recs[i][1]:
+                for b, lo, hi, w in [(b, lo, hi, False) for b, lo, hi in rd] + [(b, lo, hi, True) for b, lo, hi in wr]:
+                    hl = old.setdefault(b, [])
+                    for lo2, hi2, w2, d in hl:
+                        if d != i and ((ispsum.get(b, False) and recs[d][0] != q) or (lo < hi2 and lo2 < hi and (w or w2))): pred[i].add(d)
+                    if w and not ispsum.get(b, False): hl[:] = [x for x in hl if not (lo <= x[0] and x[1] <= hi)]
+                    hl.append((lo, hi, w, i))
+            if recs[i][3] == "a": pred[i].add(sent[recs[i][4]])
+        succ = [[] for _ in range(n)]
+        for i in range(n):
+            for d in pred[i]: succ[d].append(i)
+
+        def lag(d, i):
+            if recs[d][3] == "d": return recs[d][4]
+            if recs[i][3] == "a":
+                t, m = recs[i][4]
+                if m[0] == "b": return LAG[2]
+                return LAG[0] if route(core, t, T, topo)[1][m] is None else LAG[1]
+            if recs[d][3] == "r": return 3.0
+            return LAG[3] if recs[d][0] == recs[i][0] else LAG[4]
+
+        prio = [0.0] * n
+        for i in range(n - 1, -1, -1):
+            prio[i] = recs[i][2] + max([lag(i, j) + prio[j] for j in succ[i]] + [0.0])
+        left = [len(p) for p in pred]
+        est = [0.0] * n
+        ready = {}
+        free = {}
+        for i in range(n):
+            if left[i] == 0: ready.setdefault(recs[i][0], []).append(i)
+        order = []
+        for _ in range(n):
+            best = None
+            for q, rl in ready.items():
+                if not rl: continue
+                t0 = max(free.get(q, 0.0), min(est[i] for i in rl))
+                if best is None or t0 < best[0]: best = (t0, q)
+            t0, q = best
+            i = max([x for x in ready[q] if est[x] <= t0 + 1e-9], key=lambda x: (prio[x], -x))
+            ready[q].remove(i)
+            order.append(i)
+            end = t0 + recs[i][2]
+            if q != "net": free[q] = end
+            for j in succ[i]:
+                est[j] = max(est[j], end + lag(i, j))
+                left[j] -= 1
+                if left[j] == 0: ready.setdefault(recs[j][0], []).append(j)
+        for i in order:
+            q, items, _, kind, x = recs[i]
+            for rd, wr, fn in items:
+                if kind == "a":
+                    sem = "a%s%d" % (x[1], x[0]); cnt[sem] = 8
+                    record("net", [(b, lo, hi, True) for b, lo, hi in wr], sem, 8)
+                    continue
+                deps, acc = track(q, rd, wr)
+                need(q, deps)
+                if kind == "r":
+                    t, m, s = fn()
+                    dst, via = route(core, t, T, topo)
+                    send(g, T, topo, core, dst if via[m] is None else via[m], m, t, ap(s))
+                    sem = "l%s%d" % (m, t); cnt[sem] = 8
+                elif kind == "d":
+                    sem = "d%d" % nd[0]; nd[0] += 1
+                    fn().then_inc(T.sem[sem], 16); cnt[sem] = 16
+                else:
+                    sem = "q" + q
+                    cnt[sem] = cnt.get(sem, 0) + 1
+                    fn().then_inc(T.sem[sem], 1)
+                record(q, acc, sem, cnt[sem])
+
+    def tt(out, a, b, op):
+        comp("v", [a, b], [out], lambda r, w: g.vector.tensor_tensor(out=ap(w[0]), in0=ap(r[0]), in1=ap(r[1]), op=op), "tt")
+
+    def ts(out, a, s1, op0, s2=None, op1=None):
+        def call(r, w):
+            x1 = ap(r[1]) if isinstance(s1, tuple) else s1
+            x2 = ap(r[2]) if isinstance(s2, tuple) else s2
+            if op1 is None: return g.vector.tensor_scalar(out=ap(w[0]), in0=ap(r[0]), scalar1=x1, scalar2=None, op0=op0)
+            return g.vector.tensor_scalar(out=ap(w[0]), in0=ap(r[0]), scalar1=x1, scalar2=x2, op0=op0, op1=op1)
+        comp("v", [a, s1, s2], [out], call)
+
+    def cp(out, a):
+        comp("v", [a], [out], lambda r, w: g.vector.tensor_copy(out=ap(w[0]), in_=ap(r[0])))
+
+    def fill(out, x):
+        comp("v", [], [out], lambda r, w: g.vector.memset(ap(w[0]), x), "fill")
+
+    def act(out, a, func=AF.Copy, scale=1.0, bias=None):
+        def call(r, w):
+            sc = ap(r[1]) if isinstance(scale, tuple) else scale
+            if bias is None: return g.scalar.activation(out=ap(w[0]), in_=ap(r[0]), func=func, scale=sc)
+            return g.scalar.activation(out=ap(w[0]), in_=ap(r[0]), func=AF.Identity, bias=ap(r[2]), scale=sc)
+        comp("s", [a, scale, bias], [out], call)
+
+    def scatter_act(out, a):
+        comp("s", [a], [out], lambda r, w: g.scalar.activation(out=ap(w[0]), in_=ap(r[0]), func=AF.Silu))
+
+    def mm(out, lhsT, rhs, start, stop):
+        comp("t", [lhsT, rhs], [out], lambda r, w: g.tensor.matmul(ap(w[0]), ap(r[0]), ap(r[1]), start, stop))
+
+    def iota(out, pattern, base, cm, after=()):
+        comp("g", list(after), [out], lambda r, w: g.iota(ap(w[0]), pattern, base, cm, allow_small_or_imprecise_dtypes=True))
+
+    def asel(out, a, pattern, op, base, cm):
+        comp("g", [a], [out], lambda r, w: g.affine_select(ap(w[0]), ap(r[0]), pattern, op, 0.0, base, cm))
+
+    def conv1(bank, parts):
+        def run():
+            for h in range(2):
+                for n, (src, np, pick) in enumerate(parts):
+                    mm(R(bank, 256 + 128 * h, 384 + 128 * h), R(src, 128 * h, 128 * h + 128, 1, np), pick, n == 0, n == len(parts) - 1)
+        together(run)
+
+    def conv2(bank, lo, q, b8="B8"):
+        tt(R(q), R(bank, 256, 512), R("MK"), OP.mult)
+        together(lambda: [mm(R(bank, lo + 8 * h, lo + 8 * h + 8), R(q, 128 * h, 128 * h + 128), R(b8), True, True) for h in range(2)])
+
+    BIG = 1.0e6
+    Pc, PsE, Pdp, Pt = (R("V0", 128 * i, 128 * i + 128) for i in range(4))
+    Pthr, Pk, Pkb, Pu = (R("V1", 128 * i, 128 * i + 128) for i in range(4))
+
+    dma("y", T.csI[:], T.cs[:], [], [("csI", 0, 128)])
+    dma("y", T.hdI[:], T.hold[:], [], [("hdI", 0, 128)])
+    dma("y", T.V[:, VB:DB], T.x[:], [], [("V", VB, DB)])
+    dma("y", T.V[:, E0:E0 + 2048], T.snap[:], [], [("V", E0, E0 + 2048)])
+    dma("y", T.wkI[:], T.wake[:], [], [("wkI", 0, 16)])
+    fill(R("ONE"), 1.0)
+    iota(R("i1", 0, 1), [[0, 1]], 0, 1)
+    asel(R("BTM"), R("ONE", 0, 128), [[-16, 8], [0, 16]], OP.is_ge, 0, 1)
+    asel(R("B128"), R("BTM"), [[16, 8], [0, 16]], OP.is_ge, 15, -1)
+    iota(R("kI"), [[1, 8], [0, 16]], 0, 0)
+    iota(R("eaA"), [[16, 128]], 0, 0)
+    asel(R("BTM"), R("B128"), [[-1, 128]], OP.is_ge, 0, 1)
+    asel(R("ID"), R("B128"), [[-1, 128]], OP.is_equal, 0, 1)
+    iota(R("OR"), [[1, 256]], 0, 0)
+    iota(R("clOp"), [[0, 16], [1, 16]], 0, 0)
+    iota(R("IW"), [[1, LW]], 0, 0, [R("ID"), R("clOp"), R("OR"), R("eaA"), R("kI")])
+    fill(R("SEL2"), 0.0)
+    for i in range(16):
+        ts(R("SEL2", 129 * i, 128 * i + 128, 16), R("B128", i, 128, 16), 2.0, OP.mult)
+    ts(R("i1", 1, 2), R("i1", 0, 1), 15, OP.bitwise_and)
+    ts(R("i1", 2, 3), R("i1", 0, 1), 1, OP.bitwise_and)
+    ts(R("i1", 3, 4), R("i1", 1, 2), 1, OP.arith_shift_right)
+    cp(C(0), R("i1", 1, 2))
+    cp(C(1), R("i1", 2, 3))
+    ts(C(2), C(1), -1.0, OP.mult, 1.0, OP.add)
+    ts(C(3), R("i1", 3, 4), 256.0, OP.mult)
+    ts(C(4), C(0), 8.0, OP.is_lt, 0.5 - 1024.0, OP.mult)
+    ts(C(5), C(4), 1024.0, OP.add)
+    ts(C(9), C(1), 64.0, OP.add)
+    ts(R("SELPK"), R("SEL2"), C(5), OP.mult)
+    cp(Pk, R("kI"))
+    ts(R("jW"), R("eaA"), C(0), OP.add)
+    ts(R("t5"), R("jW"), 4096.0, OP.add)
+    cp(Pc, R("csI"))
+    cp(R("c16"), Pc)
+    ts(R("LV0", 0, 256), R("OR"), C(2), OP.mult, C(9), OP.add)
+    cp(R("t1"), R("hdI"))
+    tt(R("t3"), Pc, R("t5"), OP.subtract)
+    tt(R("t3"), R("t3"), R("t1"), OP.mult)
+    tt(R("t3"), R("t3"), R("t5"), OP.add)
+    cp(R("ei16"), R("t3"))
+    cp(R("LV0", 256, 512), R("LV0", 0, 256))
+    cp(R("LV0", 512, 1024), R("LV0", 0, 512))
+    cp(R("LV0", 1024, 2048), R("LV0", 0, 1024))
+    fill(R("LK", 0, LW), 0.0)
+
+    Ecur = [E0]
+
+    def P_chunk(buf, lo, h):
+        together(lambda: [mm(R("PSP", 64 * h, 64 * h + 64), R("SELPK", 128 * i, 128 * i + 128), R(buf, lo + 1024 * h + i, lo + 1024 * h + 1024, 16),
+                             i == 0, i == 15) for i in range(16)])
+
+    def hash_front():
+        cp(R("Pi"), R("PSP", 0, 128))
+        ts(R("A"), R("Pi"), 2047, OP.bitwise_and)
+        ts(R("Bv"), R("Pi"), 11, OP.arith_shift_right)
+        tt(R("sm"), R("A"), R("Bv"), OP.add)
+
+    def hash_back(y):
+        tt(R("pr"), R("A"), R("Bv"), OP.mult)
+        ts(R("h", 0, 16), R("pr", 0, 16), 3, OP.arith_shift_right, 4095, OP.bitwise_and)
+        ts(R("h", 16, 128), R("pr", 16, 128), 3, OP.arith_shift_right, 511, OP.bitwise_and)
+        for k in range(1, 8):
+            tt(R("h", 16 * k, 16 * k + 16), R("h", 16 * k, 16 * k + 16), R("h", 16 * k - 16, 16 * k), OP.add)
+        tt(R(y), R("h"), Pk, OP.add)
+        ts(R(y), R(y), 4095, OP.bitwise_and)
+
+    def lanes_win():
+        tt(R("winR", 0, 256, 1, 8), R("PSA", 0, 256, 1, 8), R("thrR", 0, 256, 1, 8), OP.is_le)
+        conv1("PSD", [("winR", 8, R("PK8", 0, 128, 1, 8))])
+
+    def gather_front(t, between):
+        gt = "got%d" % (t & 1)
+        for h in range(2):
+            lo = 1024 * h
+            if h == 1 and t > 0: lanes_win()
+            act(R(gt, lo, lo + 1024), IX(R("V", VB, DB), R("c16", 64 * h, 64 * h + 64)))
+            tt(R("mx", lo, lo + 1024), IX(R("V", VB, DB), R("c16", 64 * h, 64 * h + 64)), R("V", Ecur[0] + lo, Ecur[0] + lo + 1024), OP.max)
+            out_send(t, "b%d" % h, R(gt, lo, lo + 1024))
+            if h == 0: P_chunk(gt, 0, h)
+        for h in range(2):
+            if h == 1:
+                if t > 0: conv2("PSD", 0, "q1")
+                P_chunk(gt, 0, h)
+                between()
+            together(lambda: [mm(R("PSM", 64 * h, 64 * h + 64), R("SEL2", 128 * i, 128 * i + 128), R("mx", 1024 * h + i, 1024 * h + 1024, 16),
+                                 i == 0, i == 15) for i in range(16)])
+
+    def list_table():
+        act(R("cR"), IX(R("IW", 0, 4096), R("c16")), scale=2048.0)
+        dma("y", T.K[0:128:2, :], T.cR[0:128:16, :], [("cR", 0, 2048)], [("K", 0, 256)])
+        dma("y", T.K[1:128:2, :], T.cR[0:128:16, :], [("cR", 0, 2048)], [("K", 256, 512)])
+
+    def tree(src, out, op):
+        tt(R("red", 0, 64), R(src, 0, 64), R(src, 64, 128), op)
+        tt(R("red", 64, 96), R("red", 0, 32), R("red", 32, 64), op)
+        tt(out, R("red", 64, 80), R("red", 80, 96), op)
+
+    def flags_front():
+        hash_front()
+        tt(R("d1"), R("PSM", 0, 128), R("sm"), OP.subtract)
+        tt(R("bd"), R("d1"), Pthr, OP.is_gt)
+        tree("bd", L("tr"), OP.add)
+
+    for h in range(2): P_chunk("V", E0, h)
+    hash_front()
+    cp(PsE, R("sm"))
+    gather_front(0, lambda: None)
+    hash_back("yI1")
+    cp(R("NCE"), R("yI1"))
+    ts(Pthr, PsE, 150.0, OP.add)
+    ts(R("t2"), R("t1"), -1.0 / 32, OP.mult, 1.0 / 32, OP.add)
+    tree("t2", L("n32"), OP.add)
+    flags_front()
+    tt(R("code0"), L("tr"), L("n32"), OP.add)
+    out_send(0, "co", R("code0"))
+    hash_back("yI0")
+    out_send(0, "nc", R("yI0"))
+    cp(L("cur"), R("jW", 0, 16)); cp(R("cur16"), L("cur"))
+    scatter_act(IX(R("LK"), R("ei16")), R("LV0"))
+    list_table()
+    lna = math.log(1.75)
+    ts(L("lm"), R("jW", 0, 16), -128.0, OP.add)
+    act(L("wW"), L("lm"), AF.Exp, -lna)
+    ts(R("thrR"), R("OR"), -128.0, OP.add)
+    act(R("thrR"), R("thrR"), AF.Exp, -lna)
+    ts(R("thrR"), R("thrR"), 2.5, OP.mult)
+    ts(Pkb, Pk, 4096.0, OP.mult)
+    ts(R("t1"), R("t1"), 65536.0, OP.mult)
+    tt(R("HB"), R("t1"), Pkb, OP.add)
+    ts(R("kp1"), Pk, 1.0, OP.add)
+    ts(C(6), C(0), 0.0, OP.is_equal)
+    ts(C(7), C(0), 1.0, OP.is_equal)
+    ts(C(8), C(0), 1.0, OP.add, 0.5, OP.mult)
+    for t in range(STEPS):
+        ts(C(10 + t), C(1), float(t + 2), OP.mult, 64.0, OP.add)
+    fill(C(16), -2048.0); fill(C(17), -64.0)
+    ts(R("PKP"), R("B128"), C(6), OP.mult)
+    ts(R("PKH"), R("B128"), C(6), OP.mult)
+    ts(R("PKO"), R("B128"), C(7), OP.mult)
+    cp(R("B8"), R("B128", 0, 128, 16))
+    cp(R("B8H"), R("B128", 0, 128, 16))
+    ts(R("MK"), R("clOp"), C(0), OP.is_equal)
+    mm(R("PSD", 0, 128, 1, 8), R("PKP", 0, 128, 16), R("PKP"), True, True)
+    cp(R("PK8", 0, 128, 1, 8), R("PSD", 0, 128, 1, 8))
+    ts(R("JC"), R("OR"), C(3), OP.add)
+    ts(R("DUM", 0, 24), R("jW", 0, 24), 4096.0, OP.add, 2048.0, OP.mult)
+    ts(R("DUM", 24, 48), R("jW", 0, 24), 4096.0, OP.add, 2048.0, OP.mult)
+    ts(L("dm256"), R("jW", 0, 16), 256.0, OP.add)
+    ts(L("dm4096"), R("jW", 0, 16), 4096.0, OP.add)
+    fill(L("z"), 0.0); fill(L("dec"), 0.0); fill(R("ZB"), 0.0)
+    fill(R("V", DB, E1), 0.0)
+    ts(R("BTM"), R("BTM"), -1.0, OP.mult)
+    cp(R("dec16"), L("dec"))
+
+    def renew_state(y):
+        tt(R("t1"), R("sm"), PsE, OP.subtract)
+        tt(R("t1"), R("t1"), Pdp, OP.mult)
+        tt(PsE, PsE, R("t1"), OP.add)
+        tt(R("t2"), R(y), R("NCE"), OP.subtract)
+        tt(Pt, R("t2"), Pdp, OP.mult)
+        tt(R("NCE"), R("NCE"), Pt, OP.add)
+
+    def lanes_pre(t, between):
+        tt(R("key"), R("HB"), Pc, OP.add)
+        tree("key", L("keyv"), OP.min)
+        cp(R("keI"), L("keyv"))
+        ts(R("ceI"), R("keI"), 4095, OP.bitwise_and)
+        ts(L("full"), L("keyv"), 65536.0, OP.is_ge, 4096.0, OP.mult)
+        tt(L("x1"), R("ceI"), L("full"), OP.max)
+        cp(R("cl16"), L("x1"))
+        act(R("clOp"), IX(R("IW"), R("cl16")))
+        act(R("clR"), IX(R("clOp"), R("cur16")), bias=C(16))
+        act(R("decR"), IX(R("IW", 0, 8), R("dec16")), scale=-1.0)
+        act(R("OPW", 0, 256), R("ZB"))
+        act(R("LV"), IX(R("IW", 0, 256), R("cur16")), scale=C(2), bias=C(10 + t))
+        conv1("PSA", [("clR", 128, R("PKH"))])
+        ts(R("fkI"), R("keI"), 12, OP.arith_shift_right)
+        ts(L("fk1"), R("fkI"), 1.0, OP.add)
+        ts(R("acI"), R("wkI"), t, OP.arith_shift_right, 1, OP.bitwise_and)
+        cp(L("act"), R("acI"))
+        act(R("COMP", 0, 48), R("DUM"))
+        between()
+        conv2("PSA", 0, "qh", "B8H")
+        tt(R("t4"), Pkb, R("HB"), OP.subtract)
+        cp(L("clS"), R("PSA", 0, 16))
+        ts(L("cl"), L("clS"), 2048.0, OP.add)
+        cp(R("lc16"), L("cl"))
+        act(R("G1"), IX(R("LK", 0, LW), R("lc16")), bias=C(17))
+
+    def judge(t):
+        tt(L("X"), R("code%d" % (t & 1)), R("lc%d" % t), OP.add)
+        ts(R("rdy"), L("X"), 0.0, OP.is_equal)
+        together(lambda: [mm(R("PSR", 0, 16), R("B128"), R("rdy"), True, True), mm(R("PSR", 16, 32), R("BTM"), R("rdy"), True, True)])
+        conv1("PSA", [("G1", 128, R("PKP"))])
+        ts(R("cab", 16, 32), L("X"), 1.0, OP.is_ge)
+        ts(L("nr"), L("X"), 0.0, OP.is_gt)
+        tt(L("e"), L("dm256"), L("nr"), OP.mult)
+        comp("v", [R("PSR", 0, 16), L("z")], [L("inc")],
+             lambda r, w: g.vector.tensor_tensor_scan(ap(w[0]), ap(r[0]), ap(r[1]), 0.0, OP.add, OP.add))
+        tt(L("rank"), R("PSR", 16, 32), L("inc"), OP.add)
+        ts(L("cm"), L("rank"), 48.0, OP.is_lt)
+        tt(R("cab", 0, 16), L("cm"), R("rdy"), OP.mult)
+        tt(L("done"), R("cab", 0, 16), R("cab", 16, 32), OP.add)
+        cp(R("dn16"), L("done"))
+        act(R("dnR"), IX(R("IW", 0, 8), R("dn16")))
+        act(R("gnR"), IX(R("dnR"), R("cur16")))
+        tt(L("x5"), L("rank"), L("e"), OP.max)
+        cp(R("off16"), L("x5"))
+        conv2("PSA", 16, "q0")
+        together(lambda: [mm(R("PSC", 128 * j + 16 * k, 128 * j + 16 * k + 16), R("ID"), R("cab", 16 * j, 16 * j + 16), True, True)
+                          for j in range(2) for k in range(8)])
+        conv1("PSR", [("gnR", 128, R("PKP"))])
+        comp("v", [("n", "K", 0, 512, 1, 128), R("JC")], [IX(R("COMP"), R("off16"))],
+             lambda r, w: g.vector.tensor_tensor(out=ap(w[0]), in0=T.K[:], in1=T.JC[:], op=OP.add))
+        cp(R("p16"), R("PSA", 16, 32))
+        cp(L("p"), R("p16"))
+        ts(R("Lt", 0, 24), R("COMP", 0, 24), C(2), OP.mult)
+        ts(R("Lt", 24, 48), R("COMP", 24, 48), C(1), OP.mult)
+        tt(R("Ls", 0, 24), R("Lt", 0, 24), R("Lt", 24, 48), OP.add)
+        ts(R("Ls", 24, 48), R("Ls", 0, 24), 2047, OP.bitwise_and)
+        cp(R("L16", 0, 24), R("Ls", 24, 48))
+        act(R("decL"), IX(R("decR"), R("p16")))
+        act(R("Dl"), IX(R("lb%d" % t), R("L16", 0, 24)))
+        conv1("PSA", [("G1", 128, R("PKO")), ("decL", 128, R("PKP"))])
+        ts(R("Ls", 48, 72), R("Ls", 0, 24), 11, OP.arith_shift_right)
+        cp(R("L16", 24, 48), R("Ls", 48, 72))
+        conv2("PSR", 32, "q1")
+        for c in range(16):
+            ts(R("EQ", 272 * c, 256 * c + 256), R("clR", 16 * c, 256), L("clS", c, c + 1), OP.is_equal)
+        conv2("PSA", 32, "q0")
+        ts(L("nf"), L("cl"), 4096.0, OP.is_lt)
+        tt(L("an"), L("act"), L("nf"), OP.mult)
+        tt(R("t3"), R("NCE"), Pc, OP.subtract)
+        ts(L("val"), R("PSA", 32, 48), 0.0, OP.is_gt)
+        tt(L("mv"), L("an"), L("val"), OP.mult)
+        tt(L("cand"), L("an"), L("mv"), OP.subtract)
+
+    def lanes_moves():
+        tt(L("x1"), L("p"), L("cur"), OP.subtract)
+        tt(L("x1"), L("x1"), L("mv"), OP.mult)
+        tt(L("cur1"), L("cur"), L("x1"), OP.add)
+        tt(L("x4"), R("jW", 0, 16), L("cur1"), OP.subtract)
+        tt(L("x4"), L("x4"), R("PSR", 32, 48), OP.mult)
+
+    def new_cells(t):
+        tt(R("t1"), R("ln%d" % t), Pc, OP.subtract)
+        tt(R("t1"), R("t1"), R("PSC", 0, 128), OP.mult)
+        tt(R("t2"), R("t3"), R("PSC", 128, 256), OP.mult)
+        tt(Pc, Pc, R("t1"), OP.add)
+        tt(Pc, Pc, R("t2"), OP.add)
+        cp(R("c16"), Pc)
+
+    def commit_columns():
+        cp(IX(R("V", VB, E1), R("L16", 24, 48)), R("Dl"))
+
+    def masks():
+        cp(R("cmS"), R("PSC", 0, 128))
+        tt(Pdp, R("PSC", 128, 256), R("cmS"), OP.add)
+
+    def thresholds():
+        ts(R("t1"), Pdp, BIG, OP.mult, 150.0, OP.add)
+        tt(Pthr, PsE, R("t1"), OP.add)
+
+    def lanes_claim():
+        ts(L("x6"), R("PSR", 32, 48), -1.0, OP.mult, 1.0, OP.add)
+        tt(L("ac"), L("x6"), L("cand"), OP.mult)
+        tt(L("aw"), L("ac"), L("wW"), OP.mult)
+        for k in range(8):
+            ts(R("LH", 16 * k, 16 * k + 16), L("aw"), R("GC", k, k + 1), OP.mult)
+        together(lambda: [mm(R("PSA", 16 * c, 256, 1, 8), R("LH", c, 128, 16), R("EQ", 272 * c, 256 * c + 256), c == 0, c == 15) for c in range(16)])
+
+    def lanes_out(t):
+        tt(L("win"), L("ac"), R("PSD", 0, 16), OP.mult)
+        ts(L("lose"), L("win"), -1.0, OP.mult, 1.0, OP.add)
+        tt(L("x1"), L("lose"), L("dm256"), OP.mult)
+        tt(L("x1"), L("x1"), L("cur"), OP.max)
+        cp(R("oo16"), L("x1"))
+        cp(IX(R("OPW"), R("oo16")), R("ONE"))
+        conv1("PSD", [("OPW", 128, R("PKP"))])
+        lanes_moves()
+        conv2("PSD", 16, "q1")
+        if t < STEPS - 1:
+            tt(L("x5"), L("lose"), L("dm4096"), OP.mult)
+            tt(L("x5"), L("x5"), L("cl"), OP.max)
+            cp(R("ol16"), L("x5"))
+            ts(L("x6"), L("n32"), -1.0, OP.mult, 0.25, OP.add)
+            tt(L("x6"), L("x6"), L("done"), OP.mult)
+            tt(L("n32a"), L("n32"), L("x6"), OP.add)
+            ts(L("x6"), L("done"), float(t + 2), OP.mult)
+            tt(L("dec"), L("dec"), L("x6"), OP.max)
+            cp(R("dec16"), L("dec"))
+            tt(L("cur"), L("cur1"), L("x4"), OP.add)
+            cp(R("cur16"), L("cur"))
+        else:
+            tt(L("cur"), L("cur1"), L("x4"), OP.add)
+
+    def holders():
+        tt(R("rw"), L("fk1"), R("PSD", 16, 32), OP.mult)
+        together(lambda: [mm(R("PSD", 128 + 16 * k, 144 + 16 * k), R("ID"), R("rw"), True, True) for k in range(8)])
+
+    def holders2():
+        tt(Pt, R("t4"), Pdp, OP.mult)
+        tt(R("HB"), R("HB"), Pt, OP.add)
+        tt(R("t5"), R("PSD", 128, 256), R("kp1"), OP.is_equal)
+        ts(Pu, R("t5"), 65536.0, OP.mult)
+        tt(R("HB"), R("HB"), Pu, OP.add)
+
+    def snap_window():
+        if Ecur[0] == E0: return E0, E1, E1, "eaA", "ejA"
+        return VB, VE, E0, "eaB", "ejB"
+
+    def snap_index():
+        lo, hi, new, ea, ej = snap_window()
+        tt(R("t5"), R(ea), Pc, OP.add)
+        tt(Pt, R("t5"), Pdp, OP.mult)
+        tt(R("t5"), R(ej), Pt, OP.add)
+        cp(R("ei16"), R("t5"))
+
+    def snap_gather():
+        lo, hi, new, ea, ej = snap_window()
+        act(R("V", new, new + 2048), IX(R("V", lo, hi), R("ei16")))
+        Ecur[0] = new
+
+    def const_last():
+        cp(R("GC"), R("B128", 0, 128, 16))
+        for ea, ej, vb, eb in (("eaA", "ejA", VB - E0, 0), ("eaB", "ejB", 0, E1 - VB)):
+            ts(R(ej), R("jW"), float(eb), OP.add)
+            ts(R(ea), R("jW"), -1.0, OP.mult, float(vb - eb), OP.add)
+
+    lanes_pre(0, const_last)
+    for t in range(STEPS):
+        judge(t)
+        lanes_claim()
+        new_cells(t)
+        commit_columns()
+        if t == STEPS - 1: break
+        n = t + 1
+        gather_front(n, lambda: lanes_out(t))
+        list_table()
+        masks()
+        thresholds()
+        if t < STEPS - 2:
+            snap_index()
+            snap_gather()
+        if t == 0: act(R("SELW"), R("SEL2"), scale=C(8))
+        scatter_act(IX(R("LK", 0, 4352), R("ol16")), R("LV"))
+        flags_front()
+        ts(L("wo"), R("PSD", 16, 32), -1.0 / 32, OP.mult)
+        tt(L("n32"), L("n32a"), L("wo"), OP.add)
+        tt(R("code%d" % (n & 1)), L("tr"), L("n32"), OP.add)
+        out_send(n, "co", R("code%d" % (n & 1)))
+        holders()
+        hash_back("yI%d" % (n & 1))
+        out_send(n, "nc", R("yI%d" % (n & 1)))
+        holders2()
+        lanes_pre(n, lambda: renew_state("yI%d" % (n & 1)))
+    t = STEPS - 1
+    masks()
+
+    def weigh(a, b2):
+        for b in range(a, b2):
+            mm(R("PSP", 0, 256), R("SELW", 128 * b, 128 * b + 128), R("V", VB + 256 * b, VB + 256 * b + 256), b == 0, b == 15)
+
+    weigh(0, 3)
+    lanes_win()
+    conv2("PSD", 0, "q1")
+    cp(R("sm"), Pc)
+    dma("y", T.yc[:], T.sm[:], [("sm", 0, 128)], [])
+    weigh(3, 10)
+    lanes_out(t)
+    last = res(L("cur"))
+    dma("s", T.yl[:], ap(last), flat(last), [])
+    holders()
+    weigh(10, 16)
+    holders2()
+    ts(R("d1"), R("HB"), 65536.0, OP.is_ge)
+    dma("y", T.yh[:], T.d1[:], [("d1", 0, 128)], [])
+    cp(R("yso"), R("PSP", 0, 256))
+    dma("s", T.ys[:], T.yso[:], [("yso", 0, 256)], [])
+    build()
+    for sem in sorted(cnt):
+        if known["g"].get(sem, 0) < cnt[sem]:
+            g.wait_ge(T.sem[sem], cnt[sem])

@@ -1,54 +1,56 @@
-import math
-from concourse.mybir import AluOpType as OP, ActivationFunctionType as AF
+from concourse.mybir import AluOpType as OP, ActivationFunctionType as AF, AxisListType
 
 STEPS = 5
-E0, VB, DB, E1, VE = 0, 2048, 6144, 6528, 8576
-LW = 4112
-LAG = (2.5, 4.5, 6.0, 0.1, 0.15)
+VW = 4096 + 384
+IWW = 4608
+LKW = IWW + 2048
+SNAP, GOT0, E01, GOT1, E2, GOT2, E3, GOT3, E4, GOT4 = (2048 * i for i in range(10))
+GOT = (GOT0, GOT1, GOT2, GOT3, GOT4)
+ES = (E01, E01, E2, E3, E4)
+LAG = (2.5, 4.5, 7.0, 0.1, 0.15)
+HOLD = 1000.0
+CH = (0, 512, 1024, 1536, 2048)
 
 SCRATCH = {
-    "V": ("sbuf", [128, VE], "bfloat16"),
-    "got0": ("sbuf", [128, 2048], "bfloat16"), "got1": ("sbuf", [128, 2048], "bfloat16"),
+    "V": ("sbuf", [128, VW], "bfloat16"), "EB": ("sbuf", [128, 20480], "bfloat16"),
     "mx": ("sbuf", [128, 2048], "bfloat16"), "cR": ("sbuf", [128, 2048], "float32"),
-    "IW": ("sbuf", [128, LW], "float32"), "LK": ("sbuf", [128, 6144], "float32"),
-    "LV0": ("sbuf", [128, 2048], "float32"), "LV": ("sbuf", [128, 256], "float32"),
-    "SEL2": ("sbuf", [128, 2048], "bfloat16"), "SELPK": ("sbuf", [128, 2048], "bfloat16"), "SELW": ("sbuf", [128, 2048], "bfloat16"),
-    "MK": ("sbuf", [128, 256], "bfloat16"), "PKP": ("sbuf", [128, 128], "bfloat16"), "PKO": ("sbuf", [128, 128], "bfloat16"),
-    "PKH": ("sbuf", [128, 128], "float16"), "PK8": ("sbuf", [128, 128], "bfloat16"),
-    "B8": ("sbuf", [128, 8], "bfloat16"), "B8H": ("sbuf", [128, 8], "float16"),
-    "q0": ("sbuf", [128, 256], "bfloat16"), "q1": ("sbuf", [128, 256], "bfloat16"), "qh": ("sbuf", [128, 256], "float16"),
-    "EQ": ("sbuf", [128, 4096], "bfloat16"), "LH": ("sbuf", [128, 128], "bfloat16"),
-    "ONE": ("sbuf", [128, 256], "bfloat16"), "ZB": ("sbuf", [128, 256], "bfloat16"), "OPW": ("sbuf", [128, 512], "bfloat16"),
-    "B128": ("sbuf", [128, 128], "bfloat16"), "BTM": ("sbuf", [128, 128], "bfloat16"), "ID": ("sbuf", [128, 128], "bfloat16"),
+    "IW": ("sbuf", [128, IWW], "float32"), "LK": ("sbuf", [128, LKW], "float32"),
+    "LV": ("sbuf", [128, 256], "float32"), "C64": ("sbuf", [128, 256], "float32"),
+    "SELC": ("sbuf", [128, 2048], "bfloat16"), "SELPK": ("sbuf", [128, 2048], "bfloat16"), "SELW": ("sbuf", [128, 2048], "bfloat16"),
+    "SELT": ("sbuf", [128, 1024], "bfloat16"), "EQ": ("sbuf", [128, 4096], "bfloat16"), "LH": ("sbuf", [128, 128], "bfloat16"),
+    "MK": ("sbuf", [128, 256], "bfloat16"), "qw": ("sbuf", [128, 256], "bfloat16"), "abR": ("sbuf", [128, 256], "bfloat16"),
+    "naL": ("sbuf", [128, 256], "bfloat16"), "o2": ("sbuf", [128, 112], "float32"), "o16": ("sbuf", [128, 32], "uint16"),
+    "ONE": ("sbuf", [128, 128], "bfloat16"), "OPW": ("sbuf", [128, 512], "float32"), "OPB": ("sbuf", [128, 256], "bfloat16"),
     "OR": ("sbuf", [128, 256], "float32"), "JC": ("sbuf", [128, 256], "float32"), "K": ("sbuf", [128, 256], "float32"),
-    "COMP": ("sbuf", [128, 512], "float32"), "DUM": ("sbuf", [128, 48], "float32"), "thrR": ("sbuf", [128, 256], "float32"),
-    "clOp": ("sbuf", [128, 256], "float32"), "clR": ("sbuf", [128, 256], "float16"),
-    "G1": ("sbuf", [128, 256], "bfloat16"), "decR": ("sbuf", [128, 256], "bfloat16"), "decL": ("sbuf", [128, 256], "bfloat16"),
-    "dnR": ("sbuf", [128, 256], "bfloat16"), "gnR": ("sbuf", [128, 256], "bfloat16"), "winR": ("sbuf", [128, 256], "bfloat16"),
+    "COMP": ("sbuf", [128, 512], "float32"), "DUM": ("sbuf", [128, 48], "float32"), "wR": ("sbuf", [128, 256], "float32"),
+    "clOp": ("sbuf", [128, 256], "float32"), "G": ("sbuf", [128, 256], "float32"), "RW": ("sbuf", [128, 512], "float16"),
+    "DR": ("sbuf", [128, 256], "bfloat16"), "decL": ("sbuf", [128, 256], "bfloat16"), "gnR": ("sbuf", [128, 256], "bfloat16"),
     "Dl": ("sbuf", [128, 384], "bfloat16"), "yso": ("sbuf", [128, 256], "float32"),
-    "i1": ("sbuf", [128, 8], "int32"), "col": ("sbuf", [128, 32], "float32"), "GC": ("sbuf", [128, 8], "float32"),
-    "lane": ("sbuf", [128, 688], "float32"), "red": ("sbuf", [128, 128], "float32"),
-    "code0": ("sbuf", [128, 16], "float32"), "code1": ("sbuf", [128, 16], "float32"),
-    "rdy": ("sbuf", [128, 16], "bfloat16"), "rw": ("sbuf", [128, 16], "bfloat16"), "cab": ("sbuf", [128, 32], "bfloat16"),
-    "Ls": ("sbuf", [128, 72], "int32"), "Lt": ("sbuf", [128, 48], "float32"), "L16": ("sbuf", [128, 48], "uint16"),
+    "i1": ("sbuf", [128, 48], "int32"), "col": ("sbuf", [128, 40], "float32"), "B8": ("sbuf", [128, 24], "bfloat16"),
+    "lane": ("sbuf", [128, 640], "float32"), "lb16": ("sbuf", [128, 160], "bfloat16"), "lh16": ("sbuf", [128, 64], "float16"),
+    "code0": ("sbuf", [128, 16], "float32"), "code1": ("sbuf", [128, 16], "float32"), "awk": ("sbuf", [128, 80], "float32"),
+    "Ls": ("sbuf", [128, 48], "int32"), "L16": ("sbuf", [128, 48], "uint16"), "pm16": ("sbuf", [128, 40], "uint16"),
+    "wkI": ("sbuf", [128, 16], "int32"), "wk5": ("sbuf", [128, 80], "int32"), "pI": ("sbuf", [128, 16], "int32"),
 }
-for _n in ("csI", "hdI", "kI", "Pi", "A", "Bv", "pr", "h", "yI0", "yI1"):
+for _n in ("csI", "hdI", "Cz", "cI", "Bv", "hI", "h", "yI0", "yI1"):
     SCRATCH[_n] = ("sbuf", [128, 128], "int32")
-for _n in ("HB", "kp1", "NCE", "sm", "d1", "bd", "cmS", "key", "jW", "eaA", "ejA", "eaB", "ejB", "t1", "t2", "t3", "t4", "t5"):
+for _n in ("jW", "m01", "negk", "mq", "nZ", "t1", "t2", "t3", "z", "yo1", "yo2"):
     SCRATCH[_n] = ("sbuf", [128, 128], "float32")
-for _n in ("c16", "ei16"):
+for _n in ("B128", "UT", "ID", "IDn", "IDk", "IDb", "HALF", "HALFn", "ZB", "bd", "GM"):
+    SCRATCH[_n] = ("sbuf", [128, 128], "bfloat16")
+SCRATCH["posH"] = ("sbuf", [128, 128], "float16")
+for _n in ("c16", "ei16", "ck16", "lk16"):
     SCRATCH[_n] = ("sbuf", [128, 128], "uint16")
-for _n in ("wkI", "keI", "ceI", "fkI", "acI"):
-    SCRATCH[_n] = ("sbuf", [128, 16], "int32")
-for _n in ("cl16", "cur16", "lc16", "p16", "dn16", "off16", "oo16", "ol16", "dec16"):
+for _n in ("cl16", "cur16", "p16", "off16", "ab16", "dec16"):
     SCRATCH[_n] = ("sbuf", [128, 16], "uint16")
 for _t in range(STEPS):
     SCRATCH["lb%d" % _t] = ("sbuf", [128, 2048], "bfloat16")
     SCRATCH["lc%d" % _t] = ("sbuf", [128, 16], "float32")
     SCRATCH["ln%d" % _t] = ("sbuf", [128, 128], "int32")
-for _n in ("PSP", "PSM", "PSC", "PSR", "PSA", "PSD", "V0", "V1"):
+for _n in ("PD", "PP", "PR", "PX", "PL", "PW", "V0", "V1"):
     SCRATCH[_n] = ("psum", [128, 512], "float32")
-PLACES = {"lane": 4, "q0": 3, "q1": 2, "t1": 3, "t2": 3, "t5": 3, "Pi": 2, "A": 2, "Bv": 2, "key": 2, "cl16": 2, "p16": 2}
+PLACES = {"lane": 3, "lb16": 3, "lh16": 2, "t1": 3, "t2": 3, "t3": 2, "Bv": 2, "hI": 2, "h": 2, "z": 2, "cl16": 2, "p16": 2, "c16": 2,
+          "cI": 2, "pI": 2, "mq": 2, "LV": 2, "cur16": 2}
 for _n in PLACES:
     SCRATCH[_n] = (SCRATCH[_n][0], [128, SCRATCH[_n][1][1] * PLACES[_n]], SCRATCH[_n][2])
 
@@ -59,9 +61,12 @@ for _t in range(STEPS):
         SEMAPHORES += ["a%s%d" % (_m, _t), "l%s%d" % (_m, _t)]
 
 _L = {}
-for _i, _n in enumerate("cur cl clS p act nf an mv cand ac aw wW dm256 dm4096 win cur1 x1 x2 x3 x4 x5 x6 X rank inc e cm done n32 n32a wo "
-                        "keyv full tr z lm fk1 dec val nr lose".split()):
-    _L[_n] = 16 * _i
+for _b, _names in (("lane", "cur cl clS s8 val mv cand candw wW dum q q2 q3 cur1 e1 e2 ng fd f0 dst dec ncode thrab "
+                            "d8 w1 z0 c511 thrT clB dB clA x1 x2 qq"),
+                   ("lb16", "ab cm sel done w aw winT"), ("lh16", "rdy incl rc c511h")):
+    for _i, _n in enumerate(_names.split()):
+        _L[_n] = (_b, 16 * _i)
+TILED = ("lane", "lb16", "lh16")
 
 
 def landing(m, t):
@@ -75,34 +80,32 @@ def route(core, t, T, topo):
     dst = T.cores[T.rank_of(core) ^ (1 + t % 7)]
     near = [x for x in topo.cores_of(core) if x != core and topo.die(x) == topo.die(core) and topo.may_write(x, dst)]
     far = [x for x in topo.cores_of(core) if topo.die(x) != topo.die(core) and topo.may_write(x, dst)]
-    via = {"b0": near[-1], "b1": near[-2], "co": None, "nc": None}
-    if not topo.may_write(core, dst):
-        via["co"] = far[0]; via["nc"] = far[1]
+    via = {"b0": far[0], "b1": far[1], "co": None, "nc": near[0]}
+    if not topo.may_write(core, dst): via["co"] = near[-1]
     return dst, via
-
-
-def engines8(topo, a, b):
-    return sum(1 << e for e in topo.engines(a, b)[:8])
 
 
 def send(g, T, topo, core, dst, m, t, src):
     buf, lo, hi = landing(m, t)
     rid, pid = topo.addr(dst, core)
+    es = topo.engines(core, dst)
     return g.remote_dma(out_ap=T[buf][:, lo:hi], in_ap=src, remote_sem=T.sem["a%s%d" % (m, t)], local_sem=T.sem["l%s%d" % (m, t)],
-                        pid=pid, routing_id=rid, dma_engine_mask=engines8(topo, core, dst))
+                        pid=pid, routing_id=rid, dma_engine_mask=sum(1 << e for e in (es[:8] if m == "co" else es[-8:])))
 
 
 def relay_program(g, core, T, topo):
     for src in [x for x in topo.cores_of(core) if T.rank_of(x) is not None]:
+        done = []
         for t in range(STEPS):
             dst, via = route(src, t, T, topo)
-            mine = [m for m in MSG if via[m] == core]
-            for m in mine:
+            for m in MSG:
+                if via[m] != core: continue
                 buf, lo, hi = landing(m, t)
                 g.wait_ge(T.sem["a%s%d" % (m, t)], 8)
                 send(g, T, topo, core, dst, m, t, T[buf][:, lo:hi])
-            for m in mine:
-                g.wait_ge(T.sem["l%s%d" % (m, t)], 8)
+                done.append("l%s%d" % (m, t))
+        for s in done:
+            g.wait_ge(T.sem[s], 8)
 
 
 def rank_program(g, core, T, topo):
@@ -118,23 +121,22 @@ def rank_program(g, core, T, topo):
     cnt = {}
     nd = [0]
 
-    def R(b, lo=0, hi=None, st=1, np=128):
-        return ("n", b, lo, width[b] if hi is None else hi, st, np)
+    def R(b, lo=0, hi=None, st=1):
+        return ("n", b, lo, width[b] if hi is None else hi, st)
 
-    def L(n, a=0, b=16):
-        return ("n", "lane", _L[n] + a, _L[n] + b, 1, 128)
+    def L(n):
+        return ("n", _L[n][0], _L[n][1], _L[n][1] + 16, 1)
 
     def C(i):
-        return ("n", "col", i, i + 1, 1, 128)
+        return ("n", "col", i, i + 1, 1)
 
     def IX(w, o):
         return ("i", w, o)
 
     def ap(s):
         if s[0] == "i": return ap(s[1]).indirect(ap(s[2]))
-        p = slice(0, s[5]) if s[5] < 128 else slice(None)
-        if s[4] == 1: return T[s[1]][p, s[2]:s[3]]
-        return T[s[1]][p, s[2]:s[3]:s[4]]
+        if s[4] == 1: return T[s[1]][:, s[2]:s[3]]
+        return T[s[1]][:, s[2]:s[3]:s[4]]
 
     def flat(s):
         if not isinstance(s, tuple): return []
@@ -182,10 +184,10 @@ def rank_program(g, core, T, topo):
         b = s[1]
         if b not in PLACES: return s
         wd = width[b]
-        key = (b, s[2] // 16) if b == "lane" else b
-        if w and (s[3] - s[2] == (16 if b == "lane" else wd)): ver[key] = (ver.get(key, -1) + 1) % PLACES[b]
+        key = (b, s[2] // 16) if b in TILED else b
+        if w and s[4] == 1 and (s[3] - s[2] == (16 if b in TILED else wd)): ver[key] = (ver.get(key, -1) + 1) % PLACES[b]
         sh = ver.get(key, 0) * wd
-        return ("n", b, s[2] + sh, s[3] + sh, s[4], s[5])
+        return ("n", b, s[2] + sh, s[3] + sh, s[4])
 
     recs = []
     group = []
@@ -202,13 +204,13 @@ def rank_program(g, core, T, topo):
     def span(q, kind, r, w):
         out, n = w[0], wid(w[0])
         cyc = n
-        if out[0] == "i": cyc = 3.8 * n
-        elif any(isinstance(x, tuple) and x[0] == "i" for x in r): cyc = 1.56 * n
-        elif q == "t": cyc = max(64, wid(r[1]))
+        if out[0] == "i": cyc = 3.8 * n + 50
+        elif any(isinstance(x, tuple) and x[0] == "i" for x in r): cyc = 1.56 * n + 50
+        elif q == "t": return 1.1 * 0.00083 * max(64, wid(r[1]))
         elif kind == "tt": cyc = n if any(ispsum[x[1]] for x in r) else 2 * n
         elif q == "g": cyc = 2 * n + 150
-        elif q == "v" and kind == "ts" and short(out) and all(short(x) for x in r[:1]): cyc = n / 2
-        return 1.2 * (max(64, cyc) * 0.00083 + (0.06 if q == "s" else 0.01))
+        elif q == "v" and short(out) and all(short(x) for x in r[:1]): cyc = n / 2
+        return 1.1 * (max(64, cyc) * 0.00083 + (0.06 if q == "s" else 0.01))
 
     def comp(q, reads, writes, fn, kind="ts"):
         r = [res(x) for x in reads]
@@ -230,8 +232,8 @@ def rank_program(g, core, T, topo):
         got = group.pop()
         recs.append(("t", [x[0] for x in got], sum(x[1] for x in got), "c", None))
 
-    def dma(q, out, in_, reads, writes):
-        recs.append((q, [(reads, writes, lambda: Q[q].dma_start(out, in_))], 0.06, "d", 2.5))
+    def dma(q, out, in_, reads, writes, lag=2.5):
+        recs.append((q, [(reads, writes, lambda: Q[q].dma_start(out, in_))], 0.06, "d", lag))
 
     def out_send(t, m, srcspec):
         s = res(srcspec)
@@ -242,6 +244,7 @@ def rank_program(g, core, T, topo):
     def build():
         n = len(recs)
         pred = [set() for _ in range(n)]
+        banks = [set() for _ in range(n)]
         old = {}
         for i in range(n):
             q = recs[i][0]
@@ -249,9 +252,10 @@ def rank_program(g, core, T, topo):
                 for b, lo, hi, w in [(b, lo, hi, False) for b, lo, hi in rd] + [(b, lo, hi, True) for b, lo, hi in wr]:
                     hl = old.setdefault(b, [])
                     for lo2, hi2, w2, d in hl:
-                        if d != i and ((ispsum.get(b, False) and recs[d][0] != q) or (lo < hi2 and lo2 < hi and (w or w2))): pred[i].add(d)
-                    if w and not ispsum.get(b, False): hl[:] = [x for x in hl if not (lo <= x[0] and x[1] <= hi)]
+                        if d != i and lo < hi2 and lo2 < hi and (w or w2): pred[i].add(d)
+                    if w: hl[:] = [x for x in hl if not (lo <= x[0] and x[1] <= hi)]
                     hl.append((lo, hi, w, i))
+                    if ispsum.get(b, False): banks[i].add(b)
             if recs[i][3] == "a": pred[i].add(sent[recs[i][4]])
         succ = [[] for _ in range(n)]
         for i in range(n):
@@ -268,7 +272,7 @@ def rank_program(g, core, T, topo):
 
         prio = [0.0] * n
         for i in range(n - 1, -1, -1):
-            prio[i] = recs[i][2] + max([lag(i, j) + prio[j] for j in succ[i]] + [0.0])
+            prio[i] = recs[i][2] + max([lag(i, j) + prio[j] for j in succ[i]] + [recs[i][4] if recs[i][3] == "d" else 0.0])
         left = [len(p) for p in pred]
         est = [0.0] * n
         ready = {}
@@ -276,17 +280,27 @@ def rank_program(g, core, T, topo):
         for i in range(n):
             if left[i] == 0: ready.setdefault(recs[i][0], []).append(i)
         order = []
+        held = {}
+
+        def when(i):
+            return max([est[i]] + [e + LAG[4] for b in banks[i] for q2, e in held.get(b, {}).items() if q2 != recs[i][0]])
+
         for _ in range(n):
             best = None
             for q, rl in ready.items():
                 if not rl: continue
-                t0 = max(free.get(q, 0.0), min(est[i] for i in rl))
+                t0 = max(free.get(q, 0.0), min(when(i) for i in rl))
                 if best is None or t0 < best[0]: best = (t0, q)
             t0, q = best
-            i = max([x for x in ready[q] if est[x] <= t0 + 1e-9], key=lambda x: (prio[x], -x))
+            can = [x for x in ready[q] if when(x) <= t0 + 1e-9]
+            i = max(can, key=lambda x: (prio[x], -x))
+            soon = [x for x in ready[q] if t0 < when(x) < t0 + recs[i][2] and prio[x] - prio[i] > HOLD * (when(x) - t0) + recs[i][2]]
+            if soon:
+                i = min(soon, key=when); t0 = when(i)
             ready[q].remove(i)
             order.append(i)
             end = t0 + recs[i][2]
+            for b in banks[i]: held.setdefault(b, {})[q] = end
             if q != "net": free[q] = end
             for j in succ[i]:
                 est[j] = max(est[j], end + lag(i, j))
@@ -332,18 +346,24 @@ def rank_program(g, core, T, topo):
     def fill(out, x):
         comp("v", [], [out], lambda r, w: g.vector.memset(ap(w[0]), x), "fill")
 
+    def scan(out, d0, d1, op0, op1):
+        comp("v", [d0, d1], [out], lambda r, w: g.vector.tensor_tensor_scan(ap(w[0]), ap(r[0]), ap(r[1]), 0.0, op0, op1))
+
+    def reduce_add(out, a):
+        comp("v", [a], [out], lambda r, w: g.vector.tensor_reduce(ap(w[0]), ap(r[0]), AxisListType.X, OP.add))
+
     def act(out, a, func=AF.Copy, scale=1.0, bias=None):
         def call(r, w):
             sc = ap(r[1]) if isinstance(scale, tuple) else scale
             if bias is None: return g.scalar.activation(out=ap(w[0]), in_=ap(r[0]), func=func, scale=sc)
-            return g.scalar.activation(out=ap(w[0]), in_=ap(r[0]), func=AF.Identity, bias=ap(r[2]), scale=sc)
+            return g.scalar.activation(out=ap(w[0]), in_=ap(r[0]), func=AF.Identity if func == AF.Copy else func, bias=ap(r[2]), scale=sc)
         comp("s", [a, scale, bias], [out], call)
 
     def scatter_act(out, a):
         comp("s", [a], [out], lambda r, w: g.scalar.activation(out=ap(w[0]), in_=ap(r[0]), func=AF.Silu))
 
-    def mm(out, lhsT, rhs, start, stop):
-        comp("t", [lhsT, rhs], [out], lambda r, w: g.tensor.matmul(ap(w[0]), ap(r[0]), ap(r[1]), start, stop))
+    def mm(out, lhsT, rhs, start, stop, whole=None):
+        comp("t", [lhsT, rhs], [out] + ([whole] if whole else []), lambda r, w: g.tensor.matmul(ap(w[0]), ap(r[0]), ap(r[1]), start, stop))
 
     def iota(out, pattern, base, cm, after=()):
         comp("g", list(after), [out], lambda r, w: g.iota(ap(w[0]), pattern, base, cm, allow_small_or_imprecise_dtypes=True))
@@ -351,401 +371,395 @@ def rank_program(g, core, T, topo):
     def asel(out, a, pattern, op, base, cm):
         comp("g", [a], [out], lambda r, w: g.affine_select(ap(w[0]), ap(r[0]), pattern, op, 0.0, base, cm))
 
-    def conv1(bank, parts):
+    def to_list(out, sel, src, lo, n):
+        together(lambda: [mm(out, R(sel, 128 * i, 128 * i + 128), R(src, lo + i, lo + n, 16), i == 0, i == 15) for i in range(16)])
+
+    def spread(lo, diag, src, first=None):
         def run():
-            for h in range(2):
-                for n, (src, np, pick) in enumerate(parts):
-                    mm(R(bank, 256 + 128 * h, 384 + 128 * h), R(src, 128 * h, 128 * h + 128, 1, np), pick, n == 0, n == len(parts) - 1)
+            if first: mm(R("PX", lo, lo + 128), first[0], first[1], True, False)
+            for k in range(8):
+                mm(R("PX", lo + k, lo + 128, 8), R(diag), src, not first, not first or k == 7)
         together(run)
 
-    def conv2(bank, lo, q, b8="B8"):
-        tt(R(q), R(bank, 256, 512), R("MK"), OP.mult)
-        together(lambda: [mm(R(bank, lo + 8 * h, lo + 8 * h + 8), R(q, 128 * h, 128 * h + 128), R(b8), True, True) for h in range(2)])
-
-    BIG = 1.0e6
-    Pc, PsE, Pdp, Pt = (R("V0", 128 * i, 128 * i + 128) for i in range(4))
-    Pthr, Pk, Pkb, Pu = (R("V1", 128 * i, 128 * i + 128) for i in range(4))
+    Pa, Pb, Pc, Pk = (R("V0", 128 * i, 128 * i + 128) for i in range(4))
+    Pd, Pe, Pf, Pg = (R("V1", 128 * i, 128 * i + 128) for i in range(4))
+    SX, DX, IXD, WX = (R("PX", 128 * i, 128 * i + 128) for i in range(4))
+    RA, BS = R("PR", 0, 16), R("PR", 16, 32)
+    DM = (R("o2", 0, 16), R("o2", 16, 32), R("o2", 32, 48))
+    oL = R("jW", 0, 16)
 
     dma("y", T.csI[:], T.cs[:], [], [("csI", 0, 128)])
+    dma("s", T.EB[:, SNAP:SNAP + 2048], T.snap[:], [], [("EB", SNAP, SNAP + 2048)], 3.0)
+    dma("y", T.V[:, 0:4096], T.x[:], [], [("V", 0, 4096)], 4.0)
     dma("y", T.hdI[:], T.hold[:], [], [("hdI", 0, 128)])
-    dma("y", T.V[:, VB:DB], T.x[:], [], [("V", VB, DB)])
-    dma("y", T.V[:, E0:E0 + 2048], T.snap[:], [], [("V", E0, E0 + 2048)])
     dma("y", T.wkI[:], T.wake[:], [], [("wkI", 0, 16)])
     fill(R("ONE"), 1.0)
     iota(R("i1", 0, 1), [[0, 1]], 0, 1)
-    asel(R("BTM"), R("ONE", 0, 128), [[-16, 8], [0, 16]], OP.is_ge, 0, 1)
-    asel(R("B128"), R("BTM"), [[16, 8], [0, 16]], OP.is_ge, 15, -1)
-    iota(R("kI"), [[1, 8], [0, 16]], 0, 0)
-    iota(R("eaA"), [[16, 128]], 0, 0)
-    asel(R("BTM"), R("B128"), [[-1, 128]], OP.is_ge, 0, 1)
+    iota(R("i1", 8, 16), [[16, 8]], 0, 0)
+    asel(R("UT"), R("ONE"), [[-16, 8], [0, 16]], OP.is_ge, 0, 1)
+    asel(R("B128"), R("UT"), [[16, 8], [0, 16]], OP.is_ge, 15, -1)
+    iota(R("t1"), [[16, 128]], 0, 0)
+    iota(R("t2"), [[16, 16], [256, 8]], 0, 0)
     asel(R("ID"), R("B128"), [[-1, 128]], OP.is_equal, 0, 1)
+    iota(R("t3"), [[0, 16], [1, 8]], 0, 0)
+    asel(R("UT"), R("B128"), [[-1, 128]], OP.is_ge, 0, 1)
     iota(R("OR"), [[1, 256]], 0, 0)
-    iota(R("clOp"), [[0, 16], [1, 16]], 0, 0)
-    iota(R("IW"), [[1, LW]], 0, 0, [R("ID"), R("clOp"), R("OR"), R("eaA"), R("kI")])
-    fill(R("SEL2"), 0.0)
-    for i in range(16):
-        ts(R("SEL2", 129 * i, 128 * i + 128, 16), R("B128", i, 128, 16), 2.0, OP.mult)
+    iota(R("JC"), [[128, 16], [1, 16]], 0, 0)
+    iota(R("DR"), [[0, 16], [1, 16]], 0, 0)
+    iota(R("i1", 32, 48), [[1, 16]], 0, 0)
+    for a in range(0, IWW, 576):
+        iota(R("IW", a, a + 576), [[1, 576]], a, 0)
     ts(R("i1", 1, 2), R("i1", 0, 1), 15, OP.bitwise_and)
     ts(R("i1", 2, 3), R("i1", 0, 1), 1, OP.bitwise_and)
     ts(R("i1", 3, 4), R("i1", 1, 2), 1, OP.arith_shift_right)
     cp(C(0), R("i1", 1, 2))
-    cp(C(1), R("i1", 2, 3))
-    ts(C(2), C(1), -1.0, OP.mult, 1.0, OP.add)
-    ts(C(3), R("i1", 3, 4), 256.0, OP.mult)
-    ts(C(4), C(0), 8.0, OP.is_lt, 0.5 - 1024.0, OP.mult)
-    ts(C(5), C(4), 1024.0, OP.add)
-    ts(C(9), C(1), 64.0, OP.add)
-    ts(R("SELPK"), R("SEL2"), C(5), OP.mult)
-    cp(Pk, R("kI"))
-    ts(R("jW"), R("eaA"), C(0), OP.add)
-    ts(R("t5"), R("jW"), 4096.0, OP.add)
-    cp(Pc, R("csI"))
-    cp(R("c16"), Pc)
-    ts(R("LV0", 0, 256), R("OR"), C(2), OP.mult, C(9), OP.add)
-    cp(R("t1"), R("hdI"))
-    tt(R("t3"), Pc, R("t5"), OP.subtract)
-    tt(R("t3"), R("t3"), R("t1"), OP.mult)
-    tt(R("t3"), R("t3"), R("t5"), OP.add)
-    cp(R("ei16"), R("t3"))
-    cp(R("LV0", 256, 512), R("LV0", 0, 256))
-    cp(R("LV0", 512, 1024), R("LV0", 0, 512))
-    cp(R("LV0", 1024, 2048), R("LV0", 0, 1024))
-    fill(R("LK", 0, LW), 0.0)
+    ts(C(1), R("i1", 2, 3), 2.0, OP.mult, -1.0, OP.add)
+    ts(C(2), C(1), 8192.0, OP.mult)
+    ts(C(3), R("i1", 3, 4), 16.0, OP.mult)
+    ts(C(4), C(0), 8.0, OP.is_lt, 1.0 / 2048 - 1.0, OP.mult)
+    ts(C(5), C(4), 1.0, OP.add)
+    ts(C(6), C(1), 1.0 / 8192, OP.mult)
+    ts(C(7), C(1), -0.25, OP.mult)
+    ts(C(8), C(0), 1.0, OP.add, 16.0, OP.mult)
+    ts(R("i1", 16, 24), R("i1", 8, 16), C(0), OP.add)
+    ts(R("i1", 8, 16), R("i1", 16, 24), 3, OP.arith_shift_right)
+    cp(R("pm16", 16, 24), R("i1", 8, 16))
+    ts(R("i1", 24, 32), R("i1", 16, 24), 7, OP.bitwise_and)
+    ts(R("i1", 24, 32), R("i1", 24, 32), 16.0, OP.mult)
+    tt(R("i1", 24, 32), R("i1", 24, 32), R("i1", 8, 16), OP.add)
+    cp(R("pm16", 0, 8), R("i1", 24, 32))
+    ts(R("jW"), R("t1"), C(0), OP.add)
+    ts(R("ei16"), R("t2"), C(0), OP.add)
+    cp(R("cI"), IX(R("csI"), R("pm16", 0, 8)))
+    cp(R("c16"), R("cI"))
+    fill(R("SELC"), 0.0)
+    for i in range(16):
+        ts(R("SELC", 129 * i, 128 * i + 128, 16), R("B128", i, 128, 16), 1.0 / 16, OP.mult)
+    ts(R("SELPK"), R("SELC"), C(5), OP.mult, 16.0, OP.mult)
+    ts(R("B8", 0, 8), R("B128", 0, 128, 16), -1.0, OP.mult)
+    ts(R("B8", 8, 16), R("B128", 0, 128, 16), 2.0, OP.mult)
+    fill(R("ZB"), 0.0)
+    ts(Pk, R("t3"), 8192.0 * 7, OP.add)
+    ts(R("m01"), R("t3"), 0.0, OP.is_gt)
+    ts(R("negk"), R("t3"), -8.5, OP.add)
+    fill(C(16), -2048.0); fill(C(17), -8.0); fill(C(18), -150.0); fill(C(19), 1.0 / 16)
+    fill(R("SELT"), 0.0)
+    ts(R("GM", 0, 16), R("OR", 0, 16), C(0), OP.is_equal, 32.0, OP.mult)
+    for gg in range(8):
+        cp(R("SELT", 144 * gg, 144 * gg + 16), R("GM", 0, 16))
+    ts(R("IDb"), R("ID"), -2097152.0, OP.mult)
+    fill(R("HALF"), 0.5); fill(R("HALFn"), -0.5)
 
-    Ecur = [E0]
-
-    def P_chunk(buf, lo, h):
-        together(lambda: [mm(R("PSP", 64 * h, 64 * h + 64), R("SELPK", 128 * i, 128 * i + 128), R(buf, lo + 1024 * h + i, lo + 1024 * h + 1024, 16),
-                             i == 0, i == 15) for i in range(16)])
-
-    def hash_front():
-        cp(R("Pi"), R("PSP", 0, 128))
-        ts(R("A"), R("Pi"), 2047, OP.bitwise_and)
-        ts(R("Bv"), R("Pi"), 11, OP.arith_shift_right)
-        tt(R("sm"), R("A"), R("Bv"), OP.add)
-
-    def hash_back(y):
-        tt(R("pr"), R("A"), R("Bv"), OP.mult)
-        ts(R("h", 0, 16), R("pr", 0, 16), 3, OP.arith_shift_right, 4095, OP.bitwise_and)
-        ts(R("h", 16, 128), R("pr", 16, 128), 3, OP.arith_shift_right, 511, OP.bitwise_and)
-        for k in range(1, 8):
-            tt(R("h", 16 * k, 16 * k + 16), R("h", 16 * k, 16 * k + 16), R("h", 16 * k - 16, 16 * k), OP.add)
-        tt(R(y), R("h"), Pk, OP.add)
-        ts(R(y), R(y), 4095, OP.bitwise_and)
-
-    def lanes_win():
-        tt(R("winR", 0, 256, 1, 8), R("PSA", 0, 256, 1, 8), R("thrR", 0, 256, 1, 8), OP.is_le)
-        conv1("PSD", [("winR", 8, R("PK8", 0, 128, 1, 8))])
-
-    def gather_front(t, between):
-        gt = "got%d" % (t & 1)
+    def sums_AB(lo):
         for h in range(2):
-            lo = 1024 * h
-            if h == 1 and t > 0: lanes_win()
-            act(R(gt, lo, lo + 1024), IX(R("V", VB, DB), R("c16", 64 * h, 64 * h + 64)))
-            tt(R("mx", lo, lo + 1024), IX(R("V", VB, DB), R("c16", 64 * h, 64 * h + 64)), R("V", Ecur[0] + lo, Ecur[0] + lo + 1024), OP.max)
-            out_send(t, "b%d" % h, R(gt, lo, lo + 1024))
-            if h == 0: P_chunk(gt, 0, h)
-        for h in range(2):
-            if h == 1:
-                if t > 0: conv2("PSD", 0, "q1")
-                P_chunk(gt, 0, h)
-                between()
-            together(lambda: [mm(R("PSM", 64 * h, 64 * h + 64), R("SEL2", 128 * i, 128 * i + 128), R("mx", 1024 * h + i, 1024 * h + 1024, 16),
-                                 i == 0, i == 15) for i in range(16)])
+            to_list(R("PP", 64 * h, 64 * h + 64), "SELPK", "EB", lo + 1024 * h, 1024)
 
-    def list_table():
-        act(R("cR"), IX(R("IW", 0, 4096), R("c16")), scale=2048.0)
-        dma("y", T.K[0:128:2, :], T.cR[0:128:16, :], [("cR", 0, 2048)], [("K", 0, 256)])
-        dma("y", T.K[1:128:2, :], T.cR[0:128:16, :], [("cR", 0, 2048)], [("K", 256, 512)])
+    def new_cells_of(y, stamp):
+        ts(R("Bv"), R("PP", 0, 128), -0.4985, OP.add)
+        tt(Pa, R("PP", 0, 128), R("Bv"), OP.subtract)
+        tt(R("t1"), Pa, R("Bv"), OP.mult)
+        ts(R("hI"), R("t1"), 256.0, OP.mult, -0.4375, OP.add)
+        ts(R("h"), R("hI"), 511, OP.bitwise_and)
+        ts(R("h", 0, 128, 8), R("hI", 0, 128, 8), 4095, OP.bitwise_and)
+        scan(R("t2"), R("m01"), R("h"), OP.mult, OP.add)
+        tt(R("hI"), R("t2"), Pk, OP.add)
+        ts(R(y), R("hI"), 4095 + 8192 * stamp, OP.bitwise_and)
 
-    def tree(src, out, op):
-        tt(R("red", 0, 64), R(src, 0, 64), R(src, 64, 128), op)
-        tt(R("red", 64, 96), R("red", 0, 32), R("red", 32, 64), op)
-        tt(out, R("red", 64, 80), R("red", 80, 96), op)
+    PDW = R("PD", 0, 128)
 
-    def flags_front():
-        hash_front()
-        tt(R("d1"), R("PSM", 0, 128), R("sm"), OP.subtract)
-        tt(R("bd"), R("d1"), Pthr, OP.is_gt)
-        tree("bd", L("tr"), OP.add)
+    def dist_part(src, lo, a, b, sign, stop=False):
+        together(lambda: [mm(R("PD", j // 16, j // 16 + 8), R(src, lo + j, lo + j + 128), R("B8", sign, sign + 8), False, stop and j + 128 == b, PDW)
+                          for j in range(a, b, 128)])
 
-    for h in range(2): P_chunk("V", E0, h)
-    hash_front()
-    cp(PsE, R("sm"))
-    gather_front(0, lambda: None)
-    hash_back("yI1")
-    cp(R("NCE"), R("yI1"))
-    ts(Pthr, PsE, 150.0, OP.add)
-    ts(R("t2"), R("t1"), -1.0 / 32, OP.mult, 1.0 / 32, OP.add)
-    tree("t2", L("n32"), OP.add)
-    flags_front()
-    tt(R("code0"), L("tr"), L("n32"), OP.add)
-    out_send(0, "co", R("code0"))
-    hash_back("yI0")
-    out_send(0, "nc", R("yI0"))
-    cp(L("cur"), R("jW", 0, 16)); cp(R("cur16"), L("cur"))
-    scatter_act(IX(R("LK"), R("ei16")), R("LV0"))
-    list_table()
-    lna = math.log(1.75)
-    ts(L("lm"), R("jW", 0, 16), -128.0, OP.add)
-    act(L("wW"), L("lm"), AF.Exp, -lna)
-    ts(R("thrR"), R("OR"), -128.0, OP.add)
-    act(R("thrR"), R("thrR"), AF.Exp, -lna)
-    ts(R("thrR"), R("thrR"), 2.5, OP.mult)
-    ts(Pkb, Pk, 4096.0, OP.mult)
-    ts(R("t1"), R("t1"), 65536.0, OP.mult)
-    tt(R("HB"), R("t1"), Pkb, OP.add)
-    ts(R("kp1"), Pk, 1.0, OP.add)
-    ts(C(6), C(0), 0.0, OP.is_equal)
-    ts(C(7), C(0), 1.0, OP.is_equal)
-    ts(C(8), C(0), 1.0, OP.add, 0.5, OP.mult)
+    def columns(t):
+        mm(PDW, R("ZB"), R("ZB"), True, False)
+        dist_part("EB", ES[t], 0, 2048, 0)
+        for a, b in zip(CH, CH[1:]):
+            lst = IX(R("V", 0, 4096), R("c16", a // 16, b // 16))
+            act(R("EB", GOT[t] + a, GOT[t] + b), lst)
+            tt(R("mx", a, b), lst, R("EB", ES[t] + a, ES[t] + b), OP.max)
+            dist_part("EB", GOT[t], a, b, 0)
+            dist_part("mx", 0, a, b, 8, b == 2048)
+            if b % 1024 == 0:
+                for u in ((0, 1) if t == 0 else (t + 1,) if t + 1 < STEPS else ()):
+                    out_send(u, "b%d" % (a // 1024), R("EB", GOT[t] + b - 1024, GOT[t] + b))
+        act(R("bd"), PDW, AF.Relu, 1.0, C(18))
+
+        def run():
+            if t > 0: mm(BS, R("IDb"), L("done"), True, False)
+            for gg in range(8):
+                mm(BS, R("SELT", 128 * gg, 128 * gg + 128), R("bd", gg, 128, 8), t == 0 and gg == 0, gg == 7)
+        together(run)
+
+    def code_out(t):
+        c = R("code%d" % (t & 1))
+        tt(c, BS, L("w"), OP.max)
+        out_send(t, "co", c)
+        ts(L("ncode"), c, -1.0, OP.mult)
+        ts(L("thrab"), c, -1.0, OP.mult, 24.0, OP.add)
+
+    def cells_out(t):
+        y = "yI%d" % (t & 1)
+        sums_AB(GOT[t])
+        new_cells_of(y, t + 2)
+        for u in ((0, 1) if t == 0 else (t + 1,) if t + 1 < STEPS else ()):
+            out_send(u, "nc", R(y))
+        if t > 0:
+            tt(R("t1"), DX, R(y), OP.mult)
+            tt(R("nZ"), R("nZ"), R("t1"), OP.min)
+
+    act(R("EB", E01, E01 + 2048), IX(R("EB", SNAP, SNAP + 2048), R("ei16")))
+    ts(R("t3"), IX(R("hdI"), R("pm16", 0, 8)), -1.0, OP.mult, 1.0, OP.add)
+    scan(R("z"), R("m01"), R("t3"), OP.mult, OP.add)
+    cp(L("w"), R("z", 7, 128, 8))
+    columns(0)
+    code_out(0)
+    cells_out(0)
+    sums_AB(E01)
+    new_cells_of("Cz", 1)
+    ts(R("nZ"), R("Cz"), -1.0, OP.mult)
+    cp(R("Cz"), R("cI"))
+    spread(384, "ID", L("w"), (R("ID"), R("HALF")))
+    tt(R("t1"), WX, R("z"), OP.subtract)
+    ts(R("t1"), R("t1"), 1.0, OP.add)
+    tt(R("mq"), R("t1"), R("t3"), OP.mult)
+    cp(R("ck16"), R("csI"))
+    act(R("cR"), IX(R("IW", 0, 4096), R("ck16")))
+    dma("y", T.K[0:128:2, :], T.cR[0:128:16, :], [("cR", 0, 2048)], [("K", 0, 256)])
+    dma("y", T.K[1:128:2, :], T.cR[0:128:16, :], [("cR", 0, 2048)], [("K", 256, 512)])
+    ts(R("JC"), R("JC"), C(3), OP.add, C(2), OP.mult)
+    for a in range(0, IWW, 1152):
+        fill(R("LK", a, a + 1152), 64.0)
+    ts(R("LK", 4096, IWW, 2), R("OR"), 8.0, OP.mult, 71.0, OP.add)
+    ts(R("t1"), R("jW"), float(IWW), OP.add)
+    tt(R("t2"), R("csI"), R("t1"), OP.subtract)
+    tt(R("t2"), R("t2"), R("hdI"), OP.mult)
+    tt(R("t2"), R("t2"), R("t1"), OP.add)
+    cp(R("lk16"), R("t2"))
+    fill(C(20), 65.0)
+    act(R("LV"), R("OR"), scale=8.0, bias=C(20))
+    for k in range(8):
+        scatter_act(IX(R("LK"), R("lk16", 16 * k, 16 * k + 16)), R("LV"))
+    fill(R("clOp"), 1 / 1.75); fill(R("G"), 0.0)
+    comp("v", [R("clOp"), R("G")], [R("wR")], lambda r, w: g.vector.tensor_tensor_scan(ap(w[0]), ap(r[0]), ap(r[1]), 1.75 ** 120, OP.mult, OP.add))
+    tt(R("t1"), R("wR", 0, 128), R("ID"), OP.mult)
+    reduce_add(C(9), R("t1"))
+    fill(L("thrT"), 2.5)
+    upper = R("lane", _L["thrT"][1] + 8, _L["thrT"][1] + 16)
+    ts(upper, upper, 1.75 ** -64, OP.mult, 1.75 ** -64, OP.mult)
+    ts(L("thrT"), L("thrT"), C(9), OP.mult)
+    ts(R("MK"), R("DR"), C(0), OP.is_equal)
+    tt(R("t1", 0, 16), R("wR", 0, 16), R("MK", 0, 16), OP.mult)
+    reduce_add(C(13), R("t1", 0, 16))
+    ts(C(13), C(13), 1.75 ** -119, OP.mult)
+    ts(L("wW"), R("wR", 0, 256, 16), C(13), OP.mult)
     for t in range(STEPS):
-        ts(C(10 + t), C(1), float(t + 2), OP.mult, 64.0, OP.add)
-    fill(C(16), -2048.0); fill(C(17), -64.0)
-    ts(R("PKP"), R("B128"), C(6), OP.mult)
-    ts(R("PKH"), R("B128"), C(6), OP.mult)
-    ts(R("PKO"), R("B128"), C(7), OP.mult)
-    cp(R("B8"), R("B128", 0, 128, 16))
-    cp(R("B8H"), R("B128", 0, 128, 16))
-    ts(R("MK"), R("clOp"), C(0), OP.is_equal)
-    mm(R("PSD", 0, 128, 1, 8), R("PKP", 0, 128, 16), R("PKP"), True, True)
-    cp(R("PK8", 0, 128, 1, 8), R("PSD", 0, 128, 1, 8))
-    ts(R("JC"), R("OR"), C(3), OP.add)
-    ts(R("DUM", 0, 24), R("jW", 0, 24), 4096.0, OP.add, 2048.0, OP.mult)
-    ts(R("DUM", 24, 48), R("jW", 0, 24), 4096.0, OP.add, 2048.0, OP.mult)
-    ts(L("dm256"), R("jW", 0, 16), 256.0, OP.add)
-    ts(L("dm4096"), R("jW", 0, 16), 4096.0, OP.add)
-    fill(L("z"), 0.0); fill(L("dec"), 0.0); fill(R("ZB"), 0.0)
-    fill(R("V", DB, E1), 0.0)
-    ts(R("BTM"), R("BTM"), -1.0, OP.mult)
-    cp(R("dec16"), L("dec"))
+        fill(C(21 + t), 66.0 + t); fill(C(26 + t), -1.0 - 2 * t)
+        ts(R("wk5", 16 * t, 16 * t + 16), R("wkI"), t, OP.arith_shift_right, 1, OP.bitwise_and)
+    cp(R("awk"), R("wk5"))
+    cp(L("cur"), oL)
+    ts(DM[0], oL, 256.0, OP.add)
+    ts(DM[1], oL, float(IWW), OP.add)
+    ts(DM[2], oL, float(IWW - 2048), OP.add)
+    cp(R("pm16", 24, 40), R("i1", 32, 48))
+    cp(R("B8", 16, 24), R("B128", 0, 128, 16))
+    ts(L("dum"), oL, 2.0, OP.mult, 4096.0, OP.add)
+    ts(L("c511"), oL, -1.0, OP.mult, 511.0, OP.add)
+    cp(L("c511h"), L("c511"))
+    fill(L("z0"), 0.0); fill(L("dec"), 0.0)
+    cp(R("posH"), R("jW"))
+    ts(R("UT"), R("UT"), -1.0, OP.mult)
+    ts(R("IDn"), R("ID"), -1.0, OP.mult); ts(R("IDk"), R("ID"), 2048.0, OP.mult)
+    asel(R("qw", 0, 128), R("ONE"), [[0, 16], [-16, 8]], OP.is_ge, 0, 1)
+    asel(R("GM"), R("qw", 0, 128), [[0, 16], [16, 8]], OP.is_ge, 15, -1)
+    for c in range(1, 16):
+        if c != 8: fill(R("EQ", 256 * c + 128 * (c // 8), 272 * c), 0.0)
+    fill(R("OPW"), 0.0); fill(C(14), 1.0)
+    fill(R("V", 4096, VW), 0.0)
+    ts(C(10), C(1), -0.5, OP.mult, 0.5, OP.add)
+    ts(C(11), C(1), 0.5, OP.mult, 0.5, OP.add)
+    ts(R("DUM", 0, 24), R("jW", 0, 24), 4096.0, OP.add, C(10), OP.mult)
+    ts(R("DUM", 24, 48), R("jW", 0, 24), 4096.0 + 2047.0 * 8192, OP.add, C(11), OP.mult)
+    ts(C(12), C(10), -16777216.0, OP.mult)
+    ts(R("DUM", 24, 48), R("DUM", 24, 48), C(12), OP.add)
 
-    def renew_state(y):
-        tt(R("t1"), R("sm"), PsE, OP.subtract)
-        tt(R("t1"), R("t1"), Pdp, OP.mult)
-        tt(PsE, PsE, R("t1"), OP.add)
-        tt(R("t2"), R(y), R("NCE"), OP.subtract)
-        tt(Pt, R("t2"), Pdp, OP.mult)
-        tt(R("NCE"), R("NCE"), Pt, OP.add)
+    def missing(out, half, lim):
+        spread(384, "ID", L("w"), (R("ID"), R(half)))
+        tt(Pd, R("mq"), WX, OP.is_equal)
+        tt(R("t1"), Pd, R("cI"), OP.mult)
+        scan(R("t3"), R("m01"), R("t1"), OP.mult, OP.add)
+        ts(L("f0"), L("w"), lim, OP.is_le)
+        tt(L("fd"), L("f0"), L("dum"), OP.mult)
+        tt(out, R("t3", 7, 128, 8), L("fd"), OP.add)
 
-    def lanes_pre(t, between):
-        tt(R("key"), R("HB"), Pc, OP.add)
-        tree("key", L("keyv"), OP.min)
-        cp(R("keI"), L("keyv"))
-        ts(R("ceI"), R("keI"), 4095, OP.bitwise_and)
-        ts(L("full"), L("keyv"), 65536.0, OP.is_ge, 4096.0, OP.mult)
-        tt(L("x1"), R("ceI"), L("full"), OP.max)
-        cp(R("cl16"), L("x1"))
-        act(R("clOp"), IX(R("IW"), R("cl16")))
-        act(R("clR"), IX(R("clOp"), R("cur16")), bias=C(16))
-        act(R("decR"), IX(R("IW", 0, 8), R("dec16")), scale=-1.0)
-        act(R("OPW", 0, 256), R("ZB"))
-        act(R("LV"), IX(R("IW", 0, 256), R("cur16")), scale=C(2), bias=C(10 + t))
-        conv1("PSA", [("clR", 128, R("PKH"))])
-        ts(R("fkI"), R("keI"), 12, OP.arith_shift_right)
-        ts(L("fk1"), R("fkI"), 1.0, OP.add)
-        ts(R("acI"), R("wkI"), t, OP.arith_shift_right, 1, OP.bitwise_and)
-        cp(L("act"), R("acI"))
+    def lanes_pre(t):
+        if t == 0:
+            act(R("RW", 0, 256), IX(R("IW"), R("cl16")), bias=C(16))
+            act(R("RW", 256, 512), IX(R("LK", 0, IWW), R("cl16")), scale=0.125, bias=C(17))
+        else:
+            act(R("clOp"), IX(R("IW"), R("cl16")), bias=C(16))
+            act(R("G"), IX(R("LK", 0, IWW), R("cl16")), scale=0.125, bias=C(17))
+            act(R("RW", 0, 256), IX(R("clOp"), R("cur16")))
+            act(R("RW", 256, 512), IX(R("G"), R("cur16")))
+        to_list(R("PL", 0, 32), "SELC", "RW", 0, 512)
+        ts(R("p16"), R("PL", 16, 32), -0.45, OP.add)
+        ts(R("pI"), R("PL", 16, 32), -0.45, OP.add)
+        cp(L("clS"), R("PL", 0, 16))
+        tt(L("s8"), R("PL", 16, 32), R("pI"), OP.subtract)
+        if t == 0:
+            ts(L("val"), L("s8"), 1.0 / 16, OP.is_gt)
+        else:
+            act(R("decL"), IX(R("DR"), R("p16")))
+            to_list(R("PL", 32, 48), "SELC", "decL", 0, 256)
+            tt(L("val"), L("s8"), R("PL", 32, 48), OP.is_gt)
+        aw = R("awk", 16 * t, 16 * t + 16)
+        tt(L("mv"), aw, L("val"), OP.mult)
+        tt(L("cand"), aw, L("mv"), OP.subtract)
+        tt(L("candw"), L("cand"), L("wW"), OP.mult)
+        tt(L("q"), L("cur"), DM[0], OP.subtract)
+        tt(R("o2", 48, 64), L("cand"), L("q"), OP.mult)
+        if t < STEPS - 1:
+            tt(L("qq"), L("clS"), DM[2], OP.subtract)
+            tt(R("o2", 64, 80), L("cand"), L("qq"), OP.mult)
+        tt(L("q2"), R("pI"), L("cur"), OP.subtract)
+        tt(L("q3"), L("q2"), L("mv"), OP.mult)
+        tt(L("cur1"), L("cur"), L("q3"), OP.add)
+        tt(L("e1"), L("cur1"), oL, OP.subtract)
+        for c in range(16):
+            b, lo = _L["clS"]
+            ts(R("EQ", 272 * c, 256 * c + 256), R("RW", 16 * c, 256), R(b, lo + c, lo + c + 1), OP.is_equal)
         act(R("COMP", 0, 48), R("DUM"))
-        between()
-        conv2("PSA", 0, "qh", "B8H")
-        tt(R("t4"), Pkb, R("HB"), OP.subtract)
-        cp(L("clS"), R("PSA", 0, 16))
-        ts(L("cl"), L("clS"), 2048.0, OP.add)
-        cp(R("lc16"), L("cl"))
-        act(R("G1"), IX(R("LK", 0, LW), R("lc16")), bias=C(17))
+        iota(R("C64"), [[0, 256]], 64 * (t + 1), 0)
+        if t < STEPS - 1:
+            if t == 0: act(R("LV"), R("OR"), scale=8.0, bias=C(21))
+            else: act(R("LV"), IX(R("IW", 0, 256), R("cur16")), scale=8.0, bias=C(21 + t))
+            missing(L("clB"), "HALFn", 1.0)
+            tt(L("dB"), L("clB"), L("cl"), OP.subtract)
 
     def judge(t):
-        tt(L("X"), R("code%d" % (t & 1)), R("lc%d" % t), OP.add)
-        ts(R("rdy"), L("X"), 0.0, OP.is_equal)
-        together(lambda: [mm(R("PSR", 0, 16), R("B128"), R("rdy"), True, True), mm(R("PSR", 16, 32), R("BTM"), R("rdy"), True, True)])
-        conv1("PSA", [("G1", 128, R("PKP"))])
-        ts(R("cab", 16, 32), L("X"), 1.0, OP.is_ge)
-        ts(L("nr"), L("X"), 0.0, OP.is_gt)
-        tt(L("e"), L("dm256"), L("nr"), OP.mult)
-        comp("v", [R("PSR", 0, 16), L("z")], [L("inc")],
-             lambda r, w: g.vector.tensor_tensor_scan(ap(w[0]), ap(r[0]), ap(r[1]), 0.0, OP.add, OP.add))
-        tt(L("rank"), R("PSR", 16, 32), L("inc"), OP.add)
-        ts(L("cm"), L("rank"), 48.0, OP.is_lt)
-        tt(R("cab", 0, 16), L("cm"), R("rdy"), OP.mult)
-        tt(L("done"), R("cab", 0, 16), R("cab", 16, 32), OP.add)
-        cp(R("dn16"), L("done"))
-        act(R("dnR"), IX(R("IW", 0, 8), R("dn16")))
-        act(R("gnR"), IX(R("dnR"), R("cur16")))
-        tt(L("x5"), L("rank"), L("e"), OP.max)
-        cp(R("off16"), L("x5"))
-        conv2("PSA", 16, "q0")
-        together(lambda: [mm(R("PSC", 128 * j + 16 * k, 128 * j + 16 * k + 16), R("ID"), R("cab", 16 * j, 16 * j + 16), True, True)
-                          for j in range(2) for k in range(8)])
-        conv1("PSR", [("gnR", 128, R("PKP"))])
-        comp("v", [("n", "K", 0, 512, 1, 128), R("JC")], [IX(R("COMP"), R("off16"))],
+        tw = R("lc%d" % t)
+        tt(L("rdy"), L("ncode"), tw, OP.is_equal)
+        scan(L("incl"), L("rdy"), L("z0"), OP.add, OP.add)
+        tt(L("rc"), L("rdy"), L("c511"), OP.mult)
+        tt(L("ab"), tw, L("thrab"), OP.is_ge)
+        together(lambda: [mm(RA, R("ID"), L("c511h"), True, False), mm(RA, R("UT"), L("rdy"), False, False),
+                          mm(RA, R("IDn"), L("rc"), False, False), mm(RA, R("B128"), L("incl"), False, True)])
+        cp(R("off16"), RA)
+        ts(L("cm"), RA, 48.0, OP.is_lt)
+        comp("v", [R("K", 0, 512), R("JC")], [IX(R("COMP"), R("off16"))],
              lambda r, w: g.vector.tensor_tensor(out=ap(w[0]), in0=T.K[:], in1=T.JC[:], op=OP.add))
-        cp(R("p16"), R("PSA", 16, 32))
-        cp(L("p"), R("p16"))
-        ts(R("Lt", 0, 24), R("COMP", 0, 24), C(2), OP.mult)
-        ts(R("Lt", 24, 48), R("COMP", 24, 48), C(1), OP.mult)
-        tt(R("Ls", 0, 24), R("Lt", 0, 24), R("Lt", 24, 48), OP.add)
-        ts(R("Ls", 24, 48), R("Ls", 0, 24), 2047, OP.bitwise_and)
-        cp(R("L16", 0, 24), R("Ls", 24, 48))
-        act(R("decL"), IX(R("decR"), R("p16")))
+        tt(R("Ls", 0, 24), R("COMP", 0, 24), R("COMP", 24, 48), OP.max)
+        ts(R("L16", 0, 24), R("Ls", 0, 24), C(6), OP.mult, C(7), OP.add)
         act(R("Dl"), IX(R("lb%d" % t), R("L16", 0, 24)))
-        conv1("PSA", [("G1", 128, R("PKO")), ("decL", 128, R("PKP"))])
-        ts(R("Ls", 48, 72), R("Ls", 0, 24), 11, OP.arith_shift_right)
-        cp(R("L16", 24, 48), R("Ls", 48, 72))
-        conv2("PSR", 32, "q1")
-        for c in range(16):
-            ts(R("EQ", 272 * c, 256 * c + 256), R("clR", 16 * c, 256), L("clS", c, c + 1), OP.is_equal)
-        conv2("PSA", 32, "q0")
-        ts(L("nf"), L("cl"), 4096.0, OP.is_lt)
-        tt(L("an"), L("act"), L("nf"), OP.mult)
-        tt(R("t3"), R("NCE"), Pc, OP.subtract)
-        ts(L("val"), R("PSA", 32, 48), 0.0, OP.is_gt)
-        tt(L("mv"), L("an"), L("val"), OP.mult)
-        tt(L("cand"), L("an"), L("mv"), OP.subtract)
+        ts(R("Ls", 24, 48), R("Ls", 0, 24), 8191, OP.bitwise_and)
+        cp(R("L16", 24, 48), R("Ls", 24, 48))
+        tt(L("sel"), L("cm"), L("ab"), OP.subtract)
+        tt(L("done"), L("cm"), L("ab"), OP.add)
+        spread(0, "ID", L("sel"))
+        spread(128, "IDn", L("done"))
+        tt(Pd, SX, R("ln%d" % t), OP.mult)
+        tt(R("t2"), SX, R("nZ"), OP.mult)
+        tt(Pe, Pd, R("t2"), OP.max)
+        tt(R("Cz"), Pe, R("Cz"), OP.max)
+        ts(R("cI"), R("Cz"), 4095, OP.bitwise_and)
+        if t < STEPS - 1: cp(R("c16"), R("cI"))
+        cp(IX(R("V"), R("L16", 24, 48)), R("Dl"))
+        tt(R("t3"), DX, R("negk"), OP.mult)
+        tt(R("mq"), R("mq"), R("t3"), OP.max)
 
-    def lanes_moves():
-        tt(L("x1"), L("p"), L("cur"), OP.subtract)
-        tt(L("x1"), L("x1"), L("mv"), OP.mult)
-        tt(L("cur1"), L("cur"), L("x1"), OP.add)
-        tt(L("x4"), R("jW", 0, 16), L("cur1"), OP.subtract)
-        tt(L("x4"), L("x4"), R("PSR", 32, 48), OP.mult)
-
-    def new_cells(t):
-        tt(R("t1"), R("ln%d" % t), Pc, OP.subtract)
-        tt(R("t1"), R("t1"), R("PSC", 0, 128), OP.mult)
-        tt(R("t2"), R("t3"), R("PSC", 128, 256), OP.mult)
-        tt(Pc, Pc, R("t1"), OP.add)
-        tt(Pc, Pc, R("t2"), OP.add)
-        cp(R("c16"), Pc)
-
-    def commit_columns():
-        cp(IX(R("V", VB, E1), R("L16", 24, 48)), R("Dl"))
-
-    def masks():
-        cp(R("cmS"), R("PSC", 0, 128))
-        tt(Pdp, R("PSC", 128, 256), R("cmS"), OP.add)
-
-    def thresholds():
-        ts(R("t1"), Pdp, BIG, OP.mult, 150.0, OP.add)
-        tt(Pthr, PsE, R("t1"), OP.add)
-
-    def lanes_claim():
-        ts(L("x6"), R("PSR", 32, 48), -1.0, OP.mult, 1.0, OP.add)
-        tt(L("ac"), L("x6"), L("cand"), OP.mult)
-        tt(L("aw"), L("ac"), L("wW"), OP.mult)
-        for k in range(8):
-            ts(R("LH", 16 * k, 16 * k + 16), L("aw"), R("GC", k, k + 1), OP.mult)
-        together(lambda: [mm(R("PSA", 16 * c, 256, 1, 8), R("LH", c, 128, 16), R("EQ", 272 * c, 256 * c + 256), c == 0, c == 15) for c in range(16)])
-
-    def lanes_out(t):
-        tt(L("win"), L("ac"), R("PSD", 0, 16), OP.mult)
-        ts(L("lose"), L("win"), -1.0, OP.mult, 1.0, OP.add)
-        tt(L("x1"), L("lose"), L("dm256"), OP.mult)
-        tt(L("x1"), L("x1"), L("cur"), OP.max)
-        cp(R("oo16"), L("x1"))
-        cp(IX(R("OPW"), R("oo16")), R("ONE"))
-        conv1("PSD", [("OPW", 128, R("PKP"))])
-        lanes_moves()
-        conv2("PSD", 16, "q1")
-        if t < STEPS - 1:
-            tt(L("x5"), L("lose"), L("dm4096"), OP.mult)
-            tt(L("x5"), L("x5"), L("cl"), OP.max)
-            cp(R("ol16"), L("x5"))
-            ts(L("x6"), L("n32"), -1.0, OP.mult, 0.25, OP.add)
-            tt(L("x6"), L("x6"), L("done"), OP.mult)
-            tt(L("n32a"), L("n32"), L("x6"), OP.add)
-            ts(L("x6"), L("done"), float(t + 2), OP.mult)
-            tt(L("dec"), L("dec"), L("x6"), OP.max)
+    def lanes_post(t):
+        if t < STEPS - 1 or t > 0:
+            ts(L("dst"), L("done"), float(t + 2), OP.mult)
+            tt(L("dec"), L("dec"), L("dst"), OP.max)
             cp(R("dec16"), L("dec"))
-            tt(L("cur"), L("cur1"), L("x4"), OP.add)
-            cp(R("cur16"), L("cur"))
+            act(R("DR"), IX(R("IW", 0, 8), R("dec16")), scale=0.125, bias=C(19))
+        if t == 0:
+            ts(L("ng"), L("done"), -1.0, OP.mult, 1.0, OP.add)
         else:
-            tt(L("cur"), L("cur1"), L("x4"), OP.add)
+            act(R("gnR"), IX(R("DR"), R("cur16")))
+            to_list(R("PL", 48, 64), "SELC", "gnR", 0, 256)
+            ts(L("ng"), R("PL", 48, 64), (t + 2) / 8.0, OP.is_lt)
+        n = 32 if t < STEPS - 1 else 16
+        if t == 0:
+            na = L("x1")
+            ts(na, L("ab"), -1.0, OP.mult, 1.0, OP.add)
+        else:
+            na = R("PL", 64, 80)
+            cp(R("ab16"), L("ab"))
+            act(R("abR"), IX(R("IW", 0, 8), R("ab16")), scale=-1.0, bias=C(14))
+            act(R("naL"), IX(R("abR"), R("cur16")))
+            to_list(na, "SELC", "naL", 0, 256)
+        tt(L("aw"), na, L("candw"), OP.mult)
+        tt(R("LH"), IX(L("aw"), R("pm16", 16, 24)), R("GM"), OP.mult)
+        for a in range(0, n, 16):
+            tt(R("o2", 80 + a, 96 + a), na, R("o2", 48 + a, 64 + a), OP.mult)
+        together(lambda: [mm(R("PW", 8 * h, 8 * h + 8), R("EQ", 256 * c + 128 * h, 256 * c + 128 * h + 128), R("LH", 8 * c, 8 * c + 8), c == 0, c == 8 * h + 7)
+                          for h in range(2) for c in range(8 * h + 8)])
+        tt(L("winT"), R("PW", 0, 16), L("thrT"), OP.is_le)
+        tt(R("qw"), IX(L("winT"), R("pm16", 24, 40)), R("MK"), OP.mult)
+        together(lambda: [mm(R("PW", 32 + a + 8 * h, 40 + a + 8 * h), R("qw", 128 * h, 128 * h + 128), R("B8", 16, 24), True, True)
+                          for a in range(0, n, 16) for h in range(2)])
+        tt(R("z", 0, n), R("PW", 32, 32 + n), R("o2", 80, 80 + n), OP.mult)
+        tt(R("z", 32, 32 + n), R("z", 0, n), R("o2", 0, n), OP.add)
+        cp(R("o16", 0, n), R("z", 32, 32 + n))
+        scatter_act(IX(R("OPW"), R("o16", 0, 16)), R("C64"))
+        act(R("OPB"), R("OPW", 0, 256), AF.Relu, 1.0 / 32, C(26 + t))
+        to_list(R("PW", 272, 288), "SELC", "OPB", 0, 256)
+        ts(L("d8"), L("done"), 8.0, OP.mult)
+        tt(L("w1"), L("w"), L("d8"), OP.max)
+        tt(L("w"), L("w1"), R("PW", 272, 288), OP.subtract)
+        tt(L("e2"), L("e1"), L("ng"), OP.mult)
+        tt(L("cur"), L("e2"), oL, OP.add)
+        if t < STEPS - 1:
+            cp(R("cur16"), L("cur"))
+            scatter_act(IX(R("LK", 0, IWW + 256), R("o16", 16, 32)), R("LV"))
+            tt(L("x1"), R("cI", 0, 128, 8), L("cl"), OP.subtract)
+            tt(L("x2"), L("x1"), L("done"), OP.mult)
+            tt(L("clA"), L("cl"), L("x2"), OP.add)
+            tt(L("x1"), R("PW", 272, 288), L("dB"), OP.mult)
+            tt(L("cl"), L("x1"), L("clA"), OP.add)
+            cp(R("cl16"), L("cl"))
 
-    def holders():
-        tt(R("rw"), L("fk1"), R("PSD", 16, 32), OP.mult)
-        together(lambda: [mm(R("PSD", 128 + 16 * k, 144 + 16 * k), R("ID"), R("rw"), True, True) for k in range(8)])
+    def snapshots(t):
+        lo = ES[t + 1]
+        spread(256, "IDk", L("done"), (R("ID"), R("posH")))
+        cp(R("ei16"), IXD)
+        return lambda: [act(R("EB", ES[t + 2] + a, ES[t + 2] + a + 512), IX(R("EB", lo, lo + 4096), R("ei16", a // 16, a // 16 + 32)))
+                        for a in range(0, 2048, 512)]
 
-    def holders2():
-        tt(Pt, R("t4"), Pdp, OP.mult)
-        tt(R("HB"), R("HB"), Pt, OP.add)
-        tt(R("t5"), R("PSD", 128, 256), R("kp1"), OP.is_equal)
-        ts(Pu, R("t5"), 65536.0, OP.mult)
-        tt(R("HB"), R("HB"), Pu, OP.add)
-
-    def snap_window():
-        if Ecur[0] == E0: return E0, E1, E1, "eaA", "ejA"
-        return VB, VE, E0, "eaB", "ejB"
-
-    def snap_index():
-        lo, hi, new, ea, ej = snap_window()
-        tt(R("t5"), R(ea), Pc, OP.add)
-        tt(Pt, R("t5"), Pdp, OP.mult)
-        tt(R("t5"), R(ej), Pt, OP.add)
-        cp(R("ei16"), R("t5"))
-
-    def snap_gather():
-        lo, hi, new, ea, ej = snap_window()
-        act(R("V", new, new + 2048), IX(R("V", lo, hi), R("ei16")))
-        Ecur[0] = new
-
-    def const_last():
-        cp(R("GC"), R("B128", 0, 128, 16))
-        for ea, ej, vb, eb in (("eaA", "ejA", VB - E0, 0), ("eaB", "ejB", 0, E1 - VB)):
-            ts(R(ej), R("jW"), float(eb), OP.add)
-            ts(R(ea), R("jW"), -1.0, OP.mult, float(vb - eb), OP.add)
-
-    lanes_pre(0, const_last)
+    missing(L("cl"), "HALF", 0.0)
+    cp(R("cl16"), L("cl"))
     for t in range(STEPS):
+        lanes_pre(t)
         judge(t)
-        lanes_claim()
-        new_cells(t)
-        commit_columns()
+        if t == 0: act(R("SELW"), R("SELC"), scale=C(8))
         if t == STEPS - 1: break
-        n = t + 1
-        gather_front(n, lambda: lanes_out(t))
-        list_table()
-        masks()
-        thresholds()
-        if t < STEPS - 2:
-            snap_index()
-            snap_gather()
-        if t == 0: act(R("SELW"), R("SEL2"), scale=C(8))
-        scatter_act(IX(R("LK", 0, 4352), R("ol16")), R("LV"))
-        flags_front()
-        ts(L("wo"), R("PSD", 16, 32), -1.0 / 32, OP.mult)
-        tt(L("n32"), L("n32a"), L("wo"), OP.add)
-        tt(R("code%d" % (n & 1)), L("tr"), L("n32"), OP.add)
-        out_send(n, "co", R("code%d" % (n & 1)))
-        holders()
-        hash_back("yI%d" % (n & 1))
-        out_send(n, "nc", R("yI%d" % (n & 1)))
-        holders2()
-        lanes_pre(n, lambda: renew_state("yI%d" % (n & 1)))
+        later = snapshots(t) if t < STEPS - 2 else None
+        lanes_post(t)
+        columns(t + 1)
+        code_out(t + 1)
+        cells_out(t + 1)
+        if later: later()
     t = STEPS - 1
-    masks()
-
-    def weigh(a, b2):
-        for b in range(a, b2):
-            mm(R("PSP", 0, 256), R("SELW", 128 * b, 128 * b + 128), R("V", VB + 256 * b, VB + 256 * b + 256), b == 0, b == 15)
-
-    weigh(0, 3)
-    lanes_win()
-    conv2("PSD", 0, "q1")
-    cp(R("sm"), Pc)
-    dma("y", T.yc[:], T.sm[:], [("sm", 0, 128)], [])
-    weigh(3, 10)
-    lanes_out(t)
-    last = res(L("cur"))
-    dma("s", T.yl[:], ap(last), flat(last), [])
-    holders()
-    weigh(10, 16)
-    holders2()
-    ts(R("d1"), R("HB"), 65536.0, OP.is_ge)
-    dma("y", T.yh[:], T.d1[:], [("d1", 0, 128)], [])
-    cp(R("yso"), R("PSP", 0, 256))
+    together(lambda: [mm(R("PP", 0, 256), R("SELW", 128 * b, 128 * b + 128), R("V", 256 * b, 256 * b + 256), b == 0, b == 15) for b in range(16)])
+    act(R("yso"), R("PP", 0, 256))
     dma("s", T.ys[:], T.yso[:], [("yso", 0, 256)], [])
+    ts(R("i1", 8, 16), R("i1", 16, 24), 15, OP.bitwise_and)
+    ts(R("i1", 8, 16), R("i1", 8, 16), 8.0, OP.mult)
+    ts(R("i1", 24, 32), R("i1", 16, 24), 4, OP.arith_shift_right)
+    tt(R("i1", 24, 32), R("i1", 24, 32), R("i1", 8, 16), OP.add)
+    cp(R("pm16", 8, 16), R("i1", 24, 32))
+    cp(R("yo1"), IX(R("cI"), R("pm16", 8, 16)))
+    dma("y", T.yc[:], T.yo1[:], [("yo1", 0, 128)], [])
+    lanes_post(t)
+    last = res(L("cur"))
+    dma("y", T.yl[:], ap(last), flat(last), [])
+    spread(384, "ID", L("w"), (R("ID"), R("HALF")))
+    ts(R("t2"), R("mq"), 0.0, OP.is_equal)
+    tt(Pd, R("mq"), WX, OP.is_gt)
+    tt(R("t1"), Pd, R("t2"), OP.max)
+    cp(R("yo2"), IX(R("t1"), R("pm16", 8, 16)))
+    dma("y", T.yh[:], T.yo2[:], [("yo2", 0, 128)], [])
     build()
     for sem in sorted(cnt):
         if known["g"].get(sem, 0) < cnt[sem]:

@@ -7,29 +7,33 @@ LKW = IWW + 2048
 SNAP, GOT0, E01, GOT1, E2, GOT2, E3, GOT3, E4, GOT4 = (2048 * i for i in range(10))
 GOT = (GOT0, GOT1, GOT2, GOT3, GOT4)
 ES = (E01, E01, E2, E3, E4)
-LAG = (2.5, 4.5, 7.0, 0.1, 0.15)
-HOLD = 1000.0
+LAG = (1.4, 3.0, 4.5, 0.13, 0.15)
+HOLD, ROUNDS, ORDER = (0.0, 0.3, 0.6), 4, {}
+IWV = 3
+LKV, LKS = 3, 5
 CH = (0, 512, 1024, 1536, 2048)
 
 SCRATCH = {
     "V": ("sbuf", [128, VW], "bfloat16"), "EB": ("sbuf", [128, 20480], "bfloat16"),
-    "mx": ("sbuf", [128, 2048], "bfloat16"), "cR": ("sbuf", [128, 2048], "float32"),
+    "mx": ("sbuf", [128, 2048], "bfloat16"), "KS": ("sbuf", [128, 2304], "bfloat16"), "KB": ("sbuf", [128, 144], "bfloat16"),
+    "csH": ("sbuf", [128, 128], "float16"),
     "IW": ("sbuf", [128, IWW], "float32"), "LK": ("sbuf", [128, LKW], "float32"),
     "LV": ("sbuf", [128, 256], "float32"), "C64": ("sbuf", [128, 256], "float32"),
-    "SELC": ("sbuf", [128, 2048], "bfloat16"), "SELPK": ("sbuf", [128, 2048], "bfloat16"), "SELW": ("sbuf", [128, 2048], "bfloat16"),
-    "SELT": ("sbuf", [128, 1024], "bfloat16"), "EQ": ("sbuf", [128, 4096], "bfloat16"), "LH": ("sbuf", [128, 128], "bfloat16"),
+    "SELC": ("sbuf", [128, 144], "bfloat16"), "SELPK": ("sbuf", [128, 144], "bfloat16"), "ysR": ("sbuf", [128, VW], "float32"),
+    "LV0": ("sbuf", [128, 512], "float32"), "aww": ("sbuf", [128, 16], "float32"),
+    "SELT": ("sbuf", [128, 240], "bfloat16"), "EQ": ("sbuf", [128, 4096], "bfloat16"), "LH": ("sbuf", [128, 128], "bfloat16"),
     "MK": ("sbuf", [128, 256], "bfloat16"), "qw": ("sbuf", [128, 256], "bfloat16"), "abR": ("sbuf", [128, 256], "bfloat16"),
-    "naL": ("sbuf", [128, 256], "bfloat16"), "o2": ("sbuf", [128, 112], "float32"), "o16": ("sbuf", [128, 32], "uint16"),
-    "ONE": ("sbuf", [128, 128], "bfloat16"), "OPW": ("sbuf", [128, 512], "float32"), "OPB": ("sbuf", [128, 256], "bfloat16"),
-    "OR": ("sbuf", [128, 256], "float32"), "JC": ("sbuf", [128, 256], "float32"), "K": ("sbuf", [128, 256], "float32"),
+    "naL": ("sbuf", [128, 512], "bfloat16"), "o2": ("sbuf", [128, 144], "float32"), "o16": ("sbuf", [128, 32], "uint16"),
+    "ONE": ("sbuf", [128, 128], "bfloat16"), "OPW": ("sbuf", [128, 512], "float32"), "OPB": ("sbuf", [128, 512], "bfloat16"),
+    "JC": ("sbuf", [128, 256], "float32"), "K": ("sbuf", [128, 256], "float32"),
     "COMP": ("sbuf", [128, 512], "float32"), "DUM": ("sbuf", [128, 48], "float32"), "wR": ("sbuf", [128, 256], "float32"),
     "clOp": ("sbuf", [128, 256], "float32"), "G": ("sbuf", [128, 256], "float32"), "RW": ("sbuf", [128, 512], "float16"),
     "DR": ("sbuf", [128, 256], "bfloat16"), "decL": ("sbuf", [128, 256], "bfloat16"), "gnR": ("sbuf", [128, 256], "bfloat16"),
-    "Dl": ("sbuf", [128, 384], "bfloat16"), "yso": ("sbuf", [128, 256], "float32"),
+    "Dl": ("sbuf", [128, 384], "bfloat16"), "WD": ("sbuf", [128, 384], "float32"), "W128": ("sbuf", [128, 128], "bfloat16"),
     "i1": ("sbuf", [128, 48], "int32"), "col": ("sbuf", [128, 40], "float32"), "B8": ("sbuf", [128, 24], "bfloat16"),
     "lane": ("sbuf", [128, 640], "float32"), "lb16": ("sbuf", [128, 160], "bfloat16"), "lh16": ("sbuf", [128, 64], "float16"),
     "code0": ("sbuf", [128, 16], "float32"), "code1": ("sbuf", [128, 16], "float32"), "awk": ("sbuf", [128, 80], "float32"),
-    "Ls": ("sbuf", [128, 48], "int32"), "L16": ("sbuf", [128, 48], "uint16"), "pm16": ("sbuf", [128, 40], "uint16"),
+    "Ls": ("sbuf", [128, 48], "int32"), "L16": ("sbuf", [128, 48], "uint16"), "pm16": ("sbuf", [128, 44], "uint16"),
     "wkI": ("sbuf", [128, 16], "int32"), "wk5": ("sbuf", [128, 80], "int32"), "pI": ("sbuf", [128, 16], "int32"),
 }
 for _n in ("csI", "hdI", "Cz", "cI", "Bv", "hI", "h", "yI0", "yI1"):
@@ -49,7 +53,7 @@ for _t in range(STEPS):
     SCRATCH["ln%d" % _t] = ("sbuf", [128, 128], "int32")
 for _n in ("PD", "PP", "PR", "PX", "PL", "PW", "V0", "V1"):
     SCRATCH[_n] = ("psum", [128, 512], "float32")
-PLACES = {"lane": 3, "lb16": 3, "lh16": 2, "t1": 3, "t2": 3, "t3": 2, "Bv": 2, "hI": 2, "h": 2, "z": 2, "cl16": 2, "p16": 2, "c16": 2,
+PLACES = {"lane": 3, "lb16": 3, "lh16": 2, "t1": 10, "t2": 10, "t3": 4, "Bv": 3, "hI": 4, "h": 3, "z": 2, "cl16": 2, "p16": 2, "c16": 2,
           "cI": 2, "pI": 2, "mq": 2, "LV": 2, "cur16": 2}
 for _n in PLACES:
     SCRATCH[_n] = (SCRATCH[_n][0], [128, SCRATCH[_n][1][1] * PLACES[_n]], SCRATCH[_n][2])
@@ -61,7 +65,7 @@ for _t in range(STEPS):
         SEMAPHORES += ["a%s%d" % (_m, _t), "l%s%d" % (_m, _t)]
 
 _L = {}
-for _b, _names in (("lane", "cur cl clS s8 val mv cand candw wW dum q q2 q3 cur1 e1 e2 ng fd f0 dst dec ncode thrab "
+for _b, _names in (("lane", "cur cl clS s8 val mv cand ac naw dum q2 q3 cur1 e1 e2 ng fd f0 dst dec ncode thrab "
                             "d8 w1 z0 c511 thrT clB dB clA x1 x2 qq"),
                    ("lb16", "ab cm sel done w aw winT"), ("lh16", "rdy incl rc c511h")):
     for _i, _n in enumerate(_names.split()):
@@ -206,11 +210,11 @@ def rank_program(g, core, T, topo):
         cyc = n
         if out[0] == "i": cyc = 3.8 * n + 50
         elif any(isinstance(x, tuple) and x[0] == "i" for x in r): cyc = 1.56 * n + 50
-        elif q == "t": return 1.1 * 0.00083 * max(64, wid(r[1]))
+        elif q == "t": return 0.00083 * max(64, wid(r[1]))
         elif kind == "tt": cyc = n if any(ispsum[x[1]] for x in r) else 2 * n
         elif q == "g": cyc = 2 * n + 150
         elif q == "v" and short(out) and all(short(x) for x in r[:1]): cyc = n / 2
-        return 1.1 * (max(64, cyc) * 0.00083 + (0.06 if q == "s" else 0.01))
+        return max(64, cyc) * 0.00083 + (0.06 if q == "s" else 0.01)
 
     def comp(q, reads, writes, fn, kind="ts"):
         r = [res(x) for x in reads]
@@ -237,7 +241,7 @@ def rank_program(g, core, T, topo):
 
     def out_send(t, m, srcspec):
         s = res(srcspec)
-        recs.append(("g", [(flat(s), [], lambda: (t, m, s))], 0.9, "r", None))
+        recs.append(("g", [(flat(s), [], lambda: (t, m, s))], 0.4, "r", None))
         sent[(t, m)] = len(recs) - 1
         recs.append(("net", [([], [landing(m, t)], None)], 0.0, "a", (t, m)))
 
@@ -257,11 +261,13 @@ def rank_program(g, core, T, topo):
                     hl.append((lo, hi, w, i))
                     if ispsum.get(b, False): banks[i].add(b)
             if recs[i][3] == "a": pred[i].add(sent[recs[i][4]])
+        for i in range(1, LOADS): pred[i].add(i - 1)
         succ = [[] for _ in range(n)]
         for i in range(n):
             for d in pred[i]: succ[d].append(i)
 
         def lag(d, i):
+            if i < LOADS: return 0.0
             if recs[d][3] == "d": return recs[d][4]
             if recs[i][3] == "a":
                 t, m = recs[i][4]
@@ -270,42 +276,59 @@ def rank_program(g, core, T, topo):
             if recs[d][3] == "r": return 3.0
             return LAG[3] if recs[d][0] == recs[i][0] else LAG[4]
 
-        prio = [0.0] * n
-        for i in range(n - 1, -1, -1):
-            prio[i] = recs[i][2] + max([lag(i, j) + prio[j] for j in succ[i]] + [recs[i][4] if recs[i][3] == "d" else 0.0])
-        left = [len(p) for p in pred]
-        est = [0.0] * n
-        ready = {}
-        free = {}
-        for i in range(n):
-            if left[i] == 0: ready.setdefault(recs[i][0], []).append(i)
-        order = []
-        held = {}
+        tail = [recs[i][4] if recs[i][3] == "d" else 0.0 for i in range(n)]
+        lags = {(d, i): lag(d, i) for i in range(n) for d in pred[i]}
 
-        def when(i):
-            return max([est[i]] + [e + LAG[4] for b in banks[i] for q2, e in held.get(b, {}).items() if q2 != recs[i][0]])
+        def place(prio, back, hold):
+            before, after = (succ, pred) if back else (pred, succ)
+            left = [len(p) for p in before]
+            est = list(tail) if back else [0.0] * n
+            ready, free, held, order, ends = {}, {}, {}, [], [0.0] * n
+            for i in range(n):
+                if left[i] == 0: ready.setdefault(recs[i][0], []).append(i)
 
-        for _ in range(n):
+            def when(i):
+                if not banks[i]: return est[i]
+                return max([est[i]] + [e + LAG[4] for b in banks[i] for q2, e in held.get(b, {}).items() if q2 != recs[i][0]])
+
+            for _ in range(n):
+                best = None
+                for q, rl in ready.items():
+                    if not rl: continue
+                    t0 = max(free.get(q, 0.0), min(when(i) for i in rl))
+                    if best is None or t0 < best[0]: best = (t0, q)
+                t0, q = best
+                i = max([x for x in ready[q] if when(x) <= t0 + 1e-9], key=lambda x: (prio[x], -x))
+                soon = [x for x in ready[q] if t0 < when(x) < t0 + hold * recs[i][2] and prio[x] > prio[i] + recs[i][2]]
+                if soon:
+                    i = min(soon, key=when); t0 = when(i)
+                ready[q].remove(i)
+                order.append(i)
+                ends[i] = t0 + recs[i][2]
+                for b in banks[i]: held.setdefault(b, {})[q] = ends[i]
+                if q != "net": free[q] = ends[i]
+                for j in after[i]:
+                    est[j] = max(est[j], ends[i] + (lags[(j, i)] if back else lags[(i, j)]))
+                    left[j] -= 1
+                    if left[j] == 0: ready.setdefault(recs[j][0], []).append(j)
+            return order, ends
+
+        key = (n, round(sum(lags.values()), 3))
+        if key not in ORDER:
+            way = [0.0] * n
+            for i in range(n - 1, -1, -1):
+                way[i] = recs[i][2] + max([lags[(i, j)] + way[j] for j in succ[i]] + [tail[i]])
+            ORDER["way"] = max(way)
             best = None
-            for q, rl in ready.items():
-                if not rl: continue
-                t0 = max(free.get(q, 0.0), min(when(i) for i in rl))
-                if best is None or t0 < best[0]: best = (t0, q)
-            t0, q = best
-            can = [x for x in ready[q] if when(x) <= t0 + 1e-9]
-            i = max(can, key=lambda x: (prio[x], -x))
-            soon = [x for x in ready[q] if t0 < when(x) < t0 + recs[i][2] and prio[x] - prio[i] > HOLD * (when(x) - t0) + recs[i][2]]
-            if soon:
-                i = min(soon, key=when); t0 = when(i)
-            ready[q].remove(i)
-            order.append(i)
-            end = t0 + recs[i][2]
-            for b in banks[i]: held.setdefault(b, {})[q] = end
-            if q != "net": free[q] = end
-            for j in succ[i]:
-                est[j] = max(est[j], end + lag(i, j))
-                left[j] -= 1
-                if left[j] == 0: ready.setdefault(recs[j][0], []).append(j)
+            for hold in HOLD:
+                prio = way
+                for _ in range(ROUNDS):
+                    order, ends = place(prio, False, hold)
+                    total = max(ends[i] + tail[i] for i in range(n))
+                    if best is None or total < best[0]: best = (total, order)
+                    prio = place(ends, True, hold)[1]
+            ORDER[key] = best[1]; ORDER["total"] = best[0]
+        order = ORDER[key]
         for i in order:
             q, items, _, kind, x = recs[i]
             for rd, wr, fn in items:
@@ -354,9 +377,8 @@ def rank_program(g, core, T, topo):
 
     def act(out, a, func=AF.Copy, scale=1.0, bias=None):
         def call(r, w):
-            sc = ap(r[1]) if isinstance(scale, tuple) else scale
-            if bias is None: return g.scalar.activation(out=ap(w[0]), in_=ap(r[0]), func=func, scale=sc)
-            return g.scalar.activation(out=ap(w[0]), in_=ap(r[0]), func=AF.Identity if func == AF.Copy else func, bias=ap(r[2]), scale=sc)
+            if bias is None: return g.scalar.activation(out=ap(w[0]), in_=ap(r[0]), func=func, scale=scale)
+            return g.scalar.activation(out=ap(w[0]), in_=ap(r[0]), func=AF.Identity if func == AF.Copy else func, bias=ap(r[2]), scale=scale)
         comp("s", [a, scale, bias], [out], call)
 
     def scatter_act(out, a):
@@ -372,7 +394,7 @@ def rank_program(g, core, T, topo):
         comp("g", [a], [out], lambda r, w: g.affine_select(ap(w[0]), ap(r[0]), pattern, op, 0.0, base, cm))
 
     def to_list(out, sel, src, lo, n):
-        together(lambda: [mm(out, R(sel, 128 * i, 128 * i + 128), R(src, lo + i, lo + n, 16), i == 0, i == 15) for i in range(16)])
+        together(lambda: [mm(out, R(sel, 15 - i, 143 - i), R(src, lo + i, lo + n, 16), i == 0, i == 15) for i in range(16)])
 
     def spread(lo, diag, src, first=None):
         def run():
@@ -388,11 +410,12 @@ def rank_program(g, core, T, topo):
     DM = (R("o2", 0, 16), R("o2", 16, 32), R("o2", 32, 48))
     oL = R("jW", 0, 16)
 
-    dma("y", T.csI[:], T.cs[:], [], [("csI", 0, 128)])
-    dma("s", T.EB[:, SNAP:SNAP + 2048], T.snap[:], [], [("EB", SNAP, SNAP + 2048)], 3.0)
-    dma("y", T.V[:, 0:4096], T.x[:], [], [("V", 0, 4096)], 4.0)
-    dma("y", T.hdI[:], T.hold[:], [], [("hdI", 0, 128)])
-    dma("y", T.wkI[:], T.wake[:], [], [("wkI", 0, 16)])
+    LOADS = 5
+    dma("y", T.EB[:, SNAP:SNAP + 2048], T.snap[:], [], [("EB", SNAP, SNAP + 2048)], 3.0)
+    dma("s", T.csI[:], T.cs[:], [], [("csI", 0, 128)], 3.0)
+    dma("s", T.hdI[:], T.hold[:], [], [("hdI", 0, 128)], 3.2)
+    dma("y", T.V[:, 0:4096], T.x[:], [], [("V", 0, 4096)], 5.5)
+    dma("y", T.wkI[:], T.wake[:], [], [("wkI", 0, 16)], 5.7)
     fill(R("ONE"), 1.0)
     iota(R("i1", 0, 1), [[0, 1]], 0, 1)
     iota(R("i1", 8, 16), [[16, 8]], 0, 0)
@@ -403,12 +426,13 @@ def rank_program(g, core, T, topo):
     asel(R("ID"), R("B128"), [[-1, 128]], OP.is_equal, 0, 1)
     iota(R("t3"), [[0, 16], [1, 8]], 0, 0)
     asel(R("UT"), R("B128"), [[-1, 128]], OP.is_ge, 0, 1)
-    iota(R("OR"), [[1, 256]], 0, 0)
     iota(R("JC"), [[128, 16], [1, 16]], 0, 0)
     iota(R("DR"), [[0, 16], [1, 16]], 0, 0)
     iota(R("i1", 32, 48), [[1, 16]], 0, 0)
-    for a in range(0, IWW, 576):
-        iota(R("IW", a, a + 576), [[1, 576]], a, 0)
+    iota(R("IW", 0, 512), [[1, 512]], 0, 0)
+    for a in range(512, IWW, 512):
+        if a <= 512 * IWV: ts(R("IW", a, a + 512), R("IW", 0, 512), float(a), OP.add)
+        else: iota(R("IW", a, a + 512), [[1, 512]], a, 0)
     ts(R("i1", 1, 2), R("i1", 0, 1), 15, OP.bitwise_and)
     ts(R("i1", 2, 3), R("i1", 0, 1), 1, OP.bitwise_and)
     ts(R("i1", 3, 4), R("i1", 1, 2), 1, OP.arith_shift_right)
@@ -420,7 +444,9 @@ def rank_program(g, core, T, topo):
     ts(C(5), C(4), 1.0, OP.add)
     ts(C(6), C(1), 1.0 / 8192, OP.mult)
     ts(C(7), C(1), -0.25, OP.mult)
-    ts(C(8), C(0), 1.0, OP.add, 16.0, OP.mult)
+    ts(C(8), C(0), 1.0, OP.add)
+    iota(R("col", 21, 26), [[1, 5]], 66, 0)
+    iota(R("col", 26, 31), [[-2, 5]], -1, 0)
     ts(R("i1", 16, 24), R("i1", 8, 16), C(0), OP.add)
     ts(R("i1", 8, 16), R("i1", 16, 24), 3, OP.arith_shift_right)
     cp(R("pm16", 16, 24), R("i1", 8, 16))
@@ -433,8 +459,7 @@ def rank_program(g, core, T, topo):
     cp(R("cI"), IX(R("csI"), R("pm16", 0, 8)))
     cp(R("c16"), R("cI"))
     fill(R("SELC"), 0.0)
-    for i in range(16):
-        ts(R("SELC", 129 * i, 128 * i + 128, 16), R("B128", i, 128, 16), 1.0 / 16, OP.mult)
+    ts(R("SELC", 15, 143, 16), R("B128", 0, 128, 16), 1.0 / 16, OP.mult)
     ts(R("SELPK"), R("SELC"), C(5), OP.mult, 16.0, OP.mult)
     ts(R("B8", 0, 8), R("B128", 0, 128, 16), -1.0, OP.mult)
     ts(R("B8", 8, 16), R("B128", 0, 128, 16), 2.0, OP.mult)
@@ -442,22 +467,20 @@ def rank_program(g, core, T, topo):
     ts(Pk, R("t3"), 8192.0 * 7, OP.add)
     ts(R("m01"), R("t3"), 0.0, OP.is_gt)
     ts(R("negk"), R("t3"), -8.5, OP.add)
+    ts(R("MK"), R("DR"), C(0), OP.is_equal)
+    fill(C(20), 2048.0); fill(C(15), 24.0); fill(C(31), 2.0)
     fill(C(16), -2048.0); fill(C(17), -8.0); fill(C(18), -150.0); fill(C(19), 1.0 / 16)
     fill(R("SELT"), 0.0)
-    ts(R("GM", 0, 16), R("OR", 0, 16), C(0), OP.is_equal, 32.0, OP.mult)
-    for gg in range(8):
-        cp(R("SELT", 144 * gg, 144 * gg + 16), R("GM", 0, 16))
+    ts(R("SELT", 112, 128), R("IW", 0, 16), C(0), OP.is_equal, 32.0, OP.mult)
     ts(R("IDb"), R("ID"), -2097152.0, OP.mult)
     fill(R("HALF"), 0.5); fill(R("HALFn"), -0.5)
 
-    def sums_AB(lo):
+    def new_cells_of(lo, y, stamp, bank="PP", tmp=Pa):
         for h in range(2):
-            to_list(R("PP", 64 * h, 64 * h + 64), "SELPK", "EB", lo + 1024 * h, 1024)
-
-    def new_cells_of(y, stamp):
-        ts(R("Bv"), R("PP", 0, 128), -0.4985, OP.add)
-        tt(Pa, R("PP", 0, 128), R("Bv"), OP.subtract)
-        tt(R("t1"), Pa, R("Bv"), OP.mult)
+            to_list(R(bank, 64 * h, 64 * h + 64), "SELPK", "EB", lo + 1024 * h, 1024)
+        ts(R("Bv"), R(bank, 0, 128), -0.4985, OP.add)
+        tt(tmp, R(bank, 0, 128), R("Bv"), OP.subtract)
+        tt(R("t1"), tmp, R("Bv"), OP.mult)
         ts(R("hI"), R("t1"), 256.0, OP.mult, -0.4375, OP.add)
         ts(R("h"), R("hI"), 511, OP.bitwise_and)
         ts(R("h", 0, 128, 8), R("hI", 0, 128, 8), 4095, OP.bitwise_and)
@@ -488,25 +511,24 @@ def rank_program(g, core, T, topo):
         def run():
             if t > 0: mm(BS, R("IDb"), L("done"), True, False)
             for gg in range(8):
-                mm(BS, R("SELT", 128 * gg, 128 * gg + 128), R("bd", gg, 128, 8), t == 0 and gg == 0, gg == 7)
+                mm(BS, R("SELT", 112 - 16 * gg, 240 - 16 * gg), R("bd", gg, 128, 8), t == 0 and gg == 0, gg == 7)
         together(run)
 
     def code_out(t):
         c = R("code%d" % (t & 1))
         tt(c, BS, L("w"), OP.max)
         out_send(t, "co", c)
-        ts(L("ncode"), c, -1.0, OP.mult)
-        ts(L("thrab"), c, -1.0, OP.mult, 24.0, OP.add)
+        act(L("ncode"), c, scale=-1.0)
+        act(L("thrab"), c, scale=-1.0, bias=C(15))
 
     def cells_out(t):
         y = "yI%d" % (t & 1)
-        sums_AB(GOT[t])
-        new_cells_of(y, t + 2)
+        new_cells_of(GOT[t], y, t + 2)
         for u in ((0, 1) if t == 0 else (t + 1,) if t + 1 < STEPS else ()):
             out_send(u, "nc", R(y))
         if t > 0:
-            tt(R("t1"), DX, R(y), OP.mult)
-            tt(R("nZ"), R("nZ"), R("t1"), OP.min)
+            tt(Pb, DX, R(y), OP.mult)
+            tt(R("nZ"), Pb, R("nZ"), OP.min)
 
     act(R("EB", E01, E01 + 2048), IX(R("EB", SNAP, SNAP + 2048), R("ei16")))
     ts(R("t3"), IX(R("hdI"), R("pm16", 0, 8)), -1.0, OP.mult, 1.0, OP.add)
@@ -515,46 +537,49 @@ def rank_program(g, core, T, topo):
     columns(0)
     code_out(0)
     cells_out(0)
-    sums_AB(E01)
-    new_cells_of("Cz", 1)
+    new_cells_of(E01, "Cz", 1, "PW", Pb)
     ts(R("nZ"), R("Cz"), -1.0, OP.mult)
     cp(R("Cz"), R("cI"))
     spread(384, "ID", L("w"), (R("ID"), R("HALF")))
     tt(R("t1"), WX, R("z"), OP.subtract)
     ts(R("t1"), R("t1"), 1.0, OP.add)
     tt(R("mq"), R("t1"), R("t3"), OP.mult)
-    cp(R("ck16"), R("csI"))
-    act(R("cR"), IX(R("IW", 0, 4096), R("ck16")))
-    dma("y", T.K[0:128:2, :], T.cR[0:128:16, :], [("cR", 0, 2048)], [("K", 0, 256)])
-    dma("y", T.K[1:128:2, :], T.cR[0:128:16, :], [("cR", 0, 2048)], [("K", 256, 512)])
+    ts(R("csH"), R("csI"), -2048.0, OP.add)
+    fill(R("KB"), 0.0)
+    cp(R("KB", 14, 142, 16), R("B128", 0, 128, 16)); cp(R("KB", 15, 143, 16), R("B128", 0, 128, 16))
+    for i in range(16):
+        ts(R("KS", 144 * i, 144 * i + 144), R("KB"), R("MK", i, i + 1), OP.mult)
+        together(lambda: [mm(R("PX", i, 256, 16), R("KS", 144 * i + 14 - 2 * k, 144 * i + 142 - 2 * k), R("csH", 16 * k, 16 * k + 16), k == 0, k == 7)
+                          for k in range(8)])
     ts(R("JC"), R("JC"), C(3), OP.add, C(2), OP.mult)
-    for a in range(0, IWW, 1152):
-        fill(R("LK", a, a + 1152), 64.0)
-    ts(R("LK", 4096, IWW, 2), R("OR"), 8.0, OP.mult, 71.0, OP.add)
+    act(R("K"), R("PX", 0, 256), bias=C(20))
+    for a in range(0, 4096, 512):
+        if a < 512 * LKV: fill(R("LK", a, a + 512), 64.0)
+        elif a < 512 * LKS: act(R("LK", a, a + 512), R("LK", 0, 512), AF.Silu)
+        else: iota(R("LK", a, a + 512), [[0, 512]], 64, 0)
+    iota(R("LK", 4096, IWW), [[8, 256], [0, 2]], 71, 0)
     ts(R("t1"), R("jW"), float(IWW), OP.add)
     tt(R("t2"), R("csI"), R("t1"), OP.subtract)
     tt(R("t2"), R("t2"), R("hdI"), OP.mult)
     tt(R("t2"), R("t2"), R("t1"), OP.add)
     cp(R("lk16"), R("t2"))
-    fill(C(20), 65.0)
-    act(R("LV"), R("OR"), scale=8.0, bias=C(20))
-    for k in range(8):
-        scatter_act(IX(R("LK"), R("lk16", 16 * k, 16 * k + 16)), R("LV"))
-    fill(R("clOp"), 1 / 1.75); fill(R("G"), 0.0)
-    comp("v", [R("clOp"), R("G")], [R("wR")], lambda r, w: g.vector.tensor_tensor_scan(ap(w[0]), ap(r[0]), ap(r[1]), 1.75 ** 120, OP.mult, OP.add))
-    tt(R("t1"), R("wR", 0, 128), R("ID"), OP.mult)
+    iota(R("LV0"), [[0, 2], [8, 256]], 65, 0)
+    for k in range(4):
+        scatter_act(IX(R("LK"), R("lk16", 32 * k, 32 * k + 32)), R("LV0"))
+    fill(R("t1"), 1 / 1.75)
+    comp("v", [R("t1"), R("ONE")], [Pc], lambda r, w: g.vector.tensor_tensor_scan(ap(w[0]), ap(r[0]), ap(r[1]), 1.75 ** 120, OP.mult, OP.mult))
+    tt(R("t1"), Pc, R("ID"), OP.mult)
     reduce_add(C(9), R("t1"))
     fill(L("thrT"), 2.5)
     upper = R("lane", _L["thrT"][1] + 8, _L["thrT"][1] + 16)
     ts(upper, upper, 1.75 ** -64, OP.mult, 1.75 ** -64, OP.mult)
     ts(L("thrT"), L("thrT"), C(9), OP.mult)
-    ts(R("MK"), R("DR"), C(0), OP.is_equal)
-    tt(R("t1", 0, 16), R("wR", 0, 16), R("MK", 0, 16), OP.mult)
+    tt(R("t1", 0, 16), R("V0", 256, 272), R("MK", 0, 16), OP.mult)
     reduce_add(C(13), R("t1", 0, 16))
     ts(C(13), C(13), 1.75 ** -119, OP.mult)
-    ts(L("wW"), R("wR", 0, 256, 16), C(13), OP.mult)
+    ts(R("o2", 48, 56), R("V0", 256, 384, 16), C(13), OP.mult)
+    ts(R("o2", 56, 64), R("o2", 48, 56), 1.75 ** -64, OP.mult, 1.75 ** -64, OP.mult)
     for t in range(STEPS):
-        fill(C(21 + t), 66.0 + t); fill(C(26 + t), -1.0 - 2 * t)
         ts(R("wk5", 16 * t, 16 * t + 16), R("wkI"), t, OP.arith_shift_right, 1, OP.bitwise_and)
     cp(R("awk"), R("wk5"))
     cp(L("cur"), oL)
@@ -562,11 +587,13 @@ def rank_program(g, core, T, topo):
     ts(DM[1], oL, float(IWW), OP.add)
     ts(DM[2], oL, float(IWW - 2048), OP.add)
     cp(R("pm16", 24, 40), R("i1", 32, 48))
+    ts(R("pm16", 40, 44), R("HALF", 0, 4), 0.0, OP.mult, C(0), OP.add)
     cp(R("B8", 16, 24), R("B128", 0, 128, 16))
     ts(L("dum"), oL, 2.0, OP.mult, 4096.0, OP.add)
     ts(L("c511"), oL, -1.0, OP.mult, 511.0, OP.add)
     cp(L("c511h"), L("c511"))
-    fill(L("z0"), 0.0); fill(L("dec"), 0.0)
+    fill(L("z0"), 0.0); fill(L("dec"), 0.0); fill(L("e2"), 0.0)
+    ts(R("W128"), R("B128"), C(8), OP.mult)
     cp(R("posH"), R("jW"))
     ts(R("UT"), R("UT"), -1.0, OP.mult)
     ts(R("IDn"), R("ID"), -1.0, OP.mult); ts(R("IDk"), R("ID"), 2048.0, OP.mult)
@@ -574,8 +601,8 @@ def rank_program(g, core, T, topo):
     asel(R("GM"), R("qw", 0, 128), [[0, 16], [16, 8]], OP.is_ge, 15, -1)
     for c in range(1, 16):
         if c != 8: fill(R("EQ", 256 * c + 128 * (c // 8), 272 * c), 0.0)
-    fill(R("OPW"), 0.0); fill(C(14), 1.0)
-    fill(R("V", 4096, VW), 0.0)
+    iota(R("OPW", 0, 256), [[0, 256]], 0, 0)
+    fill(C(14), 1.0)
     ts(C(10), C(1), -0.5, OP.mult, 0.5, OP.add)
     ts(C(11), C(1), 0.5, OP.mult, 0.5, OP.add)
     ts(R("DUM", 0, 24), R("jW", 0, 24), 4096.0, OP.add, C(10), OP.mult)
@@ -588,7 +615,7 @@ def rank_program(g, core, T, topo):
         tt(Pd, R("mq"), WX, OP.is_equal)
         tt(R("t1"), Pd, R("cI"), OP.mult)
         scan(R("t3"), R("m01"), R("t1"), OP.mult, OP.add)
-        ts(L("f0"), L("w"), lim, OP.is_le)
+        act(L("f0"), L("w"), AF.Relu, -1.0, lim)
         tt(L("fd"), L("f0"), L("dum"), OP.mult)
         tt(out, R("t3", 7, 128, 8), L("fd"), OP.add)
 
@@ -607,33 +634,21 @@ def rank_program(g, core, T, topo):
         cp(L("clS"), R("PL", 0, 16))
         tt(L("s8"), R("PL", 16, 32), R("pI"), OP.subtract)
         if t == 0:
-            ts(L("val"), L("s8"), 1.0 / 16, OP.is_gt)
+            ts(L("val"), L("s8"), 1.0 / 16, OP.is_le)
         else:
-            act(R("decL"), IX(R("DR"), R("p16")))
-            to_list(R("PL", 32, 48), "SELC", "decL", 0, 256)
-            tt(L("val"), L("s8"), R("PL", 32, 48), OP.is_gt)
-        aw = R("awk", 16 * t, 16 * t + 16)
-        tt(L("mv"), aw, L("val"), OP.mult)
-        tt(L("cand"), aw, L("mv"), OP.subtract)
-        tt(L("candw"), L("cand"), L("wW"), OP.mult)
-        tt(L("q"), L("cur"), DM[0], OP.subtract)
-        tt(R("o2", 48, 64), L("cand"), L("q"), OP.mult)
-        if t < STEPS - 1:
-            tt(L("qq"), L("clS"), DM[2], OP.subtract)
-            tt(R("o2", 64, 80), L("cand"), L("qq"), OP.mult)
+            act(R("naL", 0, 256), IX(R("DR"), R("p16")))
+        ts(R("o2", 64, 80), L("e2"), -256.0, OP.add)
+        if t < STEPS - 1: tt(R("o2", 80, 96), L("clS"), DM[2], OP.subtract)
         tt(L("q2"), R("pI"), L("cur"), OP.subtract)
-        tt(L("q3"), L("q2"), L("mv"), OP.mult)
-        tt(L("cur1"), L("cur"), L("q3"), OP.add)
-        tt(L("e1"), L("cur1"), oL, OP.subtract)
         for c in range(16):
             b, lo = _L["clS"]
             ts(R("EQ", 272 * c, 256 * c + 256), R("RW", 16 * c, 256), R(b, lo + c, lo + c + 1), OP.is_equal)
         act(R("COMP", 0, 48), R("DUM"))
         iota(R("C64"), [[0, 256]], 64 * (t + 1), 0)
         if t < STEPS - 1:
-            if t == 0: act(R("LV"), R("OR"), scale=8.0, bias=C(21))
+            if t == 0: iota(R("LV"), [[8, 256]], 66, 0)
             else: act(R("LV"), IX(R("IW", 0, 256), R("cur16")), scale=8.0, bias=C(21 + t))
-            missing(L("clB"), "HALFn", 1.0)
+            missing(L("clB"), "HALFn", C(31))
             tt(L("dB"), L("clB"), L("cl"), OP.subtract)
 
     def judge(t):
@@ -646,8 +661,7 @@ def rank_program(g, core, T, topo):
                           mm(RA, R("IDn"), L("rc"), False, False), mm(RA, R("B128"), L("incl"), False, True)])
         cp(R("off16"), RA)
         ts(L("cm"), RA, 48.0, OP.is_lt)
-        comp("v", [R("K", 0, 512), R("JC")], [IX(R("COMP"), R("off16"))],
-             lambda r, w: g.vector.tensor_tensor(out=ap(w[0]), in0=T.K[:], in1=T.JC[:], op=OP.add))
+        tt(IX(R("COMP"), R("off16")), R("K"), R("JC"), OP.add)
         tt(R("Ls", 0, 24), R("COMP", 0, 24), R("COMP", 24, 48), OP.max)
         ts(R("L16", 0, 24), R("Ls", 0, 24), C(6), OP.mult, C(7), OP.add)
         act(R("Dl"), IX(R("lb%d" % t), R("L16", 0, 24)))
@@ -657,55 +671,67 @@ def rank_program(g, core, T, topo):
         tt(L("done"), L("cm"), L("ab"), OP.add)
         spread(0, "ID", L("sel"))
         spread(128, "IDn", L("done"))
-        tt(Pd, SX, R("ln%d" % t), OP.mult)
+        tt(Pf, SX, R("ln%d" % t), OP.mult)
         tt(R("t2"), SX, R("nZ"), OP.mult)
-        tt(Pe, Pd, R("t2"), OP.max)
+        tt(Pe, Pf, R("t2"), OP.max)
         tt(R("Cz"), Pe, R("Cz"), OP.max)
         ts(R("cI"), R("Cz"), 4095, OP.bitwise_and)
-        if t < STEPS - 1: cp(R("c16"), R("cI"))
-        cp(IX(R("V"), R("L16", 24, 48)), R("Dl"))
-        tt(R("t3"), DX, R("negk"), OP.mult)
-        tt(R("mq"), R("mq"), R("t3"), OP.max)
+        if t < STEPS - 1:
+            cp(R("c16"), R("cI"))
+            cp(IX(R("V"), R("L16", 24, 48)), R("Dl"))
+        else:
+            mm(R("PD", 0, 384), R("W128"), R("Dl"), True, True)
+            act(R("WD"), R("PD", 0, 384))
+            cp(IX(R("ysR"), R("L16", 24, 48)), R("WD"))
+        tt(Pg, DX, R("negk"), OP.mult)
+        tt(R("mq"), Pg, R("mq"), OP.max)
 
     def lanes_post(t):
-        if t < STEPS - 1 or t > 0:
-            ts(L("dst"), L("done"), float(t + 2), OP.mult)
+        if t == 0:
+            ts(L("x1"), L("ab"), -1.0, OP.mult, 1.0, OP.add)
+        else:
+            cp(R("ab16"), L("ab"))
+            act(R("abR"), IX(R("IW", 0, 8), R("ab16")), scale=-1.0, bias=C(14))
+            act(R("naL", 256, 512), IX(R("abR"), R("cur16")))
+        if True:
+            act(L("dst"), L("done"), scale=float(t + 2))
             tt(L("dec"), L("dec"), L("dst"), OP.max)
             cp(R("dec16"), L("dec"))
             act(R("DR"), IX(R("IW", 0, 8), R("dec16")), scale=0.125, bias=C(19))
         if t == 0:
             ts(L("ng"), L("done"), -1.0, OP.mult, 1.0, OP.add)
         else:
-            act(R("gnR"), IX(R("DR"), R("cur16")))
-            to_list(R("PL", 48, 64), "SELC", "gnR", 0, 256)
-            ts(L("ng"), R("PL", 48, 64), (t + 2) / 8.0, OP.is_lt)
+            act(R("OPB", 256, 512), IX(R("DR"), R("cur16")))
         n = 32 if t < STEPS - 1 else 16
-        if t == 0:
-            na = L("x1")
-            ts(na, L("ab"), -1.0, OP.mult, 1.0, OP.add)
-        else:
-            na = R("PL", 64, 80)
-            cp(R("ab16"), L("ab"))
-            act(R("abR"), IX(R("IW", 0, 8), R("ab16")), scale=-1.0, bias=C(14))
-            act(R("naL"), IX(R("abR"), R("cur16")))
-            to_list(na, "SELC", "naL", 0, 256)
-        tt(L("aw"), na, L("candw"), OP.mult)
-        tt(R("LH"), IX(L("aw"), R("pm16", 16, 24)), R("GM"), OP.mult)
-        for a in range(0, n, 16):
-            tt(R("o2", 80 + a, 96 + a), na, R("o2", 48 + a, 64 + a), OP.mult)
+        if t > 0:
+            to_list(R("PL", 32, 64), "SELC", "naL", 0, 512)
+            tt(L("val"), L("s8"), R("PL", 32, 48), OP.is_le)
+        aw = R("awk", 16 * t, 16 * t + 16)
+        tt(L("naw"), L("x1") if t == 0 else R("PL", 48, 64), aw, OP.mult)
+        tt(L("ac"), L("naw"), L("val"), OP.mult)
+        tt(L("cand"), aw, L("val"), OP.mult)
+        tt(L("mv"), aw, L("cand"), OP.subtract)
+        tt(L("q3"), L("q2"), L("mv"), OP.mult)
+        tt(L("e1"), L("e2"), L("q3"), OP.add)
+        tt(R("o2", 96, 112 + n), IX(L("ac"), R("pm16", 40, 41 + n // 16)), R("o2", 48, 64 + n), OP.mult)
+        tt(R("LH"), IX(R("o2", 96, 112), R("pm16", 16, 24)), R("GM"), OP.mult)
         together(lambda: [mm(R("PW", 8 * h, 8 * h + 8), R("EQ", 256 * c + 128 * h, 256 * c + 128 * h + 128), R("LH", 8 * c, 8 * c + 8), c == 0, c == 8 * h + 7)
                           for h in range(2) for c in range(8 * h + 8)])
         tt(L("winT"), R("PW", 0, 16), L("thrT"), OP.is_le)
         tt(R("qw"), IX(L("winT"), R("pm16", 24, 40)), R("MK"), OP.mult)
         together(lambda: [mm(R("PW", 32 + a + 8 * h, 40 + a + 8 * h), R("qw", 128 * h, 128 * h + 128), R("B8", 16, 24), True, True)
                           for a in range(0, n, 16) for h in range(2)])
-        tt(R("z", 0, n), R("PW", 32, 32 + n), R("o2", 80, 80 + n), OP.mult)
+        tt(R("z", 0, n), R("PW", 32, 32 + n), R("o2", 112, 112 + n), OP.mult)
         tt(R("z", 32, 32 + n), R("z", 0, n), R("o2", 0, n), OP.add)
         cp(R("o16", 0, n), R("z", 32, 32 + n))
         scatter_act(IX(R("OPW"), R("o16", 0, 16)), R("C64"))
-        act(R("OPB"), R("OPW", 0, 256), AF.Relu, 1.0 / 32, C(26 + t))
-        to_list(R("PW", 272, 288), "SELC", "OPB", 0, 256)
-        ts(L("d8"), L("done"), 8.0, OP.mult)
+        act(R("OPB", 0, 256), R("OPW", 0, 256), AF.Relu, 1.0 / 32, C(26 + t))
+        if t == 0:
+            to_list(R("PW", 272, 288), "SELC", "OPB", 0, 256)
+        else:
+            to_list(R("PW", 272, 304), "SELC", "OPB", 0, 512)
+            ts(L("ng"), R("PW", 288, 304), (t + 2) / 8.0, OP.is_lt)
+        act(L("d8"), L("done"), scale=8.0)
         tt(L("w1"), L("w"), L("d8"), OP.max)
         tt(L("w"), L("w1"), R("PW", 272, 288), OP.subtract)
         tt(L("e2"), L("e1"), L("ng"), OP.mult)
@@ -727,12 +753,16 @@ def rank_program(g, core, T, topo):
         return lambda: [act(R("EB", ES[t + 2] + a, ES[t + 2] + a + 512), IX(R("EB", lo, lo + 4096), R("ei16", a // 16, a // 16 + 32)))
                         for a in range(0, 2048, 512)]
 
-    missing(L("cl"), "HALF", 0.0)
+    missing(L("cl"), "HALF", C(14))
     cp(R("cl16"), L("cl"))
     for t in range(STEPS):
         lanes_pre(t)
+        if t == STEPS - 1:
+            for b in range(8):
+                bank = R(("PD", "PP")[b & 1])
+                mm(bank, R("W128"), R("V", 512 * b, 512 * b + 512), True, True)
+                act(R("ysR", 512 * b, 512 * b + 512), bank)
         judge(t)
-        if t == 0: act(R("SELW"), R("SELC"), scale=C(8))
         if t == STEPS - 1: break
         later = snapshots(t) if t < STEPS - 2 else None
         lanes_post(t)
@@ -741,9 +771,7 @@ def rank_program(g, core, T, topo):
         cells_out(t + 1)
         if later: later()
     t = STEPS - 1
-    together(lambda: [mm(R("PP", 0, 256), R("SELW", 128 * b, 128 * b + 128), R("V", 256 * b, 256 * b + 256), b == 0, b == 15) for b in range(16)])
-    act(R("yso"), R("PP", 0, 256))
-    dma("s", T.ys[:], T.yso[:], [("yso", 0, 256)], [])
+    dma("y", T.ys[:], T.ysR[0:128:16, 0:4096], [("ysR", 0, 4096)], [])
     ts(R("i1", 8, 16), R("i1", 16, 24), 15, OP.bitwise_and)
     ts(R("i1", 8, 16), R("i1", 8, 16), 8.0, OP.mult)
     ts(R("i1", 24, 32), R("i1", 16, 24), 4, OP.arith_shift_right)
@@ -754,12 +782,12 @@ def rank_program(g, core, T, topo):
     lanes_post(t)
     last = res(L("cur"))
     dma("y", T.yl[:], ap(last), flat(last), [])
-    spread(384, "ID", L("w"), (R("ID"), R("HALF")))
-    ts(R("t2"), R("mq"), 0.0, OP.is_equal)
-    tt(Pd, R("mq"), WX, OP.is_gt)
-    tt(R("t1"), Pd, R("t2"), OP.max)
-    cp(R("yo2"), IX(R("t1"), R("pm16", 8, 16)))
-    dma("y", T.yh[:], T.yo2[:], [("yo2", 0, 128)], [])
+    ts(Pd, R("mq"), 0.0, OP.is_equal, 99.0, OP.mult)
+    tt(R("t1"), Pd, R("mq"), OP.max)
+    ts(R("t2"), IX(R("t1"), R("pm16", 8, 16)), -0.5, OP.add)
+    together(lambda: [mm(R("PX", 384 + 16 * k, 400 + 16 * k), R("ID"), L("w"), True, True) for k in range(8)])
+    tt(R("yo2"), R("t2"), WX, OP.is_gt)
+    dma("s", T.yh[:], T.yo2[:], [("yo2", 0, 128)], [])
     build()
     for sem in sorted(cnt):
         if known["g"].get(sem, 0) < cnt[sem]:

@@ -8,7 +8,10 @@ SNAP, GOT0, E01, GOT1, E2, GOT2, E3, GOT3, E4, GOT4 = (2048 * i for i in range(1
 GOT = (GOT0, GOT1, GOT2, GOT3, GOT4)
 ES = (E01, E01, E2, E3, E4)
 LAG = (1.4, 3.0, 4.5, 0.13, 0.15)
-HOLD, ROUNDS, ORDER = (0.0, 0.3, 0.6), 4, {}
+HOLD, ROUNDS, ORDER = (0.0, 0.3, 0.6, 1.0), 60, {}
+FIRST = 1.8
+PART = 4
+STAGE = ((), (), (), (), ())
 IWV = 3
 LKV, LKS = 3, 5
 CH = (0, 512, 1024, 1536, 2048)
@@ -30,15 +33,16 @@ SCRATCH = {
     "clOp": ("sbuf", [128, 256], "float32"), "G": ("sbuf", [128, 256], "float32"), "RW": ("sbuf", [128, 512], "float16"),
     "DR": ("sbuf", [128, 256], "bfloat16"), "decL": ("sbuf", [128, 256], "bfloat16"), "gnR": ("sbuf", [128, 256], "bfloat16"),
     "Dl": ("sbuf", [128, 384], "bfloat16"), "WD": ("sbuf", [128, 384], "float32"), "W128": ("sbuf", [128, 128], "bfloat16"),
-    "i1": ("sbuf", [128, 48], "int32"), "col": ("sbuf", [128, 40], "float32"), "B8": ("sbuf", [128, 24], "bfloat16"),
+    "i1": ("sbuf", [128, 48], "int32"), "col": ("sbuf", [128, 40], "float32"), "B8": ("sbuf", [128, 32], "bfloat16"),
+    "QD": ("sbuf", [128, 128], "float32"), "asl": ("sbuf", [128, 80], "float32"),
     "lane": ("sbuf", [128, 640], "float32"), "lb16": ("sbuf", [128, 160], "bfloat16"), "lh16": ("sbuf", [128, 64], "float16"),
     "code0": ("sbuf", [128, 16], "float32"), "code1": ("sbuf", [128, 16], "float32"), "awk": ("sbuf", [128, 80], "float32"),
-    "Ls": ("sbuf", [128, 48], "int32"), "L16": ("sbuf", [128, 48], "uint16"), "pm16": ("sbuf", [128, 44], "uint16"),
+    "Ls": ("sbuf", [128, 48], "int32"), "L16": ("sbuf", [128, 48], "uint16"), "pm16": ("sbuf", [128, 48], "uint16"),
     "wkI": ("sbuf", [128, 16], "int32"), "wk5": ("sbuf", [128, 80], "int32"), "pI": ("sbuf", [128, 16], "int32"),
 }
-for _n in ("csI", "hdI", "Cz", "cI", "Bv", "hI", "h", "yI0", "yI1"):
+for _n in ("csI", "hdI", "Cz", "cI", "Bv", "hI", "h", "yI0", "yI1", "nZ"):
     SCRATCH[_n] = ("sbuf", [128, 128], "int32")
-for _n in ("jW", "m01", "negk", "mq", "nZ", "t1", "t2", "t3", "z", "yo1", "yo2"):
+for _n in ("jW", "m01", "negk", "mq", "t1", "t2", "t3", "z", "yo1", "yo2"):
     SCRATCH[_n] = ("sbuf", [128, 128], "float32")
 for _n in ("B128", "UT", "ID", "IDn", "IDk", "IDb", "HALF", "HALFn", "ZB", "bd", "GM"):
     SCRATCH[_n] = ("sbuf", [128, 128], "bfloat16")
@@ -51,31 +55,36 @@ for _t in range(STEPS):
     SCRATCH["lb%d" % _t] = ("sbuf", [128, 2048], "bfloat16")
     SCRATCH["lc%d" % _t] = ("sbuf", [128, 16], "float32")
     SCRATCH["ln%d" % _t] = ("sbuf", [128, 128], "int32")
-for _n in ("PD", "PP", "PR", "PX", "PL", "PW", "V0", "V1"):
+for _n in ("PD", "PP", "SA", "PX", "PL", "PW", "V0", "SB"):
     SCRATCH[_n] = ("psum", [128, 512], "float32")
 PLACES = {"lane": 3, "lb16": 3, "lh16": 2, "t1": 10, "t2": 10, "t3": 4, "Bv": 3, "hI": 4, "h": 3, "z": 2, "cl16": 2, "p16": 2, "c16": 2,
           "cI": 2, "pI": 2, "mq": 2, "LV": 2, "cur16": 2}
 for _n in PLACES:
     SCRATCH[_n] = (SCRATCH[_n][0], [128, SCRATCH[_n][1][1] * PLACES[_n]], SCRATCH[_n][2])
 
-MSG = ("b0", "b1", "co", "nc")
-SEMAPHORES = ["qv", "qs", "qt", "qg"] + ["d%d" % i for i in range(28)]
+
+def messages(t):
+    return ("b0", "b1", "b2", "b3", "co", "nc") if t == 0 else ("b0", "b1", "co", "nc")
+
+
+SEMAPHORES = ["qv", "qs", "qt", "qg"] + ["d%d" % i for i in range(26)]
 for _t in range(STEPS):
-    for _m in MSG:
+    for _m in messages(_t):
         SEMAPHORES += ["a%s%d" % (_m, _t), "l%s%d" % (_m, _t)]
 
 _L = {}
-for _b, _names in (("lane", "cur cl clS s8 val mv cand ac naw dum q2 q3 cur1 e1 e2 ng fd f0 dst dec ncode thrab "
+for _b, _names in (("lane", "cur cl clS s8 val mv x9 ac dum q2 q3 cur1 e1 e2 ng fd f0 dst dec ncode thrab "
                             "d8 w1 z0 c511 thrT clB dB clA x1 x2 qq"),
-                   ("lb16", "ab cm sel done w aw winT"), ("lh16", "rdy incl rc c511h")):
+                   ("lb16", "cm ab done w winT"), ("lh16", "rdy incl rc c511h")):
     for _i, _n in enumerate(_names.split()):
         _L[_n] = (_b, 16 * _i)
 TILED = ("lane", "lb16", "lh16")
 
 
 def landing(m, t):
-    if m == "b0": return "lb%d" % t, 0, 1024
-    if m == "b1": return "lb%d" % t, 1024, 2048
+    if m[0] == "b":
+        n = 2048 // (len(messages(t)) - 2)
+        return "lb%d" % t, n * int(m[1]), n * int(m[1]) + n
     if m == "co": return "lc%d" % t, 0, 16
     return "ln%d" % t, 0, 128
 
@@ -85,6 +94,7 @@ def route(core, t, T, topo):
     near = [x for x in topo.cores_of(core) if x != core and topo.die(x) == topo.die(core) and topo.may_write(x, dst)]
     far = [x for x in topo.cores_of(core) if topo.die(x) != topo.die(core) and topo.may_write(x, dst)]
     via = {"b0": far[0], "b1": far[1], "co": None, "nc": near[0]}
+    if t == 0: via.update(b0=near[-1], b1=near[0], b2=far[0], b3=far[1])
     if not topo.may_write(core, dst): via["co"] = near[-1]
     return dst, via
 
@@ -102,7 +112,7 @@ def relay_program(g, core, T, topo):
         done = []
         for t in range(STEPS):
             dst, via = route(src, t, T, topo)
-            for m in MSG:
+            for m in messages(t):
                 if via[m] != core: continue
                 buf, lo, hi = landing(m, t)
                 g.wait_ge(T.sem["a%s%d" % (m, t)], 8)
@@ -236,12 +246,13 @@ def rank_program(g, core, T, topo):
         got = group.pop()
         recs.append(("t", [x[0] for x in got], sum(x[1] for x in got), "c", None))
 
-    def dma(q, out, in_, reads, writes, lag=2.5):
+    def dma(q, out, in_, reads, writes, lag=1.5):
         recs.append((q, [(reads, writes, lambda: Q[q].dma_start(out, in_))], 0.06, "d", lag))
 
     def out_send(t, m, srcspec):
         s = res(srcspec)
-        recs.append(("g", [(flat(s), [], lambda: (t, m, s))], 0.4, "r", None))
+        first = (t, m) == (0, "b0")
+        recs.append(("g", [(flat(s), [], lambda: (t, m, s))], 0.4 + (FIRST if first else 0.0), "r", None))
         sent[(t, m)] = len(recs) - 1
         recs.append(("net", [([], [landing(m, t)], None)], 0.0, "a", (t, m)))
 
@@ -262,16 +273,21 @@ def rank_program(g, core, T, topo):
                     if ispsum.get(b, False): banks[i].add(b)
             if recs[i][3] == "a": pred[i].add(sent[recs[i][4]])
         for i in range(1, LOADS): pred[i].add(i - 1)
+        for x in sent:
+            if x != (0, "b0"): pred[sent[x]].add(sent[(0, "b0")])
+        pred[sent[(0, "co")] + 1].add(sent[(0, "b0")] + 1)
+        pred[sent[(0, "nc")] + 1].add(sent[(0, "b1")] + 1)
         succ = [[] for _ in range(n)]
         for i in range(n):
             for d in pred[i]: succ[d].append(i)
 
         def lag(d, i):
-            if i < LOADS: return 0.0
+            if i < LOADS or recs[d][3] == recs[i][3] == "r": return 0.0
+            if recs[d][3] == recs[i][3] == "a": return 0.5
             if recs[d][3] == "d": return recs[d][4]
             if recs[i][3] == "a":
                 t, m = recs[i][4]
-                if m[0] == "b": return LAG[2]
+                if m[0] == "b": return LAG[2] + (FIRST if t < 2 else 0.0)
                 return LAG[0] if route(core, t, T, topo)[1][m] is None else LAG[1]
             if recs[d][3] == "r": return 3.0
             return LAG[3] if recs[d][0] == recs[i][0] else LAG[4]
@@ -319,14 +335,17 @@ def rank_program(g, core, T, topo):
             for i in range(n - 1, -1, -1):
                 way[i] = recs[i][2] + max([lags[(i, j)] + way[j] for j in succ[i]] + [tail[i]])
             ORDER["way"] = max(way)
-            best = None
-            for hold in HOLD:
-                prio = way
-                for _ in range(ROUNDS):
-                    order, ends = place(prio, False, hold)
-                    total = max(ends[i] + tail[i] for i in range(n))
-                    if best is None or total < best[0]: best = (total, order)
-                    prio = place(ends, True, hold)[1]
+            best, prio = None, way
+            for r in range(ROUNDS):
+                hold = HOLD[r % len(HOLD)]
+                order, ends = place(prio, False, hold)
+                total = max(ends[i] + tail[i] for i in range(n))
+                if best is None or total < best[0]: best = (total, order, ends, prio, hold)
+                if r % 3 == 2:
+                    a = (r * 0.618) % 1.0
+                    prio = [a * x + (1 - a) * y * best[0] / ORDER["way"] for x, y in zip(best[3], way)]
+                else:
+                    prio = place(ends if r % 3 else best[2], True, hold)[1]
             ORDER[key] = best[1]; ORDER["total"] = best[0]
         order = ORDER[key]
         for i in order:
@@ -385,6 +404,7 @@ def rank_program(g, core, T, topo):
         comp("s", [a], [out], lambda r, w: g.scalar.activation(out=ap(w[0]), in_=ap(r[0]), func=AF.Silu))
 
     def mm(out, lhsT, rhs, start, stop, whole=None):
+        if out[1] == "PP": whole = R("PP")
         comp("t", [lhsT, rhs], [out] + ([whole] if whole else []), lambda r, w: g.tensor.matmul(ap(w[0]), ap(r[0]), ap(r[1]), start, stop))
 
     def iota(out, pattern, base, cm, after=()):
@@ -393,32 +413,34 @@ def rank_program(g, core, T, topo):
     def asel(out, a, pattern, op, base, cm):
         comp("g", [a], [out], lambda r, w: g.affine_select(ap(w[0]), ap(r[0]), pattern, op, 0.0, base, cm))
 
-    def to_list(out, sel, src, lo, n):
-        together(lambda: [mm(out, R(sel, 15 - i, 143 - i), R(src, lo + i, lo + n, 16), i == 0, i == 15) for i in range(16)])
+    def to_list(out, sel, src, lo, n, part=16):
+        for a in range(0, 16, part):
+            together(lambda: [mm(out, R(sel, 15 - i, 143 - i), R(src, lo + i, lo + n, 16), i == 0, i == 15) for i in range(a, a + part)])
 
-    def spread(lo, diag, src, first=None):
+    def spread(out, diag, src, first):
         def run():
-            if first: mm(R("PX", lo, lo + 128), first[0], first[1], True, False)
+            mm(out, R("ID"), first, True, False)
             for k in range(8):
-                mm(R("PX", lo + k, lo + 128, 8), R(diag), src, not first, not first or k == 7)
+                mm(R(out[1], out[2] + k, out[3], 8), R(diag), src, False, k == 7)
         together(run)
 
     Pa, Pb, Pc, Pk = (R("V0", 128 * i, 128 * i + 128) for i in range(4))
-    Pd, Pe, Pf, Pg = (R("V1", 128 * i, 128 * i + 128) for i in range(4))
-    SX, DX, IXD, WX = (R("PX", 128 * i, 128 * i + 128) for i in range(4))
-    RA, BS = R("PR", 0, 16), R("PR", 16, 32)
-    DM = (R("o2", 0, 16), R("o2", 16, 32), R("o2", 32, 48))
+    Pd, Pe, Pf, Pg = Pb, Pc, Pc, Pb
+    CX, AX, DX, WX = (R("PX", 128 * i, 128 * i + 128) for i in range(4))
+    IXD = R("PL", 128, 256)
+    RA, BS = R("PW", 340, 356), R("PL", 80, 96)
+    CL = R("QD", 97, 128, 2)
+    DM = (R("QD", 1, 32, 2), R("QD", 33, 64, 2), R("o2", 32, 48))
     oL = R("jW", 0, 16)
 
     LOADS = 5
+    dma("s", T.csI[:], T.cs[:], [], [("csI", 0, 128)], 1.5)
+    dma("s", T.hdI[:], T.hold[:], [], [("hdI", 0, 128)], 1.8)
     dma("y", T.EB[:, SNAP:SNAP + 2048], T.snap[:], [], [("EB", SNAP, SNAP + 2048)], 3.0)
-    dma("s", T.csI[:], T.cs[:], [], [("csI", 0, 128)], 3.0)
-    dma("s", T.hdI[:], T.hold[:], [], [("hdI", 0, 128)], 3.2)
-    dma("y", T.V[:, 0:4096], T.x[:], [], [("V", 0, 4096)], 5.5)
-    dma("y", T.wkI[:], T.wake[:], [], [("wkI", 0, 16)], 5.7)
+    dma("y", T.V[:, 0:4096], T.x[:], [], [("V", 0, 4096)], 5.3)
+    dma("y", T.wkI[:], T.wake[:], [], [("wkI", 0, 16)], 5.6)
     fill(R("ONE"), 1.0)
     iota(R("i1", 0, 1), [[0, 1]], 0, 1)
-    iota(R("i1", 8, 16), [[16, 8]], 0, 0)
     asel(R("UT"), R("ONE"), [[-16, 8], [0, 16]], OP.is_ge, 0, 1)
     asel(R("B128"), R("UT"), [[16, 8], [0, 16]], OP.is_ge, 15, -1)
     iota(R("t1"), [[16, 128]], 0, 0)
@@ -447,13 +469,13 @@ def rank_program(g, core, T, topo):
     ts(C(8), C(0), 1.0, OP.add)
     iota(R("col", 21, 26), [[1, 5]], 66, 0)
     iota(R("col", 26, 31), [[-2, 5]], -1, 0)
-    ts(R("i1", 16, 24), R("i1", 8, 16), C(0), OP.add)
-    ts(R("i1", 8, 16), R("i1", 16, 24), 3, OP.arith_shift_right)
-    cp(R("pm16", 16, 24), R("i1", 8, 16))
-    ts(R("i1", 24, 32), R("i1", 16, 24), 7, OP.bitwise_and)
-    ts(R("i1", 24, 32), R("i1", 24, 32), 16.0, OP.mult)
-    tt(R("i1", 24, 32), R("i1", 24, 32), R("i1", 8, 16), OP.add)
-    cp(R("pm16", 0, 8), R("i1", 24, 32))
+    ts(C(33), C(0), 8.0, OP.is_ge)
+    ts(C(34), C(0), 16.0, OP.mult)
+    ts(C(35), C(33), -127.0, OP.mult, C(34), OP.add)
+    ts(R("pm16", 0, 8), R("i1", 32, 48, 2), C(35), OP.add)
+    ts(R("pm16", 16, 24), R("i1", 32, 48, 2), C(33), OP.add)
+    ts(C(36), C(0), 8.0, OP.mult)
+    ts(R("pm16", 8, 16), R("i1", 32, 40), C(36), OP.add)
     ts(R("jW"), R("t1"), C(0), OP.add)
     ts(R("ei16"), R("t2"), C(0), OP.add)
     cp(R("cI"), IX(R("csI"), R("pm16", 0, 8)))
@@ -466,18 +488,18 @@ def rank_program(g, core, T, topo):
     fill(R("ZB"), 0.0)
     ts(Pk, R("t3"), 8192.0 * 7, OP.add)
     ts(R("m01"), R("t3"), 0.0, OP.is_gt)
-    ts(R("negk"), R("t3"), -8.5, OP.add)
+    ts(R("negk"), R("t3"), -1.0, OP.mult, 8.5, OP.add)
     ts(R("MK"), R("DR"), C(0), OP.is_equal)
     fill(C(20), 2048.0); fill(C(15), 24.0); fill(C(31), 2.0)
     fill(C(16), -2048.0); fill(C(17), -8.0); fill(C(18), -150.0); fill(C(19), 1.0 / 16)
     fill(R("SELT"), 0.0)
     ts(R("SELT", 112, 128), R("IW", 0, 16), C(0), OP.is_equal, 32.0, OP.mult)
-    ts(R("IDb"), R("ID"), -2097152.0, OP.mult)
+    act(R("IDb"), R("ID"), scale=-2097152.0)
     fill(R("HALF"), 0.5); fill(R("HALFn"), -0.5)
 
     def new_cells_of(lo, y, stamp, bank="PP", tmp=Pa):
         for h in range(2):
-            to_list(R(bank, 64 * h, 64 * h + 64), "SELPK", "EB", lo + 1024 * h, 1024)
+            to_list(R(bank, 64 * h, 64 * h + 64), "SELPK", "EB", lo + 1024 * h, 1024, PART if bank == "PP" else 16)
         ts(R("Bv"), R(bank, 0, 128), -0.4985, OP.add)
         tt(tmp, R(bank, 0, 128), R("Bv"), OP.subtract)
         tt(R("t1"), tmp, R("Bv"), OP.mult)
@@ -496,16 +518,21 @@ def rank_program(g, core, T, topo):
 
     def columns(t):
         mm(PDW, R("ZB"), R("ZB"), True, False)
-        dist_part("EB", ES[t], 0, 2048, 0)
+        for a in range(0, 2048, 128 * PART): dist_part("EB", ES[t], a, a + 128 * PART, 0)
         for a, b in zip(CH, CH[1:]):
             lst = IX(R("V", 0, 4096), R("c16", a // 16, b // 16))
             act(R("EB", GOT[t] + a, GOT[t] + b), lst)
-            tt(R("mx", a, b), lst, R("EB", ES[t] + a, ES[t] + b), OP.max)
+            if a // 512 in STAGE[t]:
+                bank = R(("SA", "SB")[a // 512 & 1])
+                mm(bank, R("ID"), R("EB", ES[t] + a, ES[t] + b), True, True)
+                tt(R("mx", a, b), R("EB", GOT[t] + a, GOT[t] + b), bank, OP.max)
+            else:
+                tt(R("mx", a, b), lst, R("EB", ES[t] + a, ES[t] + b), OP.max)
             dist_part("EB", GOT[t], a, b, 0)
             dist_part("mx", 0, a, b, 8, b == 2048)
-            if b % 1024 == 0:
-                for u in ((0, 1) if t == 0 else (t + 1,) if t + 1 < STEPS else ()):
-                    out_send(u, "b%d" % (a // 1024), R("EB", GOT[t] + b - 1024, GOT[t] + b))
+            for u in ((0, 1) if t == 0 else (t + 1,) if t + 1 < STEPS else ()):
+                for m in messages(u):
+                    if m[0] == "b" and landing(m, u)[2] == b: out_send(u, m, R("EB", GOT[t] + landing(m, u)[1], GOT[t] + b))
         act(R("bd"), PDW, AF.Relu, 1.0, C(18))
 
         def run():
@@ -528,22 +555,22 @@ def rank_program(g, core, T, topo):
             out_send(u, "nc", R(y))
         if t > 0:
             tt(Pb, DX, R(y), OP.mult)
-            tt(R("nZ"), Pb, R("nZ"), OP.min)
+            tt(R("nZ"), Pb, R("nZ"), OP.max)
 
-    act(R("EB", E01, E01 + 2048), IX(R("EB", SNAP, SNAP + 2048), R("ei16")))
+    for a in range(0, 2048, 512):
+        act(R("EB", E01 + a, E01 + a + 512), IX(R("EB", SNAP, SNAP + 2048), R("ei16", a // 16, a // 16 + 32)))
     ts(R("t3"), IX(R("hdI"), R("pm16", 0, 8)), -1.0, OP.mult, 1.0, OP.add)
     scan(R("z"), R("m01"), R("t3"), OP.mult, OP.add)
     cp(L("w"), R("z", 7, 128, 8))
     columns(0)
     code_out(0)
     cells_out(0)
-    new_cells_of(E01, "Cz", 1, "PW", Pb)
-    ts(R("nZ"), R("Cz"), -1.0, OP.mult)
+    new_cells_of(E01, "nZ", 1, "PW", Pb)
     cp(R("Cz"), R("cI"))
-    spread(384, "ID", L("w"), (R("ID"), R("HALF")))
+    spread(WX, "ID", L("w"), R("HALF"))
     tt(R("t1"), WX, R("z"), OP.subtract)
-    ts(R("t1"), R("t1"), 1.0, OP.add)
-    tt(R("mq"), R("t1"), R("t3"), OP.mult)
+    ts(Pa, R("t1"), 1.0, OP.add)
+    tt(R("mq"), Pa, R("t3"), OP.mult)
     ts(R("csH"), R("csI"), -2048.0, OP.add)
     fill(R("KB"), 0.0)
     cp(R("KB", 14, 142, 16), R("B128", 0, 128, 16)); cp(R("KB", 15, 143, 16), R("B128", 0, 128, 16))
@@ -559,13 +586,15 @@ def rank_program(g, core, T, topo):
         else: iota(R("LK", a, a + 512), [[0, 512]], 64, 0)
     iota(R("LK", 4096, IWW), [[8, 256], [0, 2]], 71, 0)
     ts(R("t1"), R("jW"), float(IWW), OP.add)
-    tt(R("t2"), R("csI"), R("t1"), OP.subtract)
-    tt(R("t2"), R("t2"), R("hdI"), OP.mult)
-    tt(R("t2"), R("t2"), R("t1"), OP.add)
-    cp(R("lk16"), R("t2"))
-    iota(R("LV0"), [[0, 2], [8, 256]], 65, 0)
-    for k in range(4):
-        scatter_act(IX(R("LK"), R("lk16", 32 * k, 32 * k + 32)), R("LV0"))
+    Ps, Pt = R("SA", 0, 128), R("SA", 128, 256)
+    ts(Ps, R("jW"), -1.0, OP.mult, -float(IWW), OP.add)
+    tt(Pt, Ps, R("csI"), OP.add)
+    tt(Pt, Pt, R("hdI"), OP.mult)
+    tt(Pt, Pt, R("t1"), OP.add)
+    cp(R("lk16"), Pt)
+    iota(R("LV0", 0, 256), [[8, 256]], 65, 0)
+    for k in range(8):
+        scatter_act(IX(R("LK"), R("lk16", 16 * k, 16 * k + 16)), R("LV0", 0, 256))
     fill(R("t1"), 1 / 1.75)
     comp("v", [R("t1"), R("ONE")], [Pc], lambda r, w: g.vector.tensor_tensor_scan(ap(w[0]), ap(r[0]), ap(r[1]), 1.75 ** 120, OP.mult, OP.mult))
     tt(R("t1"), Pc, R("ID"), OP.mult)
@@ -587,20 +616,25 @@ def rank_program(g, core, T, topo):
     ts(DM[1], oL, float(IWW), OP.add)
     ts(DM[2], oL, float(IWW - 2048), OP.add)
     cp(R("pm16", 24, 40), R("i1", 32, 48))
-    ts(R("pm16", 40, 44), R("HALF", 0, 4), 0.0, OP.mult, C(0), OP.add)
-    cp(R("B8", 16, 24), R("B128", 0, 128, 16))
+    ts(R("pm16", 40, 48), R("HALF", 0, 8), 0.0, OP.mult, C(0), OP.add)
+    fill(R("B8", 16, 32), 0.0)
+    cp(R("B8", 17, 32, 2), R("B128", 0, 128, 16))
+    fill(R("PW", 272, 304), 0.0)
+    ts(R("asl"), R("wk5"), -9.0, OP.mult, 9.0, OP.add)
     ts(L("dum"), oL, 2.0, OP.mult, 4096.0, OP.add)
     ts(L("c511"), oL, -1.0, OP.mult, 511.0, OP.add)
     cp(L("c511h"), L("c511"))
     fill(L("z0"), 0.0); fill(L("dec"), 0.0); fill(L("e2"), 0.0)
     ts(R("W128"), R("B128"), C(8), OP.mult)
-    cp(R("posH"), R("jW"))
+    act(R("posH"), R("jW"))
     ts(R("UT"), R("UT"), -1.0, OP.mult)
-    ts(R("IDn"), R("ID"), -1.0, OP.mult); ts(R("IDk"), R("ID"), 2048.0, OP.mult)
+    ts(R("IDn"), R("ID"), -1.0, OP.mult); act(R("IDk"), R("ID"), scale=2048.0)
     asel(R("qw", 0, 128), R("ONE"), [[0, 16], [-16, 8]], OP.is_ge, 0, 1)
-    asel(R("GM"), R("qw", 0, 128), [[0, 16], [16, 8]], OP.is_ge, 15, -1)
+    asel(R("LH"), R("qw", 0, 128), [[0, 16], [16, 8]], OP.is_ge, 15, -1)
+    tt(R("GM"), IX(R("o2", 48, 64), R("pm16", 16, 24)), R("LH"), OP.mult)
     for c in range(1, 16):
-        if c != 8: fill(R("EQ", 256 * c + 128 * (c // 8), 272 * c), 0.0)
+        a = 256 * c + 128 * (c // 8)
+        if c != 8: dma("y", T.EQ[:, a:272 * c], T.ZB[:, 0:272 * c - a], [("ZB", 0, 128), ("wkI", 0, 16)], [("EQ", a, 272 * c)])
     iota(R("OPW", 0, 256), [[0, 256]], 0, 0)
     fill(C(14), 1.0)
     ts(C(10), C(1), -0.5, OP.mult, 0.5, OP.add)
@@ -611,7 +645,7 @@ def rank_program(g, core, T, topo):
     ts(R("DUM", 24, 48), R("DUM", 24, 48), C(12), OP.add)
 
     def missing(out, half, lim):
-        spread(384, "ID", L("w"), (R("ID"), R(half)))
+        spread(WX, "ID", L("w"), R(half))
         tt(Pd, R("mq"), WX, OP.is_equal)
         tt(R("t1"), Pd, R("cI"), OP.mult)
         scan(R("t3"), R("m01"), R("t1"), OP.mult, OP.add)
@@ -624,19 +658,17 @@ def rank_program(g, core, T, topo):
             act(R("RW", 0, 256), IX(R("IW"), R("cl16")), bias=C(16))
             act(R("RW", 256, 512), IX(R("LK", 0, IWW), R("cl16")), scale=0.125, bias=C(17))
         else:
-            act(R("clOp"), IX(R("IW"), R("cl16")), bias=C(16))
+            ts(R("clOp"), IX(R("IW"), R("cl16")), -2048.0, OP.add)
             act(R("G"), IX(R("LK", 0, IWW), R("cl16")), scale=0.125, bias=C(17))
-            act(R("RW", 0, 256), IX(R("clOp"), R("cur16")))
+            cp(R("RW", 0, 256), IX(R("clOp"), R("cur16")))
             act(R("RW", 256, 512), IX(R("G"), R("cur16")))
         to_list(R("PL", 0, 32), "SELC", "RW", 0, 512)
         ts(R("p16"), R("PL", 16, 32), -0.45, OP.add)
         ts(R("pI"), R("PL", 16, 32), -0.45, OP.add)
         cp(L("clS"), R("PL", 0, 16))
-        tt(L("s8"), R("PL", 16, 32), R("pI"), OP.subtract)
-        if t == 0:
-            ts(L("val"), L("s8"), 1.0 / 16, OP.is_le)
-        else:
-            act(R("naL", 0, 256), IX(R("DR"), R("p16")))
+        tt(L("x9"), R("PL", 16, 32), R("asl", 16 * t, 16 * t + 16), OP.add)
+        tt(L("s8"), L("x9"), R("pI"), OP.subtract)
+        if t > 0: act(R("naL", 0, 256), IX(R("DR"), R("p16")))
         ts(R("o2", 64, 80), L("e2"), -256.0, OP.add)
         if t < STEPS - 1: tt(R("o2", 80, 96), L("clS"), DM[2], OP.subtract)
         tt(L("q2"), R("pI"), L("cur"), OP.subtract)
@@ -649,7 +681,7 @@ def rank_program(g, core, T, topo):
             if t == 0: iota(R("LV"), [[8, 256]], 66, 0)
             else: act(R("LV"), IX(R("IW", 0, 256), R("cur16")), scale=8.0, bias=C(21 + t))
             missing(L("clB"), "HALFn", C(31))
-            tt(L("dB"), L("clB"), L("cl"), OP.subtract)
+            tt(R("QD", 64, 96, 2), L("clB"), CL, OP.subtract)
 
     def judge(t):
         tw = R("lc%d" % t)
@@ -667,12 +699,10 @@ def rank_program(g, core, T, topo):
         act(R("Dl"), IX(R("lb%d" % t), R("L16", 0, 24)))
         ts(R("Ls", 24, 48), R("Ls", 0, 24), 8191, OP.bitwise_and)
         cp(R("L16", 24, 48), R("Ls", 24, 48))
-        tt(L("sel"), L("cm"), L("ab"), OP.subtract)
         tt(L("done"), L("cm"), L("ab"), OP.add)
-        spread(0, "ID", L("sel"))
-        spread(128, "IDn", L("done"))
-        tt(Pf, SX, R("ln%d" % t), OP.mult)
-        tt(R("t2"), SX, R("nZ"), OP.mult)
+        together(lambda: [mm(R("PX", k, 384, 8), R("ID"), R("lb16", 0, 48), True, True) for k in range(8)])
+        tt(Pf, CX, R("ln%d" % t), OP.mult)
+        tt(R("t2"), AX, R("nZ"), OP.mult)
         tt(Pe, Pf, R("t2"), OP.max)
         tt(R("Cz"), Pe, R("Cz"), OP.max)
         ts(R("cI"), R("Cz"), 4095, OP.bitwise_and)
@@ -688,10 +718,10 @@ def rank_program(g, core, T, topo):
 
     def lanes_post(t):
         if t == 0:
-            ts(L("x1"), L("ab"), -1.0, OP.mult, 1.0, OP.add)
+            ts(L("x1"), L("ab"), -9.0, OP.mult, 1.0 / 16, OP.add)
         else:
             cp(R("ab16"), L("ab"))
-            act(R("abR"), IX(R("IW", 0, 8), R("ab16")), scale=-1.0, bias=C(14))
+            act(R("abR"), IX(R("IW", 0, 8), R("ab16")), scale=-9.0)
             act(R("naL", 256, 512), IX(R("abR"), R("cur16")))
         if True:
             act(L("dst"), L("done"), scale=float(t + 2))
@@ -705,63 +735,58 @@ def rank_program(g, core, T, topo):
         n = 32 if t < STEPS - 1 else 16
         if t > 0:
             to_list(R("PL", 32, 64), "SELC", "naL", 0, 512)
-            tt(L("val"), L("s8"), R("PL", 32, 48), OP.is_le)
-        aw = R("awk", 16 * t, 16 * t + 16)
-        tt(L("naw"), L("x1") if t == 0 else R("PL", 48, 64), aw, OP.mult)
-        tt(L("ac"), L("naw"), L("val"), OP.mult)
-        tt(L("cand"), aw, L("val"), OP.mult)
-        tt(L("mv"), aw, L("cand"), OP.subtract)
+            tt(L("s8"), L("s8"), R("PL", 48, 64), OP.subtract)
+        tt(L("ac"), L("s8"), L("x1") if t == 0 else R("PL", 32, 48), OP.is_le)
+        tt(L("mv"), R("awk", 16 * t, 16 * t + 16), L("ac"), OP.subtract)
         tt(L("q3"), L("q2"), L("mv"), OP.mult)
         tt(L("e1"), L("e2"), L("q3"), OP.add)
-        tt(R("o2", 96, 112 + n), IX(L("ac"), R("pm16", 40, 41 + n // 16)), R("o2", 48, 64 + n), OP.mult)
-        tt(R("LH"), IX(R("o2", 96, 112), R("pm16", 16, 24)), R("GM"), OP.mult)
+        tt(R("LH"), IX(L("ac"), R("pm16", 16, 24)), R("GM"), OP.mult)
+        tt(R("QD", 0, 2 * n, 2), IX(L("ac"), R("pm16", 40, 40 + n // 16)), R("o2", 64, 64 + n), OP.mult)
         together(lambda: [mm(R("PW", 8 * h, 8 * h + 8), R("EQ", 256 * c + 128 * h, 256 * c + 128 * h + 128), R("LH", 8 * c, 8 * c + 8), c == 0, c == 8 * h + 7)
                           for h in range(2) for c in range(8 * h + 8)])
         tt(L("winT"), R("PW", 0, 16), L("thrT"), OP.is_le)
         tt(R("qw"), IX(L("winT"), R("pm16", 24, 40)), R("MK"), OP.mult)
-        together(lambda: [mm(R("PW", 32 + a + 8 * h, 40 + a + 8 * h), R("qw", 128 * h, 128 * h + 128), R("B8", 16, 24), True, True)
+        together(lambda: [mm(R("PW", 32 + 2 * a + 16 * h, 48 + 2 * a + 16 * h), R("qw", 128 * h, 128 * h + 128), R("B8", 16, 32), True, True)
                           for a in range(0, n, 16) for h in range(2)])
-        tt(R("z", 0, n), R("PW", 32, 32 + n), R("o2", 112, 112 + n), OP.mult)
-        tt(R("z", 32, 32 + n), R("z", 0, n), R("o2", 0, n), OP.add)
-        cp(R("o16", 0, n), R("z", 32, 32 + n))
+        scan(R("z", 0, 2 * n), R("PW", 32, 32 + 2 * n), R("QD", 0, 2 * n), OP.mult, OP.add)
+        cp(R("o16", 0, n), R("z", 1, 2 * n, 2))
         scatter_act(IX(R("OPW"), R("o16", 0, 16)), R("C64"))
         act(R("OPB", 0, 256), R("OPW", 0, 256), AF.Relu, 1.0 / 32, C(26 + t))
         if t == 0:
-            to_list(R("PW", 272, 288), "SELC", "OPB", 0, 256)
+            to_list(R("PW", 273, 304, 2), "SELC", "OPB", 0, 256)
         else:
-            to_list(R("PW", 272, 304), "SELC", "OPB", 0, 512)
-            ts(L("ng"), R("PW", 288, 304), (t + 2) / 8.0, OP.is_lt)
+            to_list(R("PW", 273, 336, 2), "SELC", "OPB", 0, 512)
+            ts(L("ng"), R("PW", 305, 336, 2), (t + 2) / 8.0, OP.is_lt)
         act(L("d8"), L("done"), scale=8.0)
         tt(L("w1"), L("w"), L("d8"), OP.max)
-        tt(L("w"), L("w1"), R("PW", 272, 288), OP.subtract)
+        tt(L("w"), L("w1"), R("PW", 273, 304, 2), OP.subtract)
         tt(L("e2"), L("e1"), L("ng"), OP.mult)
         tt(L("cur"), L("e2"), oL, OP.add)
         if t < STEPS - 1:
             cp(R("cur16"), L("cur"))
             scatter_act(IX(R("LK", 0, IWW + 256), R("o16", 16, 32)), R("LV"))
-            tt(L("x1"), R("cI", 0, 128, 8), L("cl"), OP.subtract)
+            tt(L("x1"), R("cI", 0, 128, 8), CL, OP.subtract)
             tt(L("x2"), L("x1"), L("done"), OP.mult)
-            tt(L("clA"), L("cl"), L("x2"), OP.add)
-            tt(L("x1"), R("PW", 272, 288), L("dB"), OP.mult)
-            tt(L("cl"), L("x1"), L("clA"), OP.add)
-            cp(R("cl16"), L("cl"))
+            tt(R("QD", 65, 96, 2), CL, L("x2"), OP.add)
+            scan(R("QD", 96, 128), R("PW", 272, 304), R("QD", 64, 96), OP.mult, OP.add)
+            cp(R("cl16"), CL)
 
     def snapshots(t):
         lo = ES[t + 1]
-        spread(256, "IDk", L("done"), (R("ID"), R("posH")))
+        spread(IXD, "IDk", L("done"), R("posH"))
         cp(R("ei16"), IXD)
         return lambda: [act(R("EB", ES[t + 2] + a, ES[t + 2] + a + 512), IX(R("EB", lo, lo + 4096), R("ei16", a // 16, a // 16 + 32)))
                         for a in range(0, 2048, 512)]
 
-    missing(L("cl"), "HALF", C(14))
-    cp(R("cl16"), L("cl"))
+    missing(CL, "HALF", C(14))
+    cp(R("cl16"), CL)
     for t in range(STEPS):
         lanes_pre(t)
         if t == STEPS - 1:
             for b in range(8):
-                bank = R(("PD", "PP")[b & 1])
+                bank = R(("SA", "SB")[b & 1])
                 mm(bank, R("W128"), R("V", 512 * b, 512 * b + 512), True, True)
-                act(R("ysR", 512 * b, 512 * b + 512), bank)
+                (cp if b & 1 else act)(R("ysR", 512 * b, 512 * b + 512), bank)
         judge(t)
         if t == STEPS - 1: break
         later = snapshots(t) if t < STEPS - 2 else None
@@ -772,11 +797,6 @@ def rank_program(g, core, T, topo):
         if later: later()
     t = STEPS - 1
     dma("y", T.ys[:], T.ysR[0:128:16, 0:4096], [("ysR", 0, 4096)], [])
-    ts(R("i1", 8, 16), R("i1", 16, 24), 15, OP.bitwise_and)
-    ts(R("i1", 8, 16), R("i1", 8, 16), 8.0, OP.mult)
-    ts(R("i1", 24, 32), R("i1", 16, 24), 4, OP.arith_shift_right)
-    tt(R("i1", 24, 32), R("i1", 24, 32), R("i1", 8, 16), OP.add)
-    cp(R("pm16", 8, 16), R("i1", 24, 32))
     cp(R("yo1"), IX(R("cI"), R("pm16", 8, 16)))
     dma("y", T.yc[:], T.yo1[:], [("yo1", 0, 128)], [])
     lanes_post(t)
@@ -785,8 +805,7 @@ def rank_program(g, core, T, topo):
     ts(Pd, R("mq"), 0.0, OP.is_equal, 99.0, OP.mult)
     tt(R("t1"), Pd, R("mq"), OP.max)
     ts(R("t2"), IX(R("t1"), R("pm16", 8, 16)), -0.5, OP.add)
-    together(lambda: [mm(R("PX", 384 + 16 * k, 400 + 16 * k), R("ID"), L("w"), True, True) for k in range(8)])
-    tt(R("yo2"), R("t2"), WX, OP.is_gt)
+    tt(R("yo2"), IX(L("w"), R("pm16", 40, 48)), R("t2"), OP.is_lt)
     dma("s", T.yh[:], T.yo2[:], [("yo2", 0, 128)], [])
     build()
     for sem in sorted(cnt):

@@ -10,8 +10,9 @@ ES = (E01, E01, E2, E3, E4)
 LAG = (1.4, 3.0, 4.5, 0.13, 0.15)
 HOLD, ROUNDS, ORDER = (0.0, 0.3, 0.6, 1.0), 60, {}
 FIRST = 1.8
+PE, FIX = 0.00045, 0.017
 PART = 4
-STAGE = ((), (), (), (), ())
+STAGE = ((1, 2, 3), (0, 1, 2, 3), (0, 1, 2, 3), (0, 1, 2, 3), (0, 1, 2, 3))
 IWV = 3
 LKV, LKS = 3, 5
 CH = (0, 512, 1024, 1536, 2048)
@@ -220,11 +221,11 @@ def rank_program(g, core, T, topo):
         cyc = n
         if out[0] == "i": cyc = 3.8 * n + 50
         elif any(isinstance(x, tuple) and x[0] == "i" for x in r): cyc = 1.56 * n + 50
-        elif q == "t": return 0.00083 * max(64, wid(r[1]))
+        elif q == "t": return PE * max(64, wid(r[1]))
         elif kind == "tt": cyc = n if any(ispsum[x[1]] for x in r) else 2 * n
         elif q == "g": cyc = 2 * n + 150
         elif q == "v" and short(out) and all(short(x) for x in r[:1]): cyc = n / 2
-        return max(64, cyc) * 0.00083 + (0.06 if q == "s" else 0.01)
+        return max(64, cyc) * 0.00083 + (0.06 if q == "s" else FIX)
 
     def comp(q, reads, writes, fn, kind="ts"):
         r = [res(x) for x in reads]

from concourse.mybir import AluOpType as OP, ActivationFunctionType as AF, AxisListType

STEPS = 5
VW = 4096 + 384
IWW = 4608
LKW = IWW + 2048
SNAP, GOT0, E01, GOT1, E2, GOT2, E3, GOT3, E4, GOT4 = (2048 * i for i in range(10))
GOT = (GOT0, GOT1, GOT2, GOT3, GOT4)
ES = (E01, E01, E2, E3, E4)
LAG = (1.4, 3.0, 4.5, 0.13, 0.15)
HOLD, ROUNDS, ORDER = (0.0, 0.3, 0.6, 1.0), 60, {}
FIRST = 1.8
PE, FIX = 0.00045, 0.017
PART = 4
STAGE = ((1, 2, 3), (0, 1, 2, 3), (0, 1, 2, 3), (0, 1, 2, 3), (0, 1, 2, 3))
IWV = 3
LKV, LKS = 3, 5
CH = (0, 512, 1024, 1536, 2048)

SCRATCH = {
    "V": ("sbuf", [128, VW], "bfloat16"), "EB": ("sbuf", [128, 20480], "bfloat16"),
    "mx": ("sbuf", [128, 2048], "bfloat16"), "KS": ("sbuf", [128, 2304], "bfloat16"), "KB": ("sbuf", [128, 144], "bfloat16"),
    "csH": ("sbuf", [128, 128], "float16"),
    "IW": ("sbuf", [128, IWW], "float32"), "LK": ("sbuf", [128, LKW], "float32"),
    "LV": ("sbuf", [128, 256], "float32"), "C64": ("sbuf", [128, 256], "float32"),
    "SELC": ("sbuf", [128, 144], "bfloat16"), "SELPK": ("sbuf", [128, 144], "bfloat16"), "ysR": ("sbuf", [128, VW], "float32"),
    "LV0": ("sbuf", [128, 512], "float32"), "aww": ("sbuf", [128, 16], "float32"),
    "SELT": ("sbuf", [128, 240], "bfloat16"), "EQ": ("sbuf", [128, 4096], "bfloat16"), "LH": ("sbuf", [128, 128], "bfloat16"),
    "MK": ("sbuf", [128, 256], "bfloat16"), "qw": ("sbuf", [128, 256], "bfloat16"), "abR": ("sbuf", [128, 256], "bfloat16"),
    "naL": ("sbuf", [128, 512], "bfloat16"), "o2": ("sbuf", [128, 144], "float32"), "o16": ("sbuf", [128, 32], "uint16"),
    "ONE": ("sbuf", [128, 128], "bfloat16"), "OPW": ("sbuf", [128, 512], "float32"), "OPB": ("sbuf", [128, 512], "bfloat16"),
    "JC": ("sbuf", [128, 256], "float32"), "K": ("sbuf", [128, 256], "float32"),
    "COMP": ("sbuf", [128, 512], "float32"), "DUM": ("sbuf", [128, 48], "float32"), "wR": ("sbuf", [128, 256], "float32"),
    "clOp": ("sbuf", [128, 256], "float32"), "G": ("sbuf", [128, 256], "float32"), "RW": ("sbuf", [128, 512], "float16"),
    "DR": ("sbuf", [128, 256], "bfloat16"), "decL": ("sbuf", [128, 256], "bfloat16"), "gnR": ("sbuf", [128, 256], "bfloat16"),
    "Dl": ("sbuf", [128, 384], "bfloat16"), "WD": ("sbuf", [128, 384], "float32"), "W128": ("sbuf", [128, 128], "bfloat16"),
    "i1": ("sbuf", [128, 48], "int32"), "col": ("sbuf", [128, 40], "float32"), "B8": ("sbuf", [128, 32], "bfloat16"),
    "QD": ("sbuf", [128, 128], "float32"), "asl": ("sbuf", [128, 80], "float32"),
    "lane": ("sbuf", [128, 640], "float32"), "lb16": ("sbuf", [128, 160], "bfloat16"), "lh16": ("sbuf", [128, 64], "float16"),
    "code0": ("sbuf", [128, 16], "float32"), "code1": ("sbuf", [128, 16], "float32"), "awk": ("sbuf", [128, 80], "float32"),
    "Ls": ("sbuf", [128, 48], "int32"), "L16": ("sbuf", [128, 48], "uint16"), "pm16": ("sbuf", [128, 48], "uint16"),
    "wkI": ("sbuf", [128, 16], "int32"), "wk5": ("sbuf", [128, 80], "int32"), "pI": ("sbuf", [128, 16], "int32"),
}
for _n in ("csI", "hdI", "Cz", "cI", "Bv", "hI", "h", "yI0", "yI1", "nZ"):
    SCRATCH[_n] = ("sbuf", [128, 128], "int32")
for _n in ("jW", "m01", "negk", "mq", "t1", "t2", "t3", "z", "yo1", "yo2"):
    SCRATCH[_n] = ("sbuf", [128, 128], "float32")
for _n in ("B128", "UT", "ID", "IDn", "IDk", "IDb", "HALF", "HALFn", "ZB", "bd", "GM"):
    SCRATCH[_n] = ("sbuf", [128, 128], "bfloat16")
SCRATCH["posH"] = ("sbuf", [128, 128], "float16")
for _n in ("c16", "ei16", "ck16", "lk16"):
    SCRATCH[_n] = ("sbuf", [128, 128], "uint16")
for _n in ("cl16", "cur16", "p16", "off16", "ab16", "dec16"):
    SCRATCH[_n] = ("sbuf", [128, 16], "uint16")
for _t in range(STEPS):
    SCRATCH["lb%d" % _t] = ("sbuf", [128, 2048], "bfloat16")
    SCRATCH["lc%d" % _t] = ("sbuf", [128, 16], "float32")
    SCRATCH["ln%d" % _t] = ("sbuf", [128, 128], "int32")
for _n in ("PD", "PP", "SA", "PX", "PL", "PW", "V0", "SB"):
    SCRATCH[_n] = ("psum", [128, 512], "float32")
PLACES = {"lane": 3, "lb16": 3, "lh16": 2, "t1": 10, "t2": 10, "t3": 4, "Bv": 3, "hI": 4, "h": 3, "z": 2, "cl16": 2, "p16": 2, "c16": 2,
          "cI": 2, "pI": 2, "mq": 2, "LV": 2, "cur16": 2}
for _n in PLACES:
    SCRATCH[_n] = (SCRATCH[_n][0], [128, SCRATCH[_n][1][1] * PLACES[_n]], SCRATCH[_n][2])


def messages(t):
    return ("b0", "b1", "b2", "b3", "co", "nc") if t == 0 else ("b0", "b1", "co", "nc")


SEMAPHORES = ["qv", "qs", "qt", "qg"] + ["d%d" % i for i in range(26)]
for _t in range(STEPS):
    for _m in messages(_t):
        SEMAPHORES += ["a%s%d" % (_m, _t), "l%s%d" % (_m, _t)]

_L = {}
for _b, _names in (("lane", "cur cl clS s8 val mv x9 ac dum q2 q3 cur1 e1 e2 ng fd f0 dst dec ncode thrab "
                            "d8 w1 z0 c511 thrT clB dB clA x1 x2 qq"),
                   ("lb16", "cm ab done w winT"), ("lh16", "rdy incl rc c511h")):
    for _i, _n in enumerate(_names.split()):
        _L[_n] = (_b, 16 * _i)
TILED = ("lane", "lb16", "lh16")


def landing(m, t):
    if m[0] == "b":
        n = 2048 // (len(messages(t)) - 2)
        return "lb%d" % t, n * int(m[1]), n * int(m[1]) + n
    if m == "co": return "lc%d" % t, 0, 16
    return "ln%d" % t, 0, 128


def route(core, t, T, topo):
    dst = T.cores[T.rank_of(core) ^ (1 + t % 7)]
    near = [x for x in topo.cores_of(core) if x != core and topo.die(x) == topo.die(core) and topo.may_write(x, dst)]
    far = [x for x in topo.cores_of(core) if topo.die(x) != topo.die(core) and topo.may_write(x, dst)]
    via = {"b0": far[0], "b1": far[1], "co": None, "nc": near[0]}
    if t == 0: via.update(b0=near[-1], b1=near[0], b2=far[0], b3=far[1])
    if not topo.may_write(core, dst): via["co"] = near[-1]
    return dst, via


def send(g, T, topo, core, dst, m, t, src):
    buf, lo, hi = landing(m, t)
    rid, pid = topo.addr(dst, core)
    es = topo.engines(core, dst)
    return g.remote_dma(out_ap=T[buf][:, lo:hi], in_ap=src, remote_sem=T.sem["a%s%d" % (m, t)], local_sem=T.sem["l%s%d" % (m, t)],
                        pid=pid, routing_id=rid, dma_engine_mask=sum(1 << e for e in (es[:8] if m == "co" else es[-8:])))


def relay_program(g, core, T, topo):
    for src in [x for x in topo.cores_of(core) if T.rank_of(x) is not None]:
        done = []
        for t in range(STEPS):
            dst, via = route(src, t, T, topo)
            for m in messages(t):
                if via[m] != core: continue
                buf, lo, hi = landing(m, t)
                g.wait_ge(T.sem["a%s%d" % (m, t)], 8)
                send(g, T, topo, core, dst, m, t, T[buf][:, lo:hi])
                done.append("l%s%d" % (m, t))
        for s in done:
            g.wait_ge(T.sem[s], 8)


def rank_program(g, core, T, topo):
    if T.rank_of(core) is None:
        relay_program(g, core, T, topo)
        return
    Q = {"v": g.vector, "s": g.scalar, "t": g.tensor, "y": g.sync, "g": g}
    width = {n: b[1][1] // PLACES.get(n, 1) for n, b in SCRATCH.items()}
    ispsum = {n: b[0] == "psum" for n, b in SCRATCH.items()}
    hist = {}
    ops = []
    known = {q: {} for q in Q}
    cnt = {}
    nd = [0]

    def R(b, lo=0, hi=None, st=1):
        return ("n", b, lo, width[b] if hi is None else hi, st)

    def L(n):
        return ("n", _L[n][0], _L[n][1], _L[n][1] + 16, 1)

    def C(i):
        return ("n", "col", i, i + 1, 1)

    def IX(w, o):
        return ("i", w, o)

    def ap(s):
        if s[0] == "i": return ap(s[1]).indirect(ap(s[2]))
        if s[4] == 1: return T[s[1]][:, s[2]:s[3]]
        return T[s[1]][:, s[2]:s[3]:s[4]]

    def flat(s):
        if not isinstance(s, tuple): return []
        if s[0] == "i": return flat(s[1]) + flat(s[2])
        return [(s[1], s[2], s[3])]

    def need(q, deps):
        for d in sorted(deps, reverse=True):
            _, sem, n, kn = ops[d]
            if known[q].get(sem, 0) >= n: continue
            Q[q].wait_ge(T.sem[sem], n)
            for k2, v2 in kn.items():
                if known[q].get(k2, 0) < v2: known[q][k2] = v2

    def track(q, reads, writes):
        deps = set()
        acc = [(b, lo, hi, False) for b, lo, hi in reads] + [(b, lo, hi, True) for b, lo, hi in writes]
        for b, lo, hi, w in acc:
            for lo2, hi2, w2, d in hist.get(b, ()):
                meet = lo < hi2 and lo2 < hi and (w or w2)
                if ispsum.get(b, False):
                    if ops[d][0] != q or (q != "t" and meet): deps.add(d)
                elif meet:
                    deps.add(d)
        return deps, acc

    def record(q, acc, sem, n):
        kn = dict(known[q]) if q in known else {}
        kn[sem] = n
        ops.append((q, sem, n, kn))
        d = len(ops) - 1
        for b, lo, hi, w in acc:
            hl = hist.setdefault(b, [])
            if w and not ispsum.get(b, False):
                hist[b] = hl = [x for x in hl if not (lo <= x[0] and x[1] <= hi)]
            elif ispsum.get(b, False):
                hist[b] = hl = [x for x in hl if not (ops[x[3]][0] == q and lo <= x[0] and x[1] <= hi and (w or not x[2]))]
            hl.append((lo, hi, w, d))

    ver = {}

    def res(s, w=False):
        if not isinstance(s, tuple): return s
        if s[0] == "i": return ("i", res(s[1]), res(s[2]))
        b = s[1]
        if b not in PLACES: return s
        wd = width[b]
        key = (b, s[2] // 16) if b in TILED else b
        if w and s[4] == 1 and (s[3] - s[2] == (16 if b in TILED else wd)): ver[key] = (ver.get(key, -1) + 1) % PLACES[b]
        sh = ver.get(key, 0) * wd
        return ("n", b, s[2] + sh, s[3] + sh, s[4])

    recs = []
    group = []
    sent = {}

    def wid(s):
        if s[0] == "i": return 16 * (s[2][3] - s[2][2])
        return (s[3] - s[2] + s[4] - 1) // s[4]

    def short(s):
        b = s[1][1] if s[0] == "i" else s[1]
        return SCRATCH[b][2] in ("bfloat16", "float16", "uint16")

    def span(q, kind, r, w):
        out, n = w[0], wid(w[0])
        cyc = n
        if out[0] == "i": cyc = 3.8 * n + 50
        elif any(isinstance(x, tuple) and x[0] == "i" for x in r): cyc = 1.56 * n + 50
        elif q == "t": return PE * max(64, wid(r[1]))
        elif kind == "tt": cyc = n if any(ispsum[x[1]] for x in r) else 2 * n
        elif q == "g": cyc = 2 * n + 150
        elif q == "v" and short(out) and all(short(x) for x in r[:1]): cyc = n / 2
        return max(64, cyc) * 0.00083 + (0.06 if q == "s" else FIX)

    def comp(q, reads, writes, fn, kind="ts"):
        r = [res(x) for x in reads]
        w = [res(x, True) for x in writes]
        rd = sum((flat(x) for x in r), [])
        wr = []
        for x in w:
            if x[0] == "i":
                wr += flat(x[1]); rd += flat(x[2])
            else:
                wr += flat(x)
        item = (rd, wr, lambda: fn(r, w))
        if group: group[-1].append((item, span(q, kind, r, w)))
        else: recs.append((q, [item], span(q, kind, r, w), "c", None))

    def together(fn):
        group.append([])
        fn()
        got = group.pop()
        recs.append(("t", [x[0] for x in got], sum(x[1] for x in got), "c", None))

    def dma(q, out, in_, reads, writes, lag=1.5):
        recs.append((q, [(reads, writes, lambda: Q[q].dma_start(out, in_))], 0.06, "d", lag))

    def out_send(t, m, srcspec):
        s = res(srcspec)
        first = (t, m) == (0, "b0")
        recs.append(("g", [(flat(s), [], lambda: (t, m, s))], 0.4 + (FIRST if first else 0.0), "r", None))
        sent[(t, m)] = len(recs) - 1
        recs.append(("net", [([], [landing(m, t)], None)], 0.0, "a", (t, m)))

    def build():
        n = len(recs)
        pred = [set() for _ in range(n)]
        banks = [set() for _ in range(n)]
        old = {}
        for i in range(n):
            q = recs[i][0]
            for rd, wr, _ in recs[i][1]:
                for b, lo, hi, w in [(b, lo, hi, False) for b, lo, hi in rd] + [(b, lo, hi, True) for b, lo, hi in wr]:
                    hl = old.setdefault(b, [])
                    for lo2, hi2, w2, d in hl:
                        if d != i and lo < hi2 and lo2 < hi and (w or w2): pred[i].add(d)
                    if w: hl[:] = [x for x in hl if not (lo <= x[0] and x[1] <= hi)]
                    hl.append((lo, hi, w, i))
                    if ispsum.get(b, False): banks[i].add(b)
            if recs[i][3] == "a": pred[i].add(sent[recs[i][4]])
        for i in range(1, LOADS): pred[i].add(i - 1)
        for x in sent:
            if x != (0, "b0"): pred[sent[x]].add(sent[(0, "b0")])
        pred[sent[(0, "co")] + 1].add(sent[(0, "b0")] + 1)
        pred[sent[(0, "nc")] + 1].add(sent[(0, "b1")] + 1)
        succ = [[] for _ in range(n)]
        for i in range(n):
            for d in pred[i]: succ[d].append(i)

        def lag(d, i):
            if i < LOADS or recs[d][3] == recs[i][3] == "r": return 0.0
            if recs[d][3] == recs[i][3] == "a": return 0.5
            if recs[d][3] == "d": return recs[d][4]
            if recs[i][3] == "a":
                t, m = recs[i][4]
                if m[0] == "b": return LAG[2] + (FIRST if t < 2 else 0.0)
                return LAG[0] if route(core, t, T, topo)[1][m] is None else LAG[1]
            if recs[d][3] == "r": return 3.0
            return LAG[3] if recs[d][0] == recs[i][0] else LAG[4]

        tail = [recs[i][4] if recs[i][3] == "d" else 0.0 for i in range(n)]
        lags = {(d, i): lag(d, i) for i in range(n) for d in pred[i]}

        def place(prio, back, hold):
            before, after = (succ, pred) if back else (pred, succ)
            left = [len(p) for p in before]
            est = list(tail) if back else [0.0] * n
            ready, free, held, order, ends = {}, {}, {}, [], [0.0] * n
            for i in range(n):
                if left[i] == 0: ready.setdefault(recs[i][0], []).append(i)

            def when(i):
                if not banks[i]: return est[i]
                return max([est[i]] + [e + LAG[4] for b in banks[i] for q2, e in held.get(b, {}).items() if q2 != recs[i][0]])

            for _ in range(n):
                best = None
                for q, rl in ready.items():
                    if not rl: continue
                    t0 = max(free.get(q, 0.0), min(when(i) for i in rl))
                    if best is None or t0 < best[0]: best = (t0, q)
                t0, q = best
                i = max([x for x in ready[q] if when(x) <= t0 + 1e-9], key=lambda x: (prio[x], -x))
                soon = [x for x in ready[q] if t0 < when(x) < t0 + hold * recs[i][2] and prio[x] > prio[i] + recs[i][2]]
                if soon:
                    i = min(soon, key=when); t0 = when(i)
                ready[q].remove(i)
                order.append(i)
                ends[i] = t0 + recs[i][2]
                for b in banks[i]: held.setdefault(b, {})[q] = ends[i]
                if q != "net": free[q] = ends[i]
                for j in after[i]:
                    est[j] = max(est[j], ends[i] + (lags[(j, i)] if back else lags[(i, j)]))
                    left[j] -= 1
                    if left[j] == 0: ready.setdefault(recs[j][0], []).append(j)
            return order, ends

        key = (n, round(sum(lags.values()), 3))
        if key not in ORDER:
            way = [0.0] * n
            for i in range(n - 1, -1, -1):
                way[i] = recs[i][2] + max([lags[(i, j)] + way[j] for j in succ[i]] + [tail[i]])
            ORDER["way"] = max(way)
            best, prio = None, way
            for r in range(ROUNDS):
                hold = HOLD[r % len(HOLD)]
                order, ends = place(prio, False, hold)
                total = max(ends[i] + tail[i] for i in range(n))
                if best is None or total < best[0]: best = (total, order, ends, prio, hold)
                if r % 3 == 2:
                    a = (r * 0.618) % 1.0
                    prio = [a * x + (1 - a) * y * best[0] / ORDER["way"] for x, y in zip(best[3], way)]
                else:
                    prio = place(ends if r % 3 else best[2], True, hold)[1]
            ORDER[key] = best[1]; ORDER["total"] = best[0]
        order = ORDER[key]
        for i in order:
            q, items, _, kind, x = recs[i]
            for rd, wr, fn in items:
                if kind == "a":
                    sem = "a%s%d" % (x[1], x[0]); cnt[sem] = 8
                    record("net", [(b, lo, hi, True) for b, lo, hi in wr], sem, 8)
                    continue
                deps, acc = track(q, rd, wr)
                need(q, deps)
                if kind == "r":
                    t, m, s = fn()
                    dst, via = route(core, t, T, topo)
                    send(g, T, topo, core, dst if via[m] is None else via[m], m, t, ap(s))
                    sem = "l%s%d" % (m, t); cnt[sem] = 8
                elif kind == "d":
                    sem = "d%d" % nd[0]; nd[0] += 1
                    fn().then_inc(T.sem[sem], 16); cnt[sem] = 16
                else:
                    sem = "q" + q
                    cnt[sem] = cnt.get(sem, 0) + 1
                    fn().then_inc(T.sem[sem], 1)
                record(q, acc, sem, cnt[sem])

    def tt(out, a, b, op):
        comp("v", [a, b], [out], lambda r, w: g.vector.tensor_tensor(out=ap(w[0]), in0=ap(r[0]), in1=ap(r[1]), op=op), "tt")

    def ts(out, a, s1, op0, s2=None, op1=None):
        def call(r, w):
            x1 = ap(r[1]) if isinstance(s1, tuple) else s1
            x2 = ap(r[2]) if isinstance(s2, tuple) else s2
            if op1 is None: return g.vector.tensor_scalar(out=ap(w[0]), in0=ap(r[0]), scalar1=x1, scalar2=None, op0=op0)
            return g.vector.tensor_scalar(out=ap(w[0]), in0=ap(r[0]), scalar1=x1, scalar2=x2, op0=op0, op1=op1)
        comp("v", [a, s1, s2], [out], call)

    def cp(out, a):
        comp("v", [a], [out], lambda r, w: g.vector.tensor_copy(out=ap(w[0]), in_=ap(r[0])))

    def fill(out, x):
        comp("v", [], [out], lambda r, w: g.vector.memset(ap(w[0]), x), "fill")

    def scan(out, d0, d1, op0, op1):
        comp("v", [d0, d1], [out], lambda r, w: g.vector.tensor_tensor_scan(ap(w[0]), ap(r[0]), ap(r[1]), 0.0, op0, op1))

    def reduce_add(out, a):
        comp("v", [a], [out], lambda r, w: g.vector.tensor_reduce(ap(w[0]), ap(r[0]), AxisListType.X, OP.add))

    def act(out, a, func=AF.Copy, scale=1.0, bias=None):
        def call(r, w):
            if bias is None: return g.scalar.activation(out=ap(w[0]), in_=ap(r[0]), func=func, scale=scale)
            return g.scalar.activation(out=ap(w[0]), in_=ap(r[0]), func=AF.Identity if func == AF.Copy else func, bias=ap(r[2]), scale=scale)
        comp("s", [a, scale, bias], [out], call)

    def scatter_act(out, a):
        comp("s", [a], [out], lambda r, w: g.scalar.activation(out=ap(w[0]), in_=ap(r[0]), func=AF.Silu))

    def mm(out, lhsT, rhs, start, stop, whole=None):
        if out[1] == "PP": whole = R("PP")
        comp("t", [lhsT, rhs], [out] + ([whole] if whole else []), lambda r, w: g.tensor.matmul(ap(w[0]), ap(r[0]), ap(r[1]), start, stop))

    def iota(out, pattern, base, cm, after=()):
        comp("g", list(after), [out], lambda r, w: g.iota(ap(w[0]), pattern, base, cm, allow_small_or_imprecise_dtypes=True))

    def asel(out, a, pattern, op, base, cm):
        comp("g", [a], [out], lambda r, w: g.affine_select(ap(w[0]), ap(r[0]), pattern, op, 0.0, base, cm))

    def to_list(out, sel, src, lo, n, part=16):
        for a in range(0, 16, part):
            together(lambda: [mm(out, R(sel, 15 - i, 143 - i), R(src, lo + i, lo + n, 16), i == 0, i == 15) for i in range(a, a + part)])

    def spread(out, diag, src, first):
        def run():
            mm(out, R("ID"), first, True, False)
            for k in range(8):
                mm(R(out[1], out[2] + k, out[3], 8), R(diag), src, False, k == 7)
        together(run)

    Pa, Pb, Pc, Pk = (R("V0", 128 * i, 128 * i + 128) for i in range(4))
    Pd, Pe, Pf, Pg = Pb, Pc, Pc, Pb
    CX, AX, DX, WX = (R("PX", 128 * i, 128 * i + 128) for i in range(4))
    IXD = R("PL", 128, 256)
    RA, BS = R("PW", 340, 356), R("PL", 80, 96)
    CL = R("QD", 97, 128, 2)
    DM = (R("QD", 1, 32, 2), R("QD", 33, 64, 2), R("o2", 32, 48))
    oL = R("jW", 0, 16)

    LOADS = 5
    dma("s", T.csI[:], T.cs[:], [], [("csI", 0, 128)], 1.5)
    dma("s", T.hdI[:], T.hold[:], [], [("hdI", 0, 128)], 1.8)
    dma("y", T.EB[:, SNAP:SNAP + 2048], T.snap[:], [], [("EB", SNAP, SNAP + 2048)], 3.0)
    dma("y", T.V[:, 0:4096], T.x[:], [], [("V", 0, 4096)], 5.3)
    dma("y", T.wkI[:], T.wake[:], [], [("wkI", 0, 16)], 5.6)
    fill(R("ONE"), 1.0)
    iota(R("i1", 0, 1), [[0, 1]], 0, 1)
    asel(R("UT"), R("ONE"), [[-16, 8], [0, 16]], OP.is_ge, 0, 1)
    asel(R("B128"), R("UT"), [[16, 8], [0, 16]], OP.is_ge, 15, -1)
    iota(R("t1"), [[16, 128]], 0, 0)
    iota(R("t2"), [[16, 16], [256, 8]], 0, 0)
    asel(R("ID"), R("B128"), [[-1, 128]], OP.is_equal, 0, 1)
    iota(R("t3"), [[0, 16], [1, 8]], 0, 0)
    asel(R("UT"), R("B128"), [[-1, 128]], OP.is_ge, 0, 1)
    iota(R("JC"), [[128, 16], [1, 16]], 0, 0)
    iota(R("DR"), [[0, 16], [1, 16]], 0, 0)
    iota(R("i1", 32, 48), [[1, 16]], 0, 0)
    iota(R("IW", 0, 512), [[1, 512]], 0, 0)
    for a in range(512, IWW, 512):
        if a <= 512 * IWV: ts(R("IW", a, a + 512), R("IW", 0, 512), float(a), OP.add)
        else: iota(R("IW", a, a + 512), [[1, 512]], a, 0)
    ts(R("i1", 1, 2), R("i1", 0, 1), 15, OP.bitwise_and)
    ts(R("i1", 2, 3), R("i1", 0, 1), 1, OP.bitwise_and)
    ts(R("i1", 3, 4), R("i1", 1, 2), 1, OP.arith_shift_right)
    cp(C(0), R("i1", 1, 2))
    ts(C(1), R("i1", 2, 3), 2.0, OP.mult, -1.0, OP.add)
    ts(C(2), C(1), 8192.0, OP.mult)
    ts(C(3), R("i1", 3, 4), 16.0, OP.mult)
    ts(C(4), C(0), 8.0, OP.is_lt, 1.0 / 2048 - 1.0, OP.mult)
    ts(C(5), C(4), 1.0, OP.add)
    ts(C(6), C(1), 1.0 / 8192, OP.mult)
    ts(C(7), C(1), -0.25, OP.mult)
    ts(C(8), C(0), 1.0, OP.add)
    iota(R("col", 21, 26), [[1, 5]], 66, 0)
    iota(R("col", 26, 31), [[-2, 5]], -1, 0)
    ts(C(33), C(0), 8.0, OP.is_ge)
    ts(C(34), C(0), 16.0, OP.mult)
    ts(C(35), C(33), -127.0, OP.mult, C(34), OP.add)
    ts(R("pm16", 0, 8), R("i1", 32, 48, 2), C(35), OP.add)
    ts(R("pm16", 16, 24), R("i1", 32, 48, 2), C(33), OP.add)
    ts(C(36), C(0), 8.0, OP.mult)
    ts(R("pm16", 8, 16), R("i1", 32, 40), C(36), OP.add)
    ts(R("jW"), R("t1"), C(0), OP.add)
    ts(R("ei16"), R("t2"), C(0), OP.add)
    cp(R("cI"), IX(R("csI"), R("pm16", 0, 8)))
    cp(R("c16"), R("cI"))
    fill(R("SELC"), 0.0)
    ts(R("SELC", 15, 143, 16), R("B128", 0, 128, 16), 1.0 / 16, OP.mult)
    ts(R("SELPK"), R("SELC"), C(5), OP.mult, 16.0, OP.mult)
    ts(R("B8", 0, 8), R("B128", 0, 128, 16), -1.0, OP.mult)
    ts(R("B8", 8, 16), R("B128", 0, 128, 16), 2.0, OP.mult)
    fill(R("ZB"), 0.0)
    ts(Pk, R("t3"), 8192.0 * 7, OP.add)
    ts(R("m01"), R("t3"), 0.0, OP.is_gt)
    ts(R("negk"), R("t3"), -1.0, OP.mult, 8.5, OP.add)
    ts(R("MK"), R("DR"), C(0), OP.is_equal)
    fill(C(20), 2048.0); fill(C(15), 24.0); fill(C(31), 2.0)
    fill(C(16), -2048.0); fill(C(17), -8.0); fill(C(18), -150.0); fill(C(19), 1.0 / 16)
    fill(R("SELT"), 0.0)
    ts(R("SELT", 112, 128), R("IW", 0, 16), C(0), OP.is_equal, 32.0, OP.mult)
    act(R("IDb"), R("ID"), scale=-2097152.0)
    fill(R("HALF"), 0.5); fill(R("HALFn"), -0.5)

    def new_cells_of(lo, y, stamp, bank="PP", tmp=Pa):
        for h in range(2):
            to_list(R(bank, 64 * h, 64 * h + 64), "SELPK", "EB", lo + 1024 * h, 1024, PART if bank == "PP" else 16)
        ts(R("Bv"), R(bank, 0, 128), -0.4985, OP.add)
        tt(tmp, R(bank, 0, 128), R("Bv"), OP.subtract)
        tt(R("t1"), tmp, R("Bv"), OP.mult)
        ts(R("hI"), R("t1"), 256.0, OP.mult, -0.4375, OP.add)
        ts(R("h"), R("hI"), 511, OP.bitwise_and)
        ts(R("h", 0, 128, 8), R("hI", 0, 128, 8), 4095, OP.bitwise_and)
        scan(R("t2"), R("m01"), R("h"), OP.mult, OP.add)
        tt(R("hI"), R("t2"), Pk, OP.add)
        ts(R(y), R("hI"), 4095 + 8192 * stamp, OP.bitwise_and)

    PDW = R("PD", 0, 128)

    def dist_part(src, lo, a, b, sign, stop=False):
        together(lambda: [mm(R("PD", j // 16, j // 16 + 8), R(src, lo + j, lo + j + 128), R("B8", sign, sign + 8), False, stop and j + 128 == b, PDW)
                          for j in range(a, b, 128)])

    def columns(t):
        mm(PDW, R("ZB"), R("ZB"), True, False)
        for a in range(0, 2048, 128 * PART): dist_part("EB", ES[t], a, a + 128 * PART, 0)
        for a, b in zip(CH, CH[1:]):
            lst = IX(R("V", 0, 4096), R("c16", a // 16, b // 16))
            act(R("EB", GOT[t] + a, GOT[t] + b), lst)
            if a // 512 in STAGE[t]:
                bank = R(("SA", "SB")[a // 512 & 1])
                mm(bank, R("ID"), R("EB", ES[t] + a, ES[t] + b), True, True)
                tt(R("mx", a, b), R("EB", GOT[t] + a, GOT[t] + b), bank, OP.max)
            else:
                tt(R("mx", a, b), lst, R("EB", ES[t] + a, ES[t] + b), OP.max)
            dist_part("EB", GOT[t], a, b, 0)
            dist_part("mx", 0, a, b, 8, b == 2048)
            for u in ((0, 1) if t == 0 else (t + 1,) if t + 1 < STEPS else ()):
                for m in messages(u):
                    if m[0] == "b" and landing(m, u)[2] == b: out_send(u, m, R("EB", GOT[t] + landing(m, u)[1], GOT[t] + b))
        act(R("bd"), PDW, AF.Relu, 1.0, C(18))

        def run():
            if t > 0: mm(BS, R("IDb"), L("done"), True, False)
            for gg in range(8):
                mm(BS, R("SELT", 112 - 16 * gg, 240 - 16 * gg), R("bd", gg, 128, 8), t == 0 and gg == 0, gg == 7)
        together(run)

    def code_out(t):
        c = R("code%d" % (t & 1))
        tt(c, BS, L("w"), OP.max)
        out_send(t, "co", c)
        act(L("ncode"), c, scale=-1.0)
        act(L("thrab"), c, scale=-1.0, bias=C(15))

    def cells_out(t):
        y = "yI%d" % (t & 1)
        new_cells_of(GOT[t], y, t + 2)
        for u in ((0, 1) if t == 0 else (t + 1,) if t + 1 < STEPS else ()):
            out_send(u, "nc", R(y))
        if t > 0:
            tt(Pb, DX, R(y), OP.mult)
            tt(R("nZ"), Pb, R("nZ"), OP.max)

    for a in range(0, 2048, 512):
        act(R("EB", E01 + a, E01 + a + 512), IX(R("EB", SNAP, SNAP + 2048), R("ei16", a // 16, a // 16 + 32)))
    ts(R("t3"), IX(R("hdI"), R("pm16", 0, 8)), -1.0, OP.mult, 1.0, OP.add)
    scan(R("z"), R("m01"), R("t3"), OP.mult, OP.add)
    cp(L("w"), R("z", 7, 128, 8))
    columns(0)
    code_out(0)
    cells_out(0)
    new_cells_of(E01, "nZ", 1, "PW", Pb)
    cp(R("Cz"), R("cI"))
    spread(WX, "ID", L("w"), R("HALF"))
    tt(R("t1"), WX, R("z"), OP.subtract)
    ts(Pa, R("t1"), 1.0, OP.add)
    tt(R("mq"), Pa, R("t3"), OP.mult)
    ts(R("csH"), R("csI"), -2048.0, OP.add)
    fill(R("KB"), 0.0)
    cp(R("KB", 14, 142, 16), R("B128", 0, 128, 16)); cp(R("KB", 15, 143, 16), R("B128", 0, 128, 16))
    for i in range(16):
        ts(R("KS", 144 * i, 144 * i + 144), R("KB"), R("MK", i, i + 1), OP.mult)
        together(lambda: [mm(R("PX", i, 256, 16), R("KS", 144 * i + 14 - 2 * k, 144 * i + 142 - 2 * k), R("csH", 16 * k, 16 * k + 16), k == 0, k == 7)
                          for k in range(8)])
    ts(R("JC"), R("JC"), C(3), OP.add, C(2), OP.mult)
    act(R("K"), R("PX", 0, 256), bias=C(20))
    for a in range(0, 4096, 512):
        if a < 512 * LKV: fill(R("LK", a, a + 512), 64.0)
        elif a < 512 * LKS: act(R("LK", a, a + 512), R("LK", 0, 512), AF.Silu)
        else: iota(R("LK", a, a + 512), [[0, 512]], 64, 0)
    iota(R("LK", 4096, IWW), [[8, 256], [0, 2]], 71, 0)
    ts(R("t1"), R("jW"), float(IWW), OP.add)
    Ps, Pt = R("SA", 0, 128), R("SA", 128, 256)
    ts(Ps, R("jW"), -1.0, OP.mult, -float(IWW), OP.add)
    tt(Pt, Ps, R("csI"), OP.add)
    tt(Pt, Pt, R("hdI"), OP.mult)
    tt(Pt, Pt, R("t1"), OP.add)
    cp(R("lk16"), Pt)
    iota(R("LV0", 0, 256), [[8, 256]], 65, 0)
    for k in range(8):
        scatter_act(IX(R("LK"), R("lk16", 16 * k, 16 * k + 16)), R("LV0", 0, 256))
    fill(R("t1"), 1 / 1.75)
    comp("v", [R("t1"), R("ONE")], [Pc], lambda r, w: g.vector.tensor_tensor_scan(ap(w[0]), ap(r[0]), ap(r[1]), 1.75 ** 120, OP.mult, OP.mult))
    tt(R("t1"), Pc, R("ID"), OP.mult)
    reduce_add(C(9), R("t1"))
    fill(L("thrT"), 2.5)
    upper = R("lane", _L["thrT"][1] + 8, _L["thrT"][1] + 16)
    ts(upper, upper, 1.75 ** -64, OP.mult, 1.75 ** -64, OP.mult)
    ts(L("thrT"), L("thrT"), C(9), OP.mult)
    tt(R("t1", 0, 16), R("V0", 256, 272), R("MK", 0, 16), OP.mult)
    reduce_add(C(13), R("t1", 0, 16))
    ts(C(13), C(13), 1.75 ** -119, OP.mult)
    ts(R("o2", 48, 56), R("V0", 256, 384, 16), C(13), OP.mult)
    ts(R("o2", 56, 64), R("o2", 48, 56), 1.75 ** -64, OP.mult, 1.75 ** -64, OP.mult)
    for t in range(STEPS):
        ts(R("wk5", 16 * t, 16 * t + 16), R("wkI"), t, OP.arith_shift_right, 1, OP.bitwise_and)
    cp(R("awk"), R("wk5"))
    cp(L("cur"), oL)
    ts(DM[0], oL, 256.0, OP.add)
    ts(DM[1], oL, float(IWW), OP.add)
    ts(DM[2], oL, float(IWW - 2048), OP.add)
    cp(R("pm16", 24, 40), R("i1", 32, 48))
    ts(R("pm16", 40, 48), R("HALF", 0, 8), 0.0, OP.mult, C(0), OP.add)
    fill(R("B8", 16, 32), 0.0)
    cp(R("B8", 17, 32, 2), R("B128", 0, 128, 16))
    fill(R("PW", 272, 304), 0.0)
    ts(R("asl"), R("wk5"), -9.0, OP.mult, 9.0, OP.add)
    ts(L("dum"), oL, 2.0, OP.mult, 4096.0, OP.add)
    ts(L("c511"), oL, -1.0, OP.mult, 511.0, OP.add)
    cp(L("c511h"), L("c511"))
    fill(L("z0"), 0.0); fill(L("dec"), 0.0); fill(L("e2"), 0.0)
    ts(R("W128"), R("B128"), C(8), OP.mult)
    act(R("posH"), R("jW"))
    ts(R("UT"), R("UT"), -1.0, OP.mult)
    ts(R("IDn"), R("ID"), -1.0, OP.mult); act(R("IDk"), R("ID"), scale=2048.0)
    asel(R("qw", 0, 128), R("ONE"), [[0, 16], [-16, 8]], OP.is_ge, 0, 1)
    asel(R("LH"), R("qw", 0, 128), [[0, 16], [16, 8]], OP.is_ge, 15, -1)
    tt(R("GM"), IX(R("o2", 48, 64), R("pm16", 16, 24)), R("LH"), OP.mult)
    for c in range(1, 16):
        a = 256 * c + 128 * (c // 8)
        if c != 8: dma("y", T.EQ[:, a:272 * c], T.ZB[:, 0:272 * c - a], [("ZB", 0, 128), ("wkI", 0, 16)], [("EQ", a, 272 * c)])
    iota(R("OPW", 0, 256), [[0, 256]], 0, 0)
    fill(C(14), 1.0)
    ts(C(10), C(1), -0.5, OP.mult, 0.5, OP.add)
    ts(C(11), C(1), 0.5, OP.mult, 0.5, OP.add)
    ts(R("DUM", 0, 24), R("jW", 0, 24), 4096.0, OP.add, C(10), OP.mult)
    ts(R("DUM", 24, 48), R("jW", 0, 24), 4096.0 + 2047.0 * 8192, OP.add, C(11), OP.mult)
    ts(C(12), C(10), -16777216.0, OP.mult)
    ts(R("DUM", 24, 48), R("DUM", 24, 48), C(12), OP.add)

    def missing(out, half, lim):
        spread(WX, "ID", L("w"), R(half))
        tt(Pd, R("mq"), WX, OP.is_equal)
        tt(R("t1"), Pd, R("cI"), OP.mult)
        scan(R("t3"), R("m01"), R("t1"), OP.mult, OP.add)
        act(L("f0"), L("w"), AF.Relu, -1.0, lim)
        tt(L("fd"), L("f0"), L("dum"), OP.mult)
        tt(out, R("t3", 7, 128, 8), L("fd"), OP.add)

    def lanes_pre(t):
        if t == 0:
            act(R("RW", 0, 256), IX(R("IW"), R("cl16")), bias=C(16))
            act(R("RW", 256, 512), IX(R("LK", 0, IWW), R("cl16")), scale=0.125, bias=C(17))
        else:
            ts(R("clOp"), IX(R("IW"), R("cl16")), -2048.0, OP.add)
            act(R("G"), IX(R("LK", 0, IWW), R("cl16")), scale=0.125, bias=C(17))
            cp(R("RW", 0, 256), IX(R("clOp"), R("cur16")))
            act(R("RW", 256, 512), IX(R("G"), R("cur16")))
        to_list(R("PL", 0, 32), "SELC", "RW", 0, 512)
        ts(R("p16"), R("PL", 16, 32), -0.45, OP.add)
        ts(R("pI"), R("PL", 16, 32), -0.45, OP.add)
        cp(L("clS"), R("PL", 0, 16))
        tt(L("x9"), R("PL", 16, 32), R("asl", 16 * t, 16 * t + 16), OP.add)
        tt(L("s8"), L("x9"), R("pI"), OP.subtract)
        if t > 0: act(R("naL", 0, 256), IX(R("DR"), R("p16")))
        ts(R("o2", 64, 80), L("e2"), -256.0, OP.add)
        if t < STEPS - 1: tt(R("o2", 80, 96), L("clS"), DM[2], OP.subtract)
        tt(L("q2"), R("pI"), L("cur"), OP.subtract)
        for c in range(16):
            b, lo = _L["clS"]
            ts(R("EQ", 272 * c, 256 * c + 256), R("RW", 16 * c, 256), R(b, lo + c, lo + c + 1), OP.is_equal)
        act(R("COMP", 0, 48), R("DUM"))
        iota(R("C64"), [[0, 256]], 64 * (t + 1), 0)
        if t < STEPS - 1:
            if t == 0: iota(R("LV"), [[8, 256]], 66, 0)
            else: act(R("LV"), IX(R("IW", 0, 256), R("cur16")), scale=8.0, bias=C(21 + t))
            missing(L("clB"), "HALFn", C(31))
            tt(R("QD", 64, 96, 2), L("clB"), CL, OP.subtract)

    def judge(t):
        tw = R("lc%d" % t)
        tt(L("rdy"), L("ncode"), tw, OP.is_equal)
        scan(L("incl"), L("rdy"), L("z0"), OP.add, OP.add)
        tt(L("rc"), L("rdy"), L("c511"), OP.mult)
        tt(L("ab"), tw, L("thrab"), OP.is_ge)
        together(lambda: [mm(RA, R("ID"), L("c511h"), True, False), mm(RA, R("UT"), L("rdy"), False, False),
                          mm(RA, R("IDn"), L("rc"), False, False), mm(RA, R("B128"), L("incl"), False, True)])
        cp(R("off16"), RA)
        ts(L("cm"), RA, 48.0, OP.is_lt)
        tt(IX(R("COMP"), R("off16")), R("K"), R("JC"), OP.add)
        tt(R("Ls", 0, 24), R("COMP", 0, 24), R("COMP", 24, 48), OP.max)
        ts(R("L16", 0, 24), R("Ls", 0, 24), C(6), OP.mult, C(7), OP.add)
        act(R("Dl"), IX(R("lb%d" % t), R("L16", 0, 24)))
        ts(R("Ls", 24, 48), R("Ls", 0, 24), 8191, OP.bitwise_and)
        cp(R("L16", 24, 48), R("Ls", 24, 48))
        tt(L("done"), L("cm"), L("ab"), OP.add)
        together(lambda: [mm(R("PX", k, 384, 8), R("ID"), R("lb16", 0, 48), True, True) for k in range(8)])
        tt(Pf, CX, R("ln%d" % t), OP.mult)
        tt(R("t2"), AX, R("nZ"), OP.mult)
        tt(Pe, Pf, R("t2"), OP.max)
        tt(R("Cz"), Pe, R("Cz"), OP.max)
        ts(R("cI"), R("Cz"), 4095, OP.bitwise_and)
        if t < STEPS - 1:
            cp(R("c16"), R("cI"))
            cp(IX(R("V"), R("L16", 24, 48)), R("Dl"))
        else:
            mm(R("PD", 0, 384), R("W128"), R("Dl"), True, True)
            act(R("WD"), R("PD", 0, 384))
            cp(IX(R("ysR"), R("L16", 24, 48)), R("WD"))
        tt(Pg, DX, R("negk"), OP.mult)
        tt(R("mq"), Pg, R("mq"), OP.max)

    def lanes_post(t):
        if t == 0:
            ts(L("x1"), L("ab"), -9.0, OP.mult, 1.0 / 16, OP.add)
        else:
            cp(R("ab16"), L("ab"))
            act(R("abR"), IX(R("IW", 0, 8), R("ab16")), scale=-9.0)
            act(R("naL", 256, 512), IX(R("abR"), R("cur16")))
        if True:
            act(L("dst"), L("done"), scale=float(t + 2))
            tt(L("dec"), L("dec"), L("dst"), OP.max)
            cp(R("dec16"), L("dec"))
            act(R("DR"), IX(R("IW", 0, 8), R("dec16")), scale=0.125, bias=C(19))
        if t == 0:
            ts(L("ng"), L("done"), -1.0, OP.mult, 1.0, OP.add)
        else:
            act(R("OPB", 256, 512), IX(R("DR"), R("cur16")))
        n = 32 if t < STEPS - 1 else 16
        if t > 0:
            to_list(R("PL", 32, 64), "SELC", "naL", 0, 512)
            tt(L("s8"), L("s8"), R("PL", 48, 64), OP.subtract)
        tt(L("ac"), L("s8"), L("x1") if t == 0 else R("PL", 32, 48), OP.is_le)
        tt(L("mv"), R("awk", 16 * t, 16 * t + 16), L("ac"), OP.subtract)
        tt(L("q3"), L("q2"), L("mv"), OP.mult)
        tt(L("e1"), L("e2"), L("q3"), OP.add)
        tt(R("LH"), IX(L("ac"), R("pm16", 16, 24)), R("GM"), OP.mult)
        tt(R("QD", 0, 2 * n, 2), IX(L("ac"), R("pm16", 40, 40 + n // 16)), R("o2", 64, 64 + n), OP.mult)
        together(lambda: [mm(R("PW", 8 * h, 8 * h + 8), R("EQ", 256 * c + 128 * h, 256 * c + 128 * h + 128), R("LH", 8 * c, 8 * c + 8), c == 0, c == 8 * h + 7)
                          for h in range(2) for c in range(8 * h + 8)])
        tt(L("winT"), R("PW", 0, 16), L("thrT"), OP.is_le)
        tt(R("qw"), IX(L("winT"), R("pm16", 24, 40)), R("MK"), OP.mult)
        together(lambda: [mm(R("PW", 32 + 2 * a + 16 * h, 48 + 2 * a + 16 * h), R("qw", 128 * h, 128 * h + 128), R("B8", 16, 32), True, True)
                          for a in range(0, n, 16) for h in range(2)])
        scan(R("z", 0, 2 * n), R("PW", 32, 32 + 2 * n), R("QD", 0, 2 * n), OP.mult, OP.add)
        cp(R("o16", 0, n), R("z", 1, 2 * n, 2))
        scatter_act(IX(R("OPW"), R("o16", 0, 16)), R("C64"))
        act(R("OPB", 0, 256), R("OPW", 0, 256), AF.Relu, 1.0 / 32, C(26 + t))
        if t == 0:
            to_list(R("PW", 273, 304, 2), "SELC", "OPB", 0, 256)
        else:
            to_list(R("PW", 273, 336, 2), "SELC", "OPB", 0, 512)
            ts(L("ng"), R("PW", 305, 336, 2), (t + 2) / 8.0, OP.is_lt)
        act(L("d8"), L("done"), scale=8.0)
        tt(L("w1"), L("w"), L("d8"), OP.max)
        tt(L("w"), L("w1"), R("PW", 273, 304, 2), OP.subtract)
        tt(L("e2"), L("e1"), L("ng"), OP.mult)
        tt(L("cur"), L("e2"), oL, OP.add)
        if t < STEPS - 1:
            cp(R("cur16"), L("cur"))
            scatter_act(IX(R("LK", 0, IWW + 256), R("o16", 16, 32)), R("LV"))
            tt(L("x1"), R("cI", 0, 128, 8), CL, OP.subtract)
            tt(L("x2"), L("x1"), L("done"), OP.mult)
            tt(R("QD", 65, 96, 2), CL, L("x2"), OP.add)
            scan(R("QD", 96, 128), R("PW", 272, 304), R("QD", 64, 96), OP.mult, OP.add)
            cp(R("cl16"), CL)

    def snapshots(t):
        lo = ES[t + 1]
        spread(IXD, "IDk", L("done"), R("posH"))
        cp(R("ei16"), IXD)
        return lambda: [act(R("EB", ES[t + 2] + a, ES[t + 2] + a + 512), IX(R("EB", lo, lo + 4096), R("ei16", a // 16, a // 16 + 32)))
                        for a in range(0, 2048, 512)]

    missing(CL, "HALF", C(14))
    cp(R("cl16"), CL)
    for t in range(STEPS):
        lanes_pre(t)
        if t == STEPS - 1:
            for b in range(8):
                bank = R(("SA", "SB")[b & 1])
                mm(bank, R("W128"), R("V", 512 * b, 512 * b + 512), True, True)
                (cp if b & 1 else act)(R("ysR", 512 * b, 512 * b + 512), bank)
        judge(t)
        if t == STEPS - 1: break
        later = snapshots(t) if t < STEPS - 2 else None
        lanes_post(t)
        columns(t + 1)
        code_out(t + 1)
        cells_out(t + 1)
        if later: later()
    t = STEPS - 1
    dma("y", T.ys[:], T.ysR[0:128:16, 0:4096], [("ysR", 0, 4096)], [])
    cp(R("yo1"), IX(R("cI"), R("pm16", 8, 16)))
    dma("y", T.yc[:], T.yo1[:], [("yo1", 0, 128)], [])
    lanes_post(t)
    last = res(L("cur"))
    dma("y", T.yl[:], ap(last), flat(last), [])
    ts(Pd, R("mq"), 0.0, OP.is_equal, 99.0, OP.mult)
    tt(R("t1"), Pd, R("mq"), OP.max)
    ts(R("t2"), IX(R("t1"), R("pm16", 8, 16)), -0.5, OP.add)
    tt(R("yo2"), IX(L("w"), R("pm16", 40, 48)), R("t2"), OP.is_lt)
    dma("s", T.yh[:], T.yo2[:], [("yo2", 0, 128)], [])
    build()
    for sem in sorted(cnt):
        if known["g"].get(sem, 0) < cnt[sem]:
            g.wait_ge(T.sem[sem], cnt[sem])
